import numpy as np
import ml_dtypes


def mxq(x, axis, fmt="e4m3"):
    dtype, down = {"e4m3": (ml_dtypes.float8_e4m3fn, 7), "e5m2": (ml_dtypes.float8_e5m2, 14)}[fmt]
    v = np.moveaxis(np.asarray(x, np.float32).astype(ml_dtypes.bfloat16).astype(np.float64), axis, -1)
    blocks = v.reshape(v.shape[:-1] + (-1, 32))
    amax = np.abs(blocks).max(-1, keepdims=True)
    byte = np.maximum(np.where(amax > 0, np.frexp(amax)[1] - 1 + 127, 0) - down, 1)
    scale = np.exp2(byte - 127.0)
    codes = (blocks / scale).astype(np.float32).astype(dtype).astype(np.float64)
    return np.moveaxis((codes * scale).reshape(v.shape), -1, axis)


WIDE = False


def mx_kscale(k):
    if not WIDE:
        return np.ones(k)
    levels = np.array([10, -10, 5, -5, 0])
    if k % 512:
        return np.exp2(np.random.permutation(np.resize(levels, k // 32))).repeat(32)
    a = np.empty((k // 512, 16))
    for p in range(k // 512):
        a[p, :8] = np.random.permutation(np.resize(levels, 8))
        for g in range(8):
            far = levels[np.abs(levels - a[p, g]) >= 10]
            a[p, g + 8] = far[np.random.randint(len(far))]
    return np.exp2(a.ravel()).repeat(32)


BF16 = ml_dtypes.bfloat16


def bf(x):
    return np.asarray(x, np.float32).astype(BF16)


def f64(x):
    return np.asarray(x).astype(np.float64)

E4M3FN = np.array([(-1.0 if i & 128 else 1.0) * ((1.0 + (i & 7) / 8.0) * 2.0 ** (((i >> 3) & 15) - 7) if i & 120 else (i & 7) * 2.0 ** -9) for i in range(256)])


def e4m3fn_bytes(y):
    return np.clip(np.asarray(y, np.float64), -448.0, 448.0).astype(np.float32).astype(ml_dtypes.float8_e4m3fn).view(np.uint8)


def e4m3fn_values(b):
    return E4M3FN[b]


V, F, O, B = 1536, 1024, 512, 128


def setup_inputs():
    s, t = mx_kscale(V), mx_kscale(F)
    G = np.random.standard_normal((V, V))
    L = (G + G.T) / np.sqrt(8 * V) * s
    theta = np.random.standard_normal((F, O)) / np.sqrt(F) / t[:, None]
    L_scale = (np.abs(L).reshape(V // B, B, V // B, B).max(axis=(1, 3)) / 448).astype(np.float32)
    theta_scale = (np.abs(theta).reshape(F // B, B, O // B, B).max(axis=(1, 3)) / 448).astype(np.float32)
    L_bytes = e4m3fn_bytes(L / np.repeat(np.repeat(f64(L_scale), B, axis=0), B, axis=1))
    theta_bytes = e4m3fn_bytes(theta / np.repeat(np.repeat(f64(theta_scale), B, axis=0), B, axis=1))
    return {"L_bytes": L_bytes,
            "L_scale": L_scale,
            "t1": bf(np.random.standard_normal((V, F)) / s[:, None] * t),
            "t0": bf(np.random.standard_normal((V, F)) * t),
            "theta_bytes": theta_bytes,
            "theta_scale": theta_scale,
            "acc": bf(np.random.standard_normal((V, O)))}


def reference(L_bytes, L_scale, t1, t0, theta_bytes, theta_scale, acc):
    L = e4m3fn_values(L_bytes) * np.repeat(np.repeat(f64(L_scale), B, axis=0), B, axis=1)
    theta = e4m3fn_values(theta_bytes) * np.repeat(np.repeat(f64(theta_scale), B, axis=0), B, axis=1)
    p = mxq(L, 1, "e4m3") @ mxq(f64(t1), 0, "e4m3")
    z = 2.0 * p - f64(t0)
    y = mxq(z, 1, "e4m3") @ mxq(theta, 0, "e4m3")
    return np.maximum(f64(acc) + y, 0.0)

@@ -1,0 +1,391 @@
+from contextlib import ExitStack
+
+import concourse.mybir as mybir
+from concourse.masks import make_identity
+
+V, F, O = 1536, 1024, 512
+FLOPS = 2 * V * V * F + 2 * V * F * O
+
+F32 = mybir.dt.float32
+BF16 = mybir.dt.bfloat16
+U32 = mybir.dt.uint32
+U8 = mybir.dt.uint8
+FP8 = mybir.dt.float8_e4m3fn
+FP8X4 = mybir.dt.float8_e4m3fn_x4
+ACT = mybir.ActivationFunctionType
+ALU = mybir.AluOpType
+
+P = 128
+NT = V // P
+NP = NT // 2
+G1 = V // 512
+G2 = F // 512
+HEAD = 4
+WV = ()
+T1A = ()
+RG = ()
+RD = ()
+LWB = 6
+PB, TB, YB = 4, 3, 1
+
+
+def tile_chebyshev_filter_last_term_d7_kernel(tc, L_bytes, L_scale, t1, t0, theta_bytes, theta_scale, acc, out):
+    nc = tc.nc
+    with ExitStack() as ctx:
+        keep = ctx.enter_context(tc.tile_pool(name="keep", bufs=1))
+        work = ctx.enter_context(tc.tile_pool(name="work", bufs=3))
+        psum = ctx.enter_context(tc.psum_pool(name="psum", bufs=1))
+
+        ident = keep.tile([P, P], F32, name="ident")
+        make_identity(nc, ident[:])
+
+        if True:
+            l_sc = keep.tile([P, NT * NT], F32, name="l_sc")
+            nc.scalar.dma_start(out=l_sc[:], in_=L_scale.rearrange("a b -> (a b)").partition_broadcast(P))
+            th_sc = keep.tile([P, G2, 4], F32, name="th_sc")
+            th_sc_rows = theta_scale.rearrange("(g q) o -> q g o", q=4)
+
+            l_src = L_bytes.rearrange("(c a p) j -> c p a j", a=2, p=P)
+            t1_src = t1.rearrange("(g p t) f -> g p t f", p=P, t=4)
+            t0_src = t0.rearrange("(c a p) f -> c p a f", a=2, p=P)
+            acc_src = acc.rearrange("(c a p) o -> c p a o", a=4, p=P)
+            l_by = [keep.tile([P, 2, V], U8, name="l_by%d" % c) for c in range(NP)]
+            t1_raw = [[keep.tile([P, 4, 512], BF16, name="t1_raw%d_%d" % (g, h)) for h in range(2)] for g in range(G1)]
+            t0_sb = [keep.tile([P, 2, F], BF16, name="t0_sb%d" % c) for c in range(NP)]
+            acc_sb = [keep.tile([P, 4, O], BF16, name="acc_sb%d" % c) for c in range(3)]
+            th_by = keep.tile([P, G2, 4, O], U8, name="th_by")
+
+            def load_l(c):
+                nc.sync.dma_start(out=l_by[c][:], in_=l_src[c])
+
+            def load_t1(g, h):
+                nc.sync.dma_start(out=t1_raw[g][h][:], in_=t1_src[g][:, :, 512 * h : 512 * h + 512])
+
+            def load_t0(c):
+                nc.sync.dma_start(out=t0_sb[c][:], in_=t0_src[c])
+
+            def load_acc(c):
+                nc.sync.dma_start(out=acc_sb[c][:], in_=acc_src[c])
+
+            nc.sync.dma_start(out=l_by[0][:, 0, :], in_=l_src[0][:, 0, :])
+            for f0 in (0, 256):
+                nc.sync.dma_start(out=t1_raw[0][0][:, :, f0 : f0 + 256], in_=t1_src[0][:, :, f0 : f0 + 256])
+            nc.sync.dma_start(out=l_by[0][:, 1, :], in_=l_src[0][:, 1, :])
+            load_t1(1, 0)
+            load_l(1)
+            load_t1(2, 0)
+            load_t1(0, 1)
+            load_t0(0)
+            load_t1(1, 1)
+            load_t1(2, 1)
+            load_l(2)
+            load_t0(1)
+            for q in range(4):
+                nc.sync.dma_start(out=th_sc[32 * q : 32 * q + 32], in_=th_sc_rows[q].partition_broadcast(32))
+            nc.sync.dma_start(out=th_by[:], in_=theta_bytes.rearrange("(g p t) o -> p g t o", p=P, t=4))
+            load_l(3)
+            load_t0(2)
+            load_acc(0)
+            load_l(4)
+            load_l(5)
+            load_t0(3)
+            load_acc(1)
+            load_t0(4)
+            load_t0(5)
+            load_acc(2)
+
+            t1_mx = {}
+            t1_il = {}
+
+            def t1_copy(g, h, parts=1):
+                act = (g, h) in T1A
+                il = work.tile([P, 512, 4], BF16, name="t1_il", align_bytes=64)
+                w = 512 // parts
+                for i in range(parts):
+                    dst, src = il[:, i * w : i * w + w, :], t1_raw[g][h][:, :, i * w : i * w + w].rearrange("p t f -> p f t")
+                    if act:
+                        nc.scalar.copy(out=dst, in_=src)
+                    else:
+                        nc.vector.tensor_copy(out=dst, in_=src)
+                t1_il[g, h] = il
+
+            def t1_quant(g, h):
+                q = keep.tile([P, 512], U32, name="t1_q%d_%d" % (g, h), align_bytes=64)
+                s = keep.tile([P, 512], U8, name="t1_s%d_%d" % (g, h), align_bytes=64)
+                nc.vector.quantize_mx(out=q[:].bitcast(FP8X4), scales=s[:], in_=t1_il[g, h][:].rearrange("p f t -> p (f t)"))
+                t1_mx[g, h] = (q, s)
+
+            l_w = {}
+            l_ps = {}
+            l_il = {}
+            l_mx = {}
+
+            def widen(n, b0=0, b1=NT):
+                if n not in l_w:
+                    l_w[n] = work.tile([P, V], BF16, name="l_w", bufs=LWB)
+                src = l_by[n // 2][:, n % 2, :].bitcast(FP8)
+                for b in range(b0, b1):
+                    k = NT * n + b
+                    if n in WV:
+                        g, q = divmod(b, 4)
+                        nc.vector.tensor_scalar(
+                            out=l_w[n][:].rearrange("p (g u m e) -> p g m u e", g=G1, u=2, e=2)[:, g, 32 * q : 32 * q + 32],
+                            in0=src[:, P * b : P * b + P].rearrange("p (m u e) -> p m u e", u=2, e=2),
+                            scalar1=l_sc[:, k : k + 1],
+                            scalar2=None,
+                            op0=ALU.mult,
+                        )
+                    else:
+                        nc.scalar.activation(
+                            out=l_w[n][:, P * b : P * b + P],
+                            in_=src[:, P * b : P * b + P],
+                            func=ACT.Copy,
+                            scale=l_sc[:, k : k + 1],
+                        )
+
+            def l_turn(c, g):
+                ps = psum.tile([P, 2, 2, P], F32, name="turn", bufs=TB)
+                for a in range(2):
+                    words = l_w[2 * c + a][:].bitcast(F32)
+                    for u in range(2):
+                        if 2 * c + a in WV:
+                            part = words[:, 256 * g + 128 * u : 256 * g + 128 * u + 128]
+                        else:
+                            part = words[:, 256 * g + u : 256 * (g + 1) : 2]
+                        nc.tensor.transpose(ps[:, a, u, :], part, ident[:])
+                l_ps[c, g] = ps
+
+            def l_out(c, g):
+                il = work.tile([P, 1024], BF16, name="l_il", bufs=6, align_bytes=64)
+                nc.scalar.copy(
+                    out=il[:].bitcast(F32).rearrange("p (a i u) -> p a i u", a=2, u=2),
+                    in_=l_ps[c, g][:].rearrange("p a u i -> p a i u"),
+                )
+                l_il[c, g] = il
+
+            def l_quant(c, g):
+                q = work.tile([P, 256], U32, name="l_q%d" % g, bufs=4, align_bytes=64)
+                s = work.tile([P, 256], U8, name="l_s%d" % g, bufs=4, align_bytes=64)
+                nc.vector.quantize_mx(out=q[:].bitcast(FP8X4), scales=s[:], in_=l_il[c, g][:])
+                l_mx[c, g] = (q, s)
+
+            p_ps = {}
+            z_sb = {}
+
+            def mm1(n, h):
+                ps = psum.tile([P, 512], F32, name="prod", bufs=PB)
+                cols = slice(P * (n % 2), P * (n % 2) + P)
+                for g in range(G1):
+                    lq, ls = l_mx[n // 2, g]
+                    tq, ts = t1_mx[g, h]
+                    nc.tensor.matmul_mx(
+                        out=ps[:],
+                        lhsT=lq[:, cols].bitcast(FP8X4),
+                        lhsT_scale=ls[:, cols],
+                        rhs=tq[:].bitcast(FP8X4),
+                        rhs_scale=ts[:],
+                        start=(g == 0),
+                        stop=(g == G1 - 1),
+                    )
+                p_ps[n, h] = ps
+
+            def z_step(n, h):
+                if n not in z_sb:
+                    z_sb[n] = work.tile([P, G2, 2, 256], BF16, name="z_sb", bufs=6)
+                pv = p_ps[n, h][:].rearrange("p (m u e) -> p u m e", u=2, e=2)
+                tv = t0_sb[n // 2][:, n % 2, 512 * h : 512 * h + 512].rearrange("p (m u e) -> p u m e", u=2, e=2)
+                for u in range(2):
+                    nc.vector.scalar_tensor_tensor(
+                        out=z_sb[n][:, h, u, :].rearrange("p (m e) -> p m e", e=2),
+                        in0=pv[:, u],
+                        scalar=2.0,
+                        in1=tv[:, u],
+                        op0=ALU.mult,
+                        op1=ALU.subtract,
+                    )
+
+            zt_ps = {}
+            z_il = {}
+            z_mx = {}
+
+            def z_turn(n, gs=(0, 1)):
+                if n not in zt_ps:
+                    zt_ps[n] = psum.tile([P, G2, 2, P], F32, name="turn", bufs=TB)
+                for g in gs:
+                    for u in range(2):
+                        nc.tensor.transpose(zt_ps[n][:, g, u, :], z_sb[n][:, g, u, :].bitcast(F32), ident[:])
+
+            def z_out(n, gs=(0, 1)):
+                if n not in z_il:
+                    z_il[n] = work.tile([P, 1024], BF16, name="z_il", align_bytes=64)
+                a, b = gs[0], gs[-1] + 1
+                nc.scalar.copy(
+                    out=z_il[n][:].bitcast(F32).rearrange("p (g i u) -> p g i u", g=2, u=2)[:, a:b],
+                    in_=zt_ps[n][:].rearrange("p g u i -> p g i u")[:, a:b],
+                )
+
+            def z_quant(n, gs=(0, 1)):
+                if n not in z_mx:
+                    q = work.tile([P, 256], U32, name="z_q", align_bytes=64)
+                    s = work.tile([P, 256], U8, name="z_s", align_bytes=64)
+                    z_mx[n] = (q, s)
+                q, s = z_mx[n]
+                a, b = P * gs[0], P * (gs[-1] + 1)
+                nc.vector.quantize_mx(out=q[:, a:b].bitcast(FP8X4), scales=s[:, a:b], in_=z_il[n][:, 4 * a : 4 * b])
+
+            th_w = keep.tile([P, G2, 4, O], BF16, name="th_w")
+            th_il = keep.tile([P, G2, O, 4], BF16, name="th_il", align_bytes=64)
+            th_q = keep.tile([P, G2, O], U32, name="th_q", align_bytes=64)
+            th_s = keep.tile([P, G2, O], U8, name="th_s", align_bytes=64)
+
+            def th_widen(g):
+                nc.scalar.copy(
+                    out=th_w[:, g].rearrange("p t o -> p (t o)"), in_=th_by[:, g].rearrange("p t o -> p (t o)").bitcast(FP8)
+                )
+
+            def th_scale(g):
+                for b in range(4):
+                    nc.vector.tensor_scalar(
+                        out=th_il[:, g, P * b : P * b + P, :],
+                        in0=th_w[:, g, :, P * b : P * b + P].rearrange("p t o -> p o t"),
+                        scalar1=th_sc[:, g, b : b + 1],
+                        scalar2=None,
+                        op0=ALU.mult,
+                    )
+
+            def th_quant(g):
+                nc.vector.quantize_mx(
+                    out=th_q[:, g].bitcast(FP8X4), scales=th_s[:, g], in_=th_il[:, g].rearrange("p o t -> p (o t)")
+                )
+
+            y_ps = {}
+            sums = {}
+
+            def mm2(n, gs=(0, 1)):
+                if n not in y_ps:
+                    y_ps[n] = psum.tile([P, O], F32, name="y", bufs=YB)
+                zq, zs = z_mx[n]
+                for g in gs:
+                    cols = slice(P * g, P * g + P)
+                    nc.tensor.matmul_mx(
+                        out=y_ps[n][:],
+                        lhsT=zq[:, cols].bitcast(FP8X4),
+                        lhsT_scale=zs[:, cols],
+                        rhs=th_q[:, g].bitcast(FP8X4),
+                        rhs_scale=th_s[:, g],
+                        start=(g == 0),
+                        stop=(g == G2 - 1),
+                    )
+
+            def add_acc(n, parts=1):
+                t = work.tile([P, O], F32, name="sums")
+                for i in range(parts):
+                    w = slice(i * O // parts, (i + 1) * O // parts)
+                    nc.vector.tensor_tensor(out=t[:, w], in0=y_ps[n][:, w], in1=acc_sb[n // 4][:, n % 4, w], op=ALU.add)
+                sums[n] = t
+
+            def relu_store(n, parts=1):
+                r = work.tile([P, O], F32, name="res")
+                for i in range(parts):
+                    w = slice(i * O // parts, (i + 1) * O // parts)
+                    if n in RG:
+                        nc.gpsimd.tensor_scalar(out=r[:, w], in0=sums[n][:, w], scalar1=0.0, scalar2=0.0, op0=ALU.max, op1=ALU.add)
+                    elif n in RD:
+                        nc.vector.tensor_scalar(out=r[:, w], in0=sums[n][:, w], scalar1=0.0, scalar2=None, op0=ALU.max)
+                    else:
+                        nc.scalar.activation(out=r[:, w], in_=sums[n][:, w], func=ACT.Relu)
+                    nc.sync.dma_start(out=out[P * n : P * n + P, w], in_=r[:, w])
+
+            all_g = range(G1)
+            widen(0)
+            widen(1)
+            t1_copy(0, 0, parts=2)
+            t1_copy(1, 0)
+            t1_quant(0, 0)
+            for g in all_g:
+                l_turn(0, g)
+            widen(2, 0, 4)
+            for g in all_g:
+                l_out(0, g)
+            t1_copy(2, 0)
+            t1_quant(1, 0)
+            l_quant(0, 0)
+            l_quant(0, 1)
+            t1_quant(2, 0)
+            l_quant(0, 2)
+            mm1(0, 0)
+            mm1(1, 0)
+            widen(2, 4, 12)
+            widen(3)
+            for g in all_g:
+                l_turn(1, g)
+            t1_copy(0, 1)
+            z_step(0, 0)
+            t1_quant(0, 1)
+            z_step(1, 0)
+            t1_copy(1, 1)
+            for g in all_g:
+                l_out(1, g)
+            for g in all_g:
+                l_quant(1, g)
+            t1_quant(1, 1)
+            mm1(2, 0)
+            mm1(3, 0)
+            t1_copy(2, 1)
+            z_step(2, 0)
+            t1_quant(2, 1)
+            z_step(3, 0)
+            widen(4)
+            th_widen(0)
+            th_widen(1)
+
+            turned = []
+            last = NT - 1
+            for n in range(NT + 4):
+                if n < NT:
+                    if n >= HEAD:
+                        mm1(n, 0)
+                    mm1(n, 1)
+                outs = turned
+                turned = []
+                for c, g in outs:
+                    l_out(c, g)
+                if 2 <= n < NT + 1:
+                    z_out(n - 2)
+                if n == NT + 1:
+                    for g in range(G2):
+                        z_out(last, (g,))
+                if n + 5 < NT:
+                    widen(n + 5, 0, 6)
+                if n < NT:
+                    if n >= HEAD:
+                        z_step(n, 0)
+                for c, g in outs:
+                    l_quant(c, g)
+                if n < NT:
+                    z_step(n, 1)
+                if 2 <= n < NT + 1:
+                    z_quant(n - 2)
+                if n == NT + 1:
+                    for g in range(G2):
+                        z_quant(last, (g,))
+                if n in (0, 1):
+                    th_scale(n)
+                    th_quant(n)
+                if 3 <= n < NT + 3:
+                    mm2(n - 3)
+                    add_acc(n - 3, 2 if n - 3 == last else 1)
+                if n >= 4:
+                    relu_store(n - 4, 2 if n - 4 == last else 1)
+                if n + 5 < NT:
+                    widen(n + 5, 6, 12)
+                if 1 <= n < NT:
+                    z_turn(n - 1)
+                if n == NT:
+                    for g in range(G2):
+                        z_turn(last, (g,))
+                c = (n + 3) // 2
+                if 2 <= c < NP:
+                    for g in (0, 1) if n % 2 else (2,):
+                        l_turn(c, g)
+                        turned.append((c, g))

@@ -17,16 +17,14 @@ ALU = mybir.AluOpType
 
 P = 128
 NT = V // P
-NP = NT // 2
 G1 = V // 512
 G2 = F // 512
 HEAD = 4
-WV = ()
-T1A = ()
-RG = ()
-RD = ()
-LWB = 6
-PB, TB, YB = 4, 3, 1
+VEC_FROM = 5
+Z_FROM = 5
+DOUBLE_FROM = 8
+L_AHEAD = 3
+TH_FROM = 2
 
 
 def tile_chebyshev_filter_last_term_d7_kernel(tc, L_bytes, L_scale, t1, t0, theta_bytes, theta_scale, acc, out):
@@ -34,358 +32,332 @@ def tile_chebyshev_filter_last_term_d7_kernel(tc, L_bytes, L_scale, t1, t0, thet
     with ExitStack() as ctx:
         keep = ctx.enter_context(tc.tile_pool(name="keep", bufs=1))
         work = ctx.enter_context(tc.tile_pool(name="work", bufs=3))
-        psum = ctx.enter_context(tc.psum_pool(name="psum", bufs=1))
+        psum = ctx.enter_context(tc.psum_pool(name="psum", bufs=4))
+        ctx.enter_context(tc.manual_schedule())
 
         ident = keep.tile([P, P], F32, name="ident")
         make_identity(nc, ident[:])
 
-        if True:
-            l_sc = keep.tile([P, NT * NT], F32, name="l_sc")
-            nc.scalar.dma_start(out=l_sc[:], in_=L_scale.rearrange("a b -> (a b)").partition_broadcast(P))
-            th_sc = keep.tile([P, G2, 4], F32, name="th_sc")
-            th_sc_rows = theta_scale.rearrange("(g q) o -> q g o", q=4)
+        l_sc = keep.tile([P, NT * NT], F32, name="l_sc")
+        th_sc = keep.tile([P, G2, 4], F32, name="th_sc")
+        l_rows = L_bytes.rearrange("(n p) j -> p n j", p=P)
+        t1_src = t1.rearrange("(g p t) f -> g p t f", p=P, t=4)
+        t0_rows = t0.rearrange("(n p) f -> p n f", p=P)
+        acc_rows = acc.rearrange("(n p) o -> p n o", p=P)
+        th_by = keep.tile([P, G2, 4, O], U8, name="th_by")
+        l_by, t1_raw, t0_sb, acc_sb = {}, {}, {}, {}
 
-            l_src = L_bytes.rearrange("(c a p) j -> c p a j", a=2, p=P)
-            t1_src = t1.rearrange("(g p t) f -> g p t f", p=P, t=4)
-            t0_src = t0.rearrange("(c a p) f -> c p a f", a=2, p=P)
-            acc_src = acc.rearrange("(c a p) o -> c p a o", a=4, p=P)
-            l_by = [keep.tile([P, 2, V], U8, name="l_by%d" % c) for c in range(NP)]
-            t1_raw = [[keep.tile([P, 4, 512], BF16, name="t1_raw%d_%d" % (g, h)) for h in range(2)] for g in range(G1)]
-            t0_sb = [keep.tile([P, 2, F], BF16, name="t0_sb%d" % c) for c in range(NP)]
-            acc_sb = [keep.tile([P, 4, O], BF16, name="acc_sb%d" % c) for c in range(3)]
-            th_by = keep.tile([P, G2, 4, O], U8, name="th_by")
+        def load_rows(store, rows, dtype, name, n0, n1):
+            tl = keep.tile([P, n1 - n0, rows.shape[2]], dtype, name="%s%d" % (name, n0))
+            nc.sync.dma_start(out=tl[:], in_=rows[:, n0:n1, :])
+            for n in range(n0, n1):
+                store[n] = tl[:, n - n0, :]
 
-            def load_l(c):
-                nc.sync.dma_start(out=l_by[c][:], in_=l_src[c])
+        def load_l(n0, n1):
+            load_rows(l_by, l_rows, U8, "l_by", n0, n1)
 
-            def load_t1(g, h):
-                nc.sync.dma_start(out=t1_raw[g][h][:], in_=t1_src[g][:, :, 512 * h : 512 * h + 512])
+        def load_t0(n0, n1):
+            load_rows(t0_sb, t0_rows, BF16, "t0_sb", n0, n1)
 
-            def load_t0(c):
-                nc.sync.dma_start(out=t0_sb[c][:], in_=t0_src[c])
+        def load_acc(n0, n1):
+            load_rows(acc_sb, acc_rows, BF16, "acc_sb", n0, n1)
 
-            def load_acc(c):
-                nc.sync.dma_start(out=acc_sb[c][:], in_=acc_src[c])
+        def load_t1(g, f0, f1):
+            tl = keep.tile([P, 4, f1 - f0], BF16, name="t1_raw%d_%d" % (g, f0))
+            nc.sync.dma_start(out=tl[:], in_=t1_src[g][:, :, f0:f1])
+            for f in range(f0, f1, 256):
+                t1_raw[g, f // 256] = tl[:, :, f - f0 : f - f0 + 256]
 
-            nc.sync.dma_start(out=l_by[0][:, 0, :], in_=l_src[0][:, 0, :])
-            for f0 in (0, 256):
-                nc.sync.dma_start(out=t1_raw[0][0][:, :, f0 : f0 + 256], in_=t1_src[0][:, :, f0 : f0 + 256])
-            nc.sync.dma_start(out=l_by[0][:, 1, :], in_=l_src[0][:, 1, :])
-            load_t1(1, 0)
-            load_l(1)
-            load_t1(2, 0)
-            load_t1(0, 1)
-            load_t0(0)
-            load_t1(1, 1)
-            load_t1(2, 1)
-            load_l(2)
-            load_t0(1)
+        nc.scalar.dma_start(out=l_sc[:], in_=L_scale.rearrange("a b -> (a b)").partition_broadcast(P))
+        load_l(0, 1)
+        load_l(1, 2)
+        load_t1(0, 0, 512)
+        load_l(2, 3)
+        load_t1(0, 512, F)
+        load_t1(1, 0, F)
+        load_l(3, 4)
+        load_t1(2, 0, F)
+        load_l(4, 6)
+        load_t0(0, 2)
+        load_t0(2, 4)
+        rows = theta_scale.rearrange("(g q) o -> q g o", q=4)
+        nc.sync.dma_start(out=th_by[:], in_=theta_bytes.rearrange("(g p t) o -> p g t o", p=P, t=4))
+        for q in range(4):
+            nc.sync.dma_start(out=th_sc[32 * q : 32 * q + 32], in_=rows[q].partition_broadcast(32))
+        load_l(6, 9)
+        load_t0(4, 6)
+        load_l(9, 12)
+        load_t0(6, 9)
+        load_acc(0, 4)
+        load_t0(9, 12)
+        load_acc(4, 8)
+        load_acc(8, 12)
+
+        t1_il, t1_mx = {}, {}
+
+        def t1_copy(g, h):
+            il = work.tile([P, 512, 4], BF16, name="t1_il", bufs=2, align_bytes=64)
+            for i in range(2):
+                nc.vector.tensor_copy(
+                    out=il[:, 256 * i : 256 * (i + 1), :].rearrange("p (c i) t -> p c t i", i=4),
+                    in_=t1_raw[g, 2 * h + i].rearrange("p t (c i) -> p c t i", i=4),
+                )
+            t1_il[g, h] = il
+
+        def t1_quant(g, h):
+            q = keep.tile([P, 512], U32, name="t1_q%d_%d" % (g, h), align_bytes=64)
+            s = keep.tile([P, 512], U8, name="t1_s%d_%d" % (g, h), align_bytes=64)
+            nc.vector.quantize_mx(out=q[:].bitcast(FP8X4), scales=s[:], in_=t1_il[g, h][:].rearrange("p f t -> p (f t)"))
+            t1_mx[g, h] = (q, s)
+
+        l_w, l_ps, l_il, l_mx = {}, {}, {}, {}
+
+        def on_vector(n, g):
+            return n == 0 or (n >= VEC_FROM and g == G1 - 1)
+
+        def widen(n, g):
+            wide = work.tile([P, 512], BF16, name="l_w%d" % g, bufs=3)
+            src = l_by[n].bitcast(FP8)
             for q in range(4):
-                nc.sync.dma_start(out=th_sc[32 * q : 32 * q + 32], in_=th_sc_rows[q].partition_broadcast(32))
-            nc.sync.dma_start(out=th_by[:], in_=theta_bytes.rearrange("(g p t) o -> p g t o", p=P, t=4))
-            load_l(3)
-            load_t0(2)
-            load_acc(0)
-            load_l(4)
-            load_l(5)
-            load_t0(3)
-            load_acc(1)
-            load_t0(4)
-            load_t0(5)
-            load_acc(2)
-
-            t1_mx = {}
-            t1_il = {}
-
-            def t1_copy(g, h, parts=1):
-                act = (g, h) in T1A
-                il = work.tile([P, 512, 4], BF16, name="t1_il", align_bytes=64)
-                w = 512 // parts
-                for i in range(parts):
-                    dst, src = il[:, i * w : i * w + w, :], t1_raw[g][h][:, :, i * w : i * w + w].rearrange("p t f -> p f t")
-                    if act:
-                        nc.scalar.copy(out=dst, in_=src)
-                    else:
-                        nc.vector.tensor_copy(out=dst, in_=src)
-                t1_il[g, h] = il
-
-            def t1_quant(g, h):
-                q = keep.tile([P, 512], U32, name="t1_q%d_%d" % (g, h), align_bytes=64)
-                s = keep.tile([P, 512], U8, name="t1_s%d_%d" % (g, h), align_bytes=64)
-                nc.vector.quantize_mx(out=q[:].bitcast(FP8X4), scales=s[:], in_=t1_il[g, h][:].rearrange("p f t -> p (f t)"))
-                t1_mx[g, h] = (q, s)
-
-            l_w = {}
-            l_ps = {}
-            l_il = {}
-            l_mx = {}
-
-            def widen(n, b0=0, b1=NT):
-                if n not in l_w:
-                    l_w[n] = work.tile([P, V], BF16, name="l_w", bufs=LWB)
-                src = l_by[n // 2][:, n % 2, :].bitcast(FP8)
-                for b in range(b0, b1):
-                    k = NT * n + b
-                    if n in WV:
-                        g, q = divmod(b, 4)
-                        nc.vector.tensor_scalar(
-                            out=l_w[n][:].rearrange("p (g u m e) -> p g m u e", g=G1, u=2, e=2)[:, g, 32 * q : 32 * q + 32],
-                            in0=src[:, P * b : P * b + P].rearrange("p (m u e) -> p m u e", u=2, e=2),
-                            scalar1=l_sc[:, k : k + 1],
-                            scalar2=None,
-                            op0=ALU.mult,
-                        )
-                    else:
-                        nc.scalar.activation(
-                            out=l_w[n][:, P * b : P * b + P],
-                            in_=src[:, P * b : P * b + P],
-                            func=ACT.Copy,
-                            scale=l_sc[:, k : k + 1],
-                        )
-
-            def l_turn(c, g):
-                ps = psum.tile([P, 2, 2, P], F32, name="turn", bufs=TB)
-                for a in range(2):
-                    words = l_w[2 * c + a][:].bitcast(F32)
-                    for u in range(2):
-                        if 2 * c + a in WV:
-                            part = words[:, 256 * g + 128 * u : 256 * g + 128 * u + 128]
-                        else:
-                            part = words[:, 256 * g + u : 256 * (g + 1) : 2]
-                        nc.tensor.transpose(ps[:, a, u, :], part, ident[:])
-                l_ps[c, g] = ps
-
-            def l_out(c, g):
-                il = work.tile([P, 1024], BF16, name="l_il", bufs=6, align_bytes=64)
-                nc.scalar.copy(
-                    out=il[:].bitcast(F32).rearrange("p (a i u) -> p a i u", a=2, u=2),
-                    in_=l_ps[c, g][:].rearrange("p a u i -> p a i u"),
-                )
-                l_il[c, g] = il
-
-            def l_quant(c, g):
-                q = work.tile([P, 256], U32, name="l_q%d" % g, bufs=4, align_bytes=64)
-                s = work.tile([P, 256], U8, name="l_s%d" % g, bufs=4, align_bytes=64)
-                nc.vector.quantize_mx(out=q[:].bitcast(FP8X4), scales=s[:], in_=l_il[c, g][:])
-                l_mx[c, g] = (q, s)
-
-            p_ps = {}
-            z_sb = {}
-
-            def mm1(n, h):
-                ps = psum.tile([P, 512], F32, name="prod", bufs=PB)
-                cols = slice(P * (n % 2), P * (n % 2) + P)
-                for g in range(G1):
-                    lq, ls = l_mx[n // 2, g]
-                    tq, ts = t1_mx[g, h]
-                    nc.tensor.matmul_mx(
-                        out=ps[:],
-                        lhsT=lq[:, cols].bitcast(FP8X4),
-                        lhsT_scale=ls[:, cols],
-                        rhs=tq[:].bitcast(FP8X4),
-                        rhs_scale=ts[:],
-                        start=(g == 0),
-                        stop=(g == G1 - 1),
-                    )
-                p_ps[n, h] = ps
-
-            def z_step(n, h):
-                if n not in z_sb:
-                    z_sb[n] = work.tile([P, G2, 2, 256], BF16, name="z_sb", bufs=6)
-                pv = p_ps[n, h][:].rearrange("p (m u e) -> p u m e", u=2, e=2)
-                tv = t0_sb[n // 2][:, n % 2, 512 * h : 512 * h + 512].rearrange("p (m u e) -> p u m e", u=2, e=2)
-                for u in range(2):
-                    nc.vector.scalar_tensor_tensor(
-                        out=z_sb[n][:, h, u, :].rearrange("p (m e) -> p m e", e=2),
-                        in0=pv[:, u],
-                        scalar=2.0,
-                        in1=tv[:, u],
-                        op0=ALU.mult,
-                        op1=ALU.subtract,
-                    )
-
-            zt_ps = {}
-            z_il = {}
-            z_mx = {}
-
-            def z_turn(n, gs=(0, 1)):
-                if n not in zt_ps:
-                    zt_ps[n] = psum.tile([P, G2, 2, P], F32, name="turn", bufs=TB)
-                for g in gs:
-                    for u in range(2):
-                        nc.tensor.transpose(zt_ps[n][:, g, u, :], z_sb[n][:, g, u, :].bitcast(F32), ident[:])
-
-            def z_out(n, gs=(0, 1)):
-                if n not in z_il:
-                    z_il[n] = work.tile([P, 1024], BF16, name="z_il", align_bytes=64)
-                a, b = gs[0], gs[-1] + 1
-                nc.scalar.copy(
-                    out=z_il[n][:].bitcast(F32).rearrange("p (g i u) -> p g i u", g=2, u=2)[:, a:b],
-                    in_=zt_ps[n][:].rearrange("p g u i -> p g i u")[:, a:b],
-                )
-
-            def z_quant(n, gs=(0, 1)):
-                if n not in z_mx:
-                    q = work.tile([P, 256], U32, name="z_q", align_bytes=64)
-                    s = work.tile([P, 256], U8, name="z_s", align_bytes=64)
-                    z_mx[n] = (q, s)
-                q, s = z_mx[n]
-                a, b = P * gs[0], P * (gs[-1] + 1)
-                nc.vector.quantize_mx(out=q[:, a:b].bitcast(FP8X4), scales=s[:, a:b], in_=z_il[n][:, 4 * a : 4 * b])
-
-            th_w = keep.tile([P, G2, 4, O], BF16, name="th_w")
-            th_il = keep.tile([P, G2, O, 4], BF16, name="th_il", align_bytes=64)
-            th_q = keep.tile([P, G2, O], U32, name="th_q", align_bytes=64)
-            th_s = keep.tile([P, G2, O], U8, name="th_s", align_bytes=64)
-
-            def th_widen(g):
-                nc.scalar.copy(
-                    out=th_w[:, g].rearrange("p t o -> p (t o)"), in_=th_by[:, g].rearrange("p t o -> p (t o)").bitcast(FP8)
-                )
-
-            def th_scale(g):
-                for b in range(4):
+                b = 4 * g + q
+                sc = l_sc[:, NT * n + b : NT * n + b + 1]
+                if on_vector(n, g):
                     nc.vector.tensor_scalar(
-                        out=th_il[:, g, P * b : P * b + P, :],
-                        in0=th_w[:, g, :, P * b : P * b + P].rearrange("p t o -> p o t"),
-                        scalar1=th_sc[:, g, b : b + 1],
+                        out=wide[:].rearrange("p (u m e) -> p m u e", u=2, e=2)[:, 32 * q : 32 * q + 32],
+                        in0=src[:, P * b : P * b + P].rearrange("p (m u e) -> p m u e", u=2, e=2),
+                        scalar1=sc,
                         scalar2=None,
                         op0=ALU.mult,
                     )
+                else:
+                    nc.scalar.activation(out=wide[:, P * q : P * q + P], in_=src[:, P * b : P * b + P], func=ACT.Copy, scale=sc)
+            l_w[n, g] = wide
 
-            def th_quant(g):
-                nc.vector.quantize_mx(
-                    out=th_q[:, g].bitcast(FP8X4), scales=th_s[:, g], in_=th_il[:, g].rearrange("p o t -> p (o t)")
+        def l_turn(n, gs):
+            ps = psum.tile([P, 2, 2, P], F32, name="turn")
+            for a, g in enumerate(gs):
+                words = l_w[n, g][:].bitcast(F32)
+                for u in range(2):
+                    part = words[:, P * u : P * u + P] if on_vector(n, g) else words[:, u:256:2]
+                    nc.tensor.transpose(ps[:, a, u, :], part, ident[:])
+            l_ps[n, gs] = ps
+
+        def l_out(n, gs):
+            if n not in l_il:
+                l_il[n] = work.tile([P, V], BF16, name="l_il", bufs=3, align_bytes=64)
+            nc.scalar.copy(
+                out=l_il[n][:].bitcast(F32).rearrange("p (g i u) -> p g i u", g=G1, u=2)[:, gs[0] : gs[-1] + 1],
+                in_=l_ps[n, gs][:, : len(gs)].rearrange("p a u i -> p a i u"),
+            )
+
+        def l_quant(n):
+            q = work.tile([P, G1 * P], U32, name="l_q", bufs=HEAD + 2, align_bytes=64)
+            s = work.tile([P, G1 * P], U8, name="l_s", bufs=HEAD + 2, align_bytes=64)
+            nc.vector.quantize_mx(out=q[:].bitcast(FP8X4), scales=s[:], in_=l_il[n][:])
+            l_mx[n] = (q, s)
+
+        p_ps, z_sb, zt_ps, z_il, z_mx = {}, {}, {}, {}, {}
+
+        def mm1(n, h, gs=range(G1)):
+            if (n, h) not in p_ps:
+                p_ps[n, h] = psum.tile([P, 512], F32, name="sums")
+            ps = p_ps[n, h]
+            lq, ls = l_mx[n]
+            for g in gs:
+                cols = slice(P * g, P * g + P)
+                tq, ts = t1_mx[g, h]
+                nc.tensor.matmul_mx(
+                    out=ps[:],
+                    lhsT=lq[:, cols].bitcast(FP8X4),
+                    lhsT_scale=ls[:, cols],
+                    rhs=tq[:].bitcast(FP8X4),
+                    rhs_scale=ts[:],
+                    start=(g == 0),
+                    stop=(g == G1 - 1),
                 )
 
-            y_ps = {}
-            sums = {}
+        def z_step(n, h):
+            z = work.tile([P, 2, 256], BF16, name="z_sb%d" % h, bufs=9)
+            pv = p_ps[n, h][:].rearrange("p (m u e) -> p u m e", u=2, e=2)
+            tv = t0_sb[n][:, 512 * h : 512 * h + 512].rearrange("p (m u e) -> p u m e", u=2, e=2)
+            for u in range(2):
+                nc.vector.scalar_tensor_tensor(
+                    out=z[:, u, :].rearrange("p (m e) -> p m e", e=2),
+                    in0=pv[:, u],
+                    scalar=2.0,
+                    in1=tv[:, u],
+                    op0=ALU.mult,
+                    op1=ALU.subtract,
+                )
+            z_sb[n, h] = z
 
-            def mm2(n, gs=(0, 1)):
-                if n not in y_ps:
-                    y_ps[n] = psum.tile([P, O], F32, name="y", bufs=YB)
-                zq, zs = z_mx[n]
-                for g in gs:
-                    cols = slice(P * g, P * g + P)
-                    nc.tensor.matmul_mx(
-                        out=y_ps[n][:],
-                        lhsT=zq[:, cols].bitcast(FP8X4),
-                        lhsT_scale=zs[:, cols],
-                        rhs=th_q[:, g].bitcast(FP8X4),
-                        rhs_scale=th_s[:, g],
-                        start=(g == 0),
-                        stop=(g == G2 - 1),
-                    )
+        def z_turn(n):
+            zt_ps[n] = psum.tile([P, G2, 2, P], F32, name="turn")
+            for g in range(G2):
+                for u in range(2):
+                    nc.tensor.transpose(zt_ps[n][:, g, u, :], z_sb[n, g][:, u, :].bitcast(F32), ident[:])
 
-            def add_acc(n, parts=1):
-                t = work.tile([P, O], F32, name="sums")
-                for i in range(parts):
-                    w = slice(i * O // parts, (i + 1) * O // parts)
-                    nc.vector.tensor_tensor(out=t[:, w], in0=y_ps[n][:, w], in1=acc_sb[n // 4][:, n % 4, w], op=ALU.add)
-                sums[n] = t
+        def z_out(n):
+            z_il[n] = work.tile([P, 1024], BF16, name="z_il", align_bytes=64)
+            nc.scalar.copy(
+                out=z_il[n][:].bitcast(F32).rearrange("p (g i u) -> p g i u", g=G2, u=2),
+                in_=zt_ps[n][:].rearrange("p g u i -> p g i u"),
+            )
 
-            def relu_store(n, parts=1):
-                r = work.tile([P, O], F32, name="res")
-                for i in range(parts):
-                    w = slice(i * O // parts, (i + 1) * O // parts)
-                    if n in RG:
-                        nc.gpsimd.tensor_scalar(out=r[:, w], in0=sums[n][:, w], scalar1=0.0, scalar2=0.0, op0=ALU.max, op1=ALU.add)
-                    elif n in RD:
-                        nc.vector.tensor_scalar(out=r[:, w], in0=sums[n][:, w], scalar1=0.0, scalar2=None, op0=ALU.max)
-                    else:
-                        nc.scalar.activation(out=r[:, w], in_=sums[n][:, w], func=ACT.Relu)
-                    nc.sync.dma_start(out=out[P * n : P * n + P, w], in_=r[:, w])
+        def z_quant(n):
+            q = work.tile([P, G2 * P], U32, name="z_q", bufs=5, align_bytes=64)
+            s = work.tile([P, G2 * P], U8, name="z_s", bufs=5, align_bytes=64)
+            nc.vector.quantize_mx(out=q[:].bitcast(FP8X4), scales=s[:], in_=z_il[n][:])
+            z_mx[n] = (q, s)
 
-            all_g = range(G1)
-            widen(0)
-            widen(1)
-            t1_copy(0, 0, parts=2)
-            t1_copy(1, 0)
-            t1_quant(0, 0)
-            for g in all_g:
-                l_turn(0, g)
-            widen(2, 0, 4)
-            for g in all_g:
-                l_out(0, g)
-            t1_copy(2, 0)
-            t1_quant(1, 0)
-            l_quant(0, 0)
-            l_quant(0, 1)
-            t1_quant(2, 0)
-            l_quant(0, 2)
-            mm1(0, 0)
-            mm1(1, 0)
-            widen(2, 4, 12)
-            widen(3)
-            for g in all_g:
-                l_turn(1, g)
-            t1_copy(0, 1)
-            z_step(0, 0)
-            t1_quant(0, 1)
-            z_step(1, 0)
-            t1_copy(1, 1)
-            for g in all_g:
-                l_out(1, g)
-            for g in all_g:
-                l_quant(1, g)
-            t1_quant(1, 1)
-            mm1(2, 0)
-            mm1(3, 0)
-            t1_copy(2, 1)
-            z_step(2, 0)
-            t1_quant(2, 1)
-            z_step(3, 0)
-            widen(4)
-            th_widen(0)
-            th_widen(1)
+        th_w = keep.tile([P, G2, 4, O], BF16, name="th_w")
+        th_il = keep.tile([P, G2, O, 4], BF16, name="th_il", align_bytes=64)
+        th_q = keep.tile([P, G2, O], U32, name="th_q", align_bytes=64)
+        th_s = keep.tile([P, G2, O], U8, name="th_s", align_bytes=64)
 
-            turned = []
-            last = NT - 1
-            for n in range(NT + 4):
-                if n < NT:
-                    if n >= HEAD:
-                        mm1(n, 0)
-                    mm1(n, 1)
-                outs = turned
-                turned = []
-                for c, g in outs:
-                    l_out(c, g)
-                if 2 <= n < NT + 1:
-                    z_out(n - 2)
-                if n == NT + 1:
-                    for g in range(G2):
-                        z_out(last, (g,))
-                if n + 5 < NT:
-                    widen(n + 5, 0, 6)
-                if n < NT:
-                    if n >= HEAD:
-                        z_step(n, 0)
-                for c, g in outs:
-                    l_quant(c, g)
-                if n < NT:
-                    z_step(n, 1)
-                if 2 <= n < NT + 1:
-                    z_quant(n - 2)
-                if n == NT + 1:
-                    for g in range(G2):
-                        z_quant(last, (g,))
-                if n in (0, 1):
-                    th_scale(n)
-                    th_quant(n)
-                if 3 <= n < NT + 3:
-                    mm2(n - 3)
-                    add_acc(n - 3, 2 if n - 3 == last else 1)
-                if n >= 4:
-                    relu_store(n - 4, 2 if n - 4 == last else 1)
-                if n + 5 < NT:
-                    widen(n + 5, 6, 12)
-                if 1 <= n < NT:
-                    z_turn(n - 1)
-                if n == NT:
-                    for g in range(G2):
-                        z_turn(last, (g,))
-                c = (n + 3) // 2
-                if 2 <= c < NP:
-                    for g in (0, 1) if n % 2 else (2,):
-                        l_turn(c, g)
-                        turned.append((c, g))
+        def th_widen(g):
+            nc.scalar.copy(out=th_w[:, g].rearrange("p t o -> p (t o)"), in_=th_by[:, g].rearrange("p t o -> p (t o)").bitcast(FP8))
+
+        def th_scale(g, bs):
+            for b in bs:
+                nc.vector.tensor_scalar(
+                    out=th_il[:, g, P * b : P * b + P, :].rearrange("p (c i) t -> p c t i", i=4),
+                    in0=th_w[:, g, :, P * b : P * b + P].rearrange("p t (c i) -> p c t i", i=4),
+                    scalar1=th_sc[:, g, b : b + 1],
+                    scalar2=None,
+                    op0=ALU.mult,
+                )
+
+        def th_quant(g):
+            nc.vector.quantize_mx(out=th_q[:, g].bitcast(FP8X4), scales=th_s[:, g], in_=th_il[:, g].rearrange("p o t -> p (o t)"))
+
+        y_ps, sums = {}, {}
+
+        def mm2(n):
+            y_ps[n] = psum.tile([P, O], F32, name="sums")
+            zq, zs = z_mx[n]
+            for g in range(G2):
+                cols = slice(P * g, P * g + P)
+                nc.tensor.matmul_mx(
+                    out=y_ps[n][:],
+                    lhsT=zq[:, cols].bitcast(FP8X4),
+                    lhsT_scale=zs[:, cols],
+                    rhs=th_q[:, g].bitcast(FP8X4),
+                    rhs_scale=th_s[:, g],
+                    start=(g == 0),
+                    stop=(g == G2 - 1),
+                )
+
+        def add_acc(n):
+            sums[n] = work.tile([P, O], F32, name="y_acc", bufs=4)
+            nc.vector.tensor_tensor(out=sums[n][:], in0=y_ps[n][:], in1=acc_sb[n], op=ALU.add)
+
+        def relu_store(n):
+            r = work.tile([P, O], F32, name="res", bufs=6)
+            nc.scalar.activation(out=r[:], in_=sums[n][:], func=ACT.Relu)
+            nc.sync.dma_start(out=out[P * n : P * n + P, :], in_=r[:])
+
+        def widen_on(n, vector):
+            if n < NT:
+                for g in range(G1):
+                    if on_vector(n, g) == vector:
+                        widen(n, g)
+
+        def turn_l(n):
+            l_turn(n, (0, 1))
+            l_turn(n, (2,))
+
+        def out_l(n):
+            l_out(n, (0, 1))
+            l_out(n, (2,))
+
+        widen_on(0, True)
+        widen_on(1, False)
+        turn_l(0)
+        t1_copy(0, 0)
+        out_l(0)
+        turn_l(1)
+        widen_on(2, False)
+        t1_copy(0, 1)
+        t1_quant(0, 0)
+        out_l(1)
+        turn_l(2)
+        l_quant(0)
+        t1_quant(0, 1)
+        widen_on(3, False)
+        t1_copy(1, 0)
+        l_quant(1)
+        t1_copy(1, 1)
+        t1_quant(1, 0)
+        out_l(2)
+        for n in range(2):
+            for h in range(G2):
+                mm1(n, h, (0,))
+        turn_l(3)
+        t1_copy(2, 0)
+        t1_quant(1, 1)
+        widen_on(4, False)
+        out_l(3)
+        for h in range(G2):
+            for n in range(2):
+                mm1(n, h, (1,))
+        turn_l(4)
+        t1_copy(2, 1)
+        t1_quant(2, 0)
+        l_quant(2)
+        t1_quant(2, 1)
+        widen_on(5, False)
+        out_l(4)
+        for h in range(G2):
+            for n in range(2):
+                mm1(n, h, (2,))
+        z_step(0, 0)
+        z_step(1, 0)
+        l_quant(3)
+        z_step(0, 1)
+        z_step(1, 1)
+        widen_on(5, True)
+
+        def second(s):
+            if s < Z_FROM:
+                return []
+            done = min(s, DOUBLE_FROM) - Z_FROM + 2 * max(0, s - DOUBLE_FROM)
+            return [n for n in range(done, done + (2 if s >= DOUBLE_FROM else 1)) if n < NT]
+
+        for s in range(2, NT + 4):
+            a = s + L_AHEAD
+            k = s - TH_FROM - 1
+            if k in (2, 4):
+                th_quant(k // 2 - 1)
+            if s < NT:
+                mm1(s, 0)
+                mm1(s, 1)
+            for n in second(s - 1):
+                z_quant(n)
+            if s < NT:
+                z_step(s, 0)
+            if a - 1 < NT:
+                l_quant(a - 1)
+            for n in second(s - 2):
+                mm2(n)
+            if s < NT:
+                z_step(s, 1)
+            if 0 <= k < 2 * G2:
+                th_scale(k // 2, (2 * (k % 2), 2 * (k % 2) + 1))
+            for n in second(s - 3):
+                relu_store(n)
+            for n in second(s):
+                z_turn(n)
+            if a < NT:
+                widen_on(a + 1, True)
+            for n in second(s - 2):
+                add_acc(n)
+            if a < NT:
+                turn_l(a)
+                widen_on(a + 1, False)
+            if k in (-1, 1):
+                th_widen((k + 1) // 2)
+            for n in second(s):
+                z_out(n)
+            if a < NT:
+                out_l(a)

@@ -21,10 +21,13 @@ G1 = V // 512
 G2 = F // 512
 HEAD = 4
 VEC_FROM = 5
-Z_FROM = 5
-DOUBLE_FROM = 8
+Z_FROM = 6
+Z_DOUBLE = 7
+Y_FROM = 8
+Y_DOUBLE = 9
+VEC_G = 2
 L_AHEAD = 3
-TH_FROM = 2
+TH_FROM = 1
 
 
 def tile_chebyshev_filter_last_term_d7_kernel(tc, L_bytes, L_scale, t1, t0, theta_bytes, theta_scale, acc, out):
@@ -69,14 +72,17 @@ def tile_chebyshev_filter_last_term_d7_kernel(tc, L_bytes, L_scale, t1, t0, thet
                 t1_raw[g, f // 256] = tl[:, :, f - f0 : f - f0 + 256]
 
         nc.scalar.dma_start(out=l_sc[:], in_=L_scale.rearrange("a b -> (a b)").partition_broadcast(P))
+        warm = keep.tile([P, 2], F32, name="warm")
+        nc.vector.memset(warm[:, 0:1], 0.0)
+        nc.scalar.activation(out=warm[:, 1:2], in_=warm[:, 0:1], func=ACT.Copy)
         load_l(0, 1)
-        load_l(1, 2)
         load_t1(0, 0, 512)
-        load_l(2, 3)
         load_t1(0, 512, F)
+        load_l(1, 2)
         load_t1(1, 0, F)
-        load_l(3, 4)
+        load_l(2, 3)
         load_t1(2, 0, F)
+        load_l(3, 4)
         load_l(4, 6)
         load_t0(0, 2)
         load_t0(2, 4)
@@ -113,7 +119,7 @@ def tile_chebyshev_filter_last_term_d7_kernel(tc, L_bytes, L_scale, t1, t0, thet
         l_w, l_ps, l_il, l_mx = {}, {}, {}, {}
 
         def on_vector(n, g):
-            return n == 0 or (n >= VEC_FROM and g == G1 - 1)
+            return (n == 0 and g > 0) or (n >= VEC_FROM and g >= VEC_G)
 
         def widen(n, g):
             wide = work.tile([P, 512], BF16, name="l_w%d" % g, bufs=3)
@@ -205,8 +211,8 @@ def tile_chebyshev_filter_last_term_d7_kernel(tc, L_bytes, L_scale, t1, t0, thet
             )
 
         def z_quant(n):
-            q = work.tile([P, G2 * P], U32, name="z_q", bufs=5, align_bytes=64)
-            s = work.tile([P, G2 * P], U8, name="z_s", bufs=5, align_bytes=64)
+            q = work.tile([P, G2 * P], U32, name="z_q", bufs=8, align_bytes=64)
+            s = work.tile([P, G2 * P], U8, name="z_s", bufs=8, align_bytes=64)
             nc.vector.quantize_mx(out=q[:].bitcast(FP8X4), scales=s[:], in_=z_il[n][:])
             z_mx[n] = (q, s)
 
@@ -215,8 +221,9 @@ def tile_chebyshev_filter_last_term_d7_kernel(tc, L_bytes, L_scale, t1, t0, thet
         th_q = keep.tile([P, G2, O], U32, name="th_q", align_bytes=64)
         th_s = keep.tile([P, G2, O], U8, name="th_s", align_bytes=64)
 
-        def th_widen(g):
-            nc.scalar.copy(out=th_w[:, g].rearrange("p t o -> p (t o)"), in_=th_by[:, g].rearrange("p t o -> p (t o)").bitcast(FP8))
+        def th_widen(g, u):
+            ts = slice(2 * u, 2 * u + 2)
+            nc.scalar.copy(out=th_w[:, g, ts].rearrange("p t o -> p (t o)"), in_=th_by[:, g, ts].rearrange("p t o -> p (t o)").bitcast(FP8))
 
         def th_scale(g, bs):
             for b in bs:
@@ -272,92 +279,93 @@ def tile_chebyshev_filter_last_term_d7_kernel(tc, L_bytes, L_scale, t1, t0, thet
             l_out(n, (2,))
 
         widen_on(0, True)
-        widen_on(1, False)
+        widen_on(0, False)
         turn_l(0)
         t1_copy(0, 0)
         out_l(0)
+        widen_on(1, False)
         turn_l(1)
-        widen_on(2, False)
-        t1_copy(0, 1)
         t1_quant(0, 0)
-        out_l(1)
-        turn_l(2)
+        t1_copy(0, 1)
         l_quant(0)
+        out_l(1)
         t1_quant(0, 1)
-        widen_on(3, False)
+        widen_on(2, False)
         t1_copy(1, 0)
         l_quant(1)
-        t1_copy(1, 1)
-        t1_quant(1, 0)
-        out_l(2)
         for n in range(2):
             for h in range(G2):
                 mm1(n, h, (0,))
-        turn_l(3)
+        turn_l(2)
+        t1_copy(1, 1)
+        t1_quant(1, 0)
+        out_l(2)
+        widen_on(3, False)
         t1_copy(2, 0)
         t1_quant(1, 1)
-        widen_on(4, False)
-        out_l(3)
         for h in range(G2):
             for n in range(2):
                 mm1(n, h, (1,))
-        turn_l(4)
+        turn_l(3)
         t1_copy(2, 1)
         t1_quant(2, 0)
+        widen_on(4, False)
+        out_l(3)
         l_quant(2)
         t1_quant(2, 1)
-        widen_on(5, False)
-        out_l(4)
         for h in range(G2):
             for n in range(2):
                 mm1(n, h, (2,))
+        turn_l(4)
+        widen_on(5, False)
+        out_l(4)
         z_step(0, 0)
         z_step(1, 0)
-        l_quant(3)
         z_step(0, 1)
         z_step(1, 1)
+        l_quant(3)
         widen_on(5, True)
+        th_widen(0, 0)
 
-        def second(s):
-            if s < Z_FROM:
+        def spread(s, first, double):
+            if s < first:
                 return []
-            done = min(s, DOUBLE_FROM) - Z_FROM + 2 * max(0, s - DOUBLE_FROM)
-            return [n for n in range(done, done + (2 if s >= DOUBLE_FROM else 1)) if n < NT]
+            done = min(s, double) - first + 2 * max(0, s - double)
+            return [n for n in range(done, done + (2 if s >= double else 1)) if n < NT]
 
-        for s in range(2, NT + 4):
+        for s in range(2, NT + 5):
             a = s + L_AHEAD
-            k = s - TH_FROM - 1
-            if k in (2, 4):
-                th_quant(k // 2 - 1)
+            k = s - TH_FROM
             if s < NT:
                 mm1(s, 0)
                 mm1(s, 1)
-            for n in second(s - 1):
-                z_quant(n)
-            if s < NT:
-                z_step(s, 0)
-            if a - 1 < NT:
-                l_quant(a - 1)
-            for n in second(s - 2):
+            for n in spread(s, Y_FROM, Y_DOUBLE):
                 mm2(n)
             if s < NT:
+                z_step(s, 0)
+            for n in spread(s - 1, Z_FROM, Z_DOUBLE):
+                z_quant(n)
+            if s < NT:
                 z_step(s, 1)
-            if 0 <= k < 2 * G2:
-                th_scale(k // 2, (2 * (k % 2), 2 * (k % 2) + 1))
-            for n in second(s - 3):
+            if a - 1 < NT:
+                l_quant(a - 1)
+            for n in spread(s - 1, Y_FROM, Y_DOUBLE):
                 relu_store(n)
-            for n in second(s):
+            for n in spread(s, Z_FROM, Z_DOUBLE):
                 z_turn(n)
-            if a < NT:
-                widen_on(a + 1, True)
-            for n in second(s - 2):
+            for n in spread(s, Y_FROM, Y_DOUBLE):
                 add_acc(n)
             if a < NT:
                 turn_l(a)
+                widen_on(a + 1, True)
                 widen_on(a + 1, False)
-            if k in (-1, 1):
-                th_widen((k + 1) // 2)
-            for n in second(s):
+            if k in (4, 6):
+                th_quant(k // 2 - 2)
+            if 2 <= k < 2 * G2 + 2:
+                th_scale(k // 2 - 1, (2 * (k % 2), 2 * (k % 2) + 1))
+            for n in spread(s, Z_FROM, Z_DOUBLE):
                 z_out(n)
             if a < NT:
                 out_l(a)
+            if 0 <= k < 2 * G2:
+                th_widen(k // 2, k % 2)

@@ -35,11 +35,18 @@ def tile_chebyshev_filter_last_term_d7_kernel(tc, L_bytes, L_scale, t1, t0, thet
     with ExitStack() as ctx:
         keep = ctx.enter_context(tc.tile_pool(name="keep", bufs=1))
         work = ctx.enter_context(tc.tile_pool(name="work", bufs=3))
-        psum = ctx.enter_context(tc.psum_pool(name="psum", bufs=4))
+        psum = ctx.enter_context(tc.psum_pool(name="psum", bufs=1))
         ctx.enter_context(tc.manual_schedule())
 
         ident = keep.tile([P, P], F32, name="ident")
         make_identity(nc, ident[:])
+
+        sum_banks, turn_banks = [0, 1, 2, 3, 4], [5, 6, 7]
+
+        def next_bank(ring, shape):
+            b = ring.pop(0)
+            ring.append(b)
+            return psum.tile(shape, F32, name="bank%d" % b)
 
         l_sc = keep.tile([P, NT * NT], F32, name="l_sc")
         th_sc = keep.tile([P, G2, 4], F32, name="th_sc")
@@ -77,12 +84,12 @@ def tile_chebyshev_filter_last_term_d7_kernel(tc, L_bytes, L_scale, t1, t0, thet
         nc.scalar.activation(out=warm[:, 1:2], in_=warm[:, 0:1], func=ACT.Copy)
         load_l(0, 1)
         load_t1(0, 0, 512)
-        load_t1(0, 512, F)
         load_l(1, 2)
-        load_t1(1, 0, F)
+        load_t1(0, 512, F)
         load_l(2, 3)
-        load_t1(2, 0, F)
+        load_t1(1, 0, F)
         load_l(3, 4)
+        load_t1(2, 0, F)
         load_l(4, 6)
         load_t0(0, 2)
         load_t0(2, 4)
@@ -101,10 +108,10 @@ def tile_chebyshev_filter_last_term_d7_kernel(tc, L_bytes, L_scale, t1, t0, thet
 
         t1_il, t1_mx = {}, {}
 
-        def t1_copy(g, h):
-            il = work.tile([P, 512, 4], BF16, name="t1_il", bufs=2, align_bytes=64)
+        def t1_copy(g, h, copy=nc.vector.tensor_copy):
+            il = work.tile([P, 512, 4], BF16, name="t1_il", bufs=3, align_bytes=64)
             for i in range(2):
-                nc.vector.tensor_copy(
+                copy(
                     out=il[:, 256 * i : 256 * (i + 1), :].rearrange("p (c i) t -> p c t i", i=4),
                     in_=t1_raw[g, 2 * h + i].rearrange("p t (c i) -> p c t i", i=4),
                 )
@@ -140,7 +147,7 @@ def tile_chebyshev_filter_last_term_d7_kernel(tc, L_bytes, L_scale, t1, t0, thet
             l_w[n, g] = wide
 
         def l_turn(n, gs):
-            ps = psum.tile([P, 2, 2, P], F32, name="turn")
+            ps = next_bank(turn_banks, [P, 2, 2, P])
             for a, g in enumerate(gs):
                 words = l_w[n, g][:].bitcast(F32)
                 for u in range(2):
@@ -166,7 +173,7 @@ def tile_chebyshev_filter_last_term_d7_kernel(tc, L_bytes, L_scale, t1, t0, thet
 
         def mm1(n, h, gs=range(G1)):
             if (n, h) not in p_ps:
-                p_ps[n, h] = psum.tile([P, 512], F32, name="sums")
+                p_ps[n, h] = next_bank(sum_banks, [P, 512])
             ps = p_ps[n, h]
             lq, ls = l_mx[n]
             for g in gs:
@@ -198,7 +205,7 @@ def tile_chebyshev_filter_last_term_d7_kernel(tc, L_bytes, L_scale, t1, t0, thet
             z_sb[n, h] = z
 
         def z_turn(n):
-            zt_ps[n] = psum.tile([P, G2, 2, P], F32, name="turn")
+            zt_ps[n] = next_bank(turn_banks, [P, G2, 2, P])
             for g in range(G2):
                 for u in range(2):
                     nc.tensor.transpose(zt_ps[n][:, g, u, :], z_sb[n, g][:, u, :].bitcast(F32), ident[:])
@@ -241,7 +248,7 @@ def tile_chebyshev_filter_last_term_d7_kernel(tc, L_bytes, L_scale, t1, t0, thet
         y_ps, sums = {}, {}
 
         def mm2(n):
-            y_ps[n] = psum.tile([P, O], F32, name="sums")
+            y_ps[n] = next_bank(sum_banks, [P, O])
             zq, zs = z_mx[n]
             for g in range(G2):
                 cols = slice(P * g, P * g + P)
@@ -255,14 +262,14 @@ def tile_chebyshev_filter_last_term_d7_kernel(tc, L_bytes, L_scale, t1, t0, thet
                     stop=(g == G2 - 1),
                 )
 
-        def add_acc(n):
-            sums[n] = work.tile([P, O], F32, name="y_acc", bufs=4)
-            nc.vector.tensor_tensor(out=sums[n][:], in0=y_ps[n][:], in1=acc_sb[n], op=ALU.add)
+        def add_acc(n, cols=slice(0, O)):
+            sums[n, cols.start] = work.tile([P, cols.stop - cols.start], F32, name="y_acc", bufs=4)
+            nc.vector.tensor_tensor(out=sums[n, cols.start][:], in0=y_ps[n][:, cols], in1=acc_sb[n][:, cols], op=ALU.add)
 
-        def relu_store(n):
-            r = work.tile([P, O], F32, name="res", bufs=6)
-            nc.scalar.activation(out=r[:], in_=sums[n][:], func=ACT.Relu)
-            nc.sync.dma_start(out=out[P * n : P * n + P, :], in_=r[:])
+        def relu_store(n, cols=slice(0, O)):
+            r = work.tile([P, cols.stop - cols.start], F32, name="res", bufs=6)
+            nc.scalar.activation(out=r[:], in_=sums[n, cols.start][:], func=ACT.Relu)
+            nc.sync.dma_start(out=out[P * n : P * n + P, cols], in_=r[:])
 
         def widen_on(n, vector):
             if n < NT:
@@ -282,50 +289,54 @@ def tile_chebyshev_filter_last_term_d7_kernel(tc, L_bytes, L_scale, t1, t0, thet
         widen_on(0, False)
         turn_l(0)
         t1_copy(0, 0)
-        out_l(0)
         widen_on(1, False)
+        out_l(0)
         turn_l(1)
         t1_quant(0, 0)
         t1_copy(0, 1)
+        widen(2, 0)
         l_quant(0)
         out_l(1)
         t1_quant(0, 1)
-        widen_on(2, False)
-        t1_copy(1, 0)
         l_quant(1)
         for n in range(2):
             for h in range(G2):
                 mm1(n, h, (0,))
+        widen(2, 1)
+        widen(2, 2)
         turn_l(2)
+        t1_copy(1, 0)
+        widen_on(3, False)
         t1_copy(1, 1)
         t1_quant(1, 0)
         out_l(2)
-        widen_on(3, False)
-        t1_copy(2, 0)
+        turn_l(3)
         t1_quant(1, 1)
         for h in range(G2):
             for n in range(2):
                 mm1(n, h, (1,))
-        turn_l(3)
-        t1_copy(2, 1)
-        t1_quant(2, 0)
+        t1_copy(2, 0)
+        l_quant(2)
         widen_on(4, False)
         out_l(3)
-        l_quant(2)
-        t1_quant(2, 1)
-        for h in range(G2):
-            for n in range(2):
-                mm1(n, h, (2,))
+        mm1(2, 0, (0, 1))
+        t1_copy(2, 1)
+        t1_quant(2, 0)
         turn_l(4)
+        t1_quant(2, 1)
+        for n in range(3):
+            mm1(n, 0, (2,))
+        for n in range(2):
+            mm1(n, 1, (2,))
         widen_on(5, False)
         out_l(4)
+        th_widen(0, 0)
+        l_quant(3)
         z_step(0, 0)
+        widen_on(5, True)
         z_step(1, 0)
         z_step(0, 1)
         z_step(1, 1)
-        l_quant(3)
-        widen_on(5, True)
-        th_widen(0, 0)
 
         def spread(s, first, double):
             if s < first:
@@ -333,12 +344,15 @@ def tile_chebyshev_filter_last_term_d7_kernel(tc, L_bytes, L_scale, t1, t0, thet
             done = min(s, double) - first + 2 * max(0, s - double)
             return [n for n in range(done, done + (2 if s >= double else 1)) if n < NT]
 
-        for s in range(2, NT + 5):
+        for s in range(2, NT - 1):
             a = s + L_AHEAD
             k = s - TH_FROM
             if s < NT:
-                mm1(s, 0)
+                if (s, 0) not in p_ps:
+                    mm1(s, 0)
                 mm1(s, 1)
+            if s == 2:
+                turn_banks.append(sum_banks.pop(0))
             for n in spread(s, Y_FROM, Y_DOUBLE):
                 mm2(n)
             if s < NT:
@@ -369,3 +383,40 @@ def tile_chebyshev_filter_last_term_d7_kernel(tc, L_bytes, L_scale, t1, t0, thet
                 out_l(a)
             if 0 <= k < 2 * G2:
                 th_widen(k // 2, k % 2)
+
+        last = NT - 1
+        mm2(last - 6)
+        mm2(last - 5)
+        mm1(last, 0)
+        mm1(last, 1)
+        z_quant(last - 4)
+        z_quant(last - 3)
+        relu_store(last - 8)
+        relu_store(last - 7)
+        add_acc(last - 6)
+        z_step(last, 0)
+        z_step(last, 1)
+        add_acc(last - 5)
+        z_turn(last - 2)
+        z_turn(last - 1)
+        z_out(last - 2)
+        z_out(last - 1)
+        z_turn(last)
+        mm2(last - 4)
+        mm2(last - 3)
+        z_out(last)
+        relu_store(last - 6)
+        relu_store(last - 5)
+        z_quant(last - 2)
+        z_quant(last - 1)
+        add_acc(last - 4)
+        z_quant(last)
+        for n in range(last - 2, NT):
+            mm2(n)
+        relu_store(last - 4)
+        for n in range(last - 3, last):
+            add_acc(n)
+            relu_store(n)
+        for cols in (slice(0, O // 2), slice(O // 2, O)):
+            add_acc(last, cols)
+            relu_store(last, cols)

@@ -20,7 +20,7 @@ NT = V // P
 G1 = V // 512
 G2 = F // 512
 HEAD = 4
-VEC_FROM = 5
+VEC_FROM = 4
 Z_FROM = 6
 Z_DOUBLE = 7
 Y_FROM = 8
@@ -108,14 +108,14 @@ def tile_chebyshev_filter_last_term_d7_kernel(tc, L_bytes, L_scale, t1, t0, thet
 
         t1_il, t1_mx = {}, {}
 
-        def t1_copy(g, h, copy=nc.vector.tensor_copy):
-            il = work.tile([P, 512, 4], BF16, name="t1_il", bufs=3, align_bytes=64)
-            for i in range(2):
+        def t1_copy(g, h, parts=(0, 1), copy=nc.vector.tensor_copy):
+            if (g, h) not in t1_il:
+                t1_il[g, h] = work.tile([P, 512, 4], BF16, name="t1_il", bufs=4, align_bytes=64)
+            for i in parts:
                 copy(
-                    out=il[:, 256 * i : 256 * (i + 1), :].rearrange("p (c i) t -> p c t i", i=4),
+                    out=t1_il[g, h][:, 256 * i : 256 * (i + 1), :].rearrange("p (c i) t -> p c t i", i=4),
                     in_=t1_raw[g, 2 * h + i].rearrange("p t (c i) -> p c t i", i=4),
                 )
-            t1_il[g, h] = il
 
         def t1_quant(g, h):
             q = keep.tile([P, 512], U32, name="t1_q%d_%d" % (g, h), align_bytes=64)
@@ -210,18 +210,23 @@ def tile_chebyshev_filter_last_term_d7_kernel(tc, L_bytes, L_scale, t1, t0, thet
                 for u in range(2):
                     nc.tensor.transpose(zt_ps[n][:, g, u, :], z_sb[n, g][:, u, :].bitcast(F32), ident[:])
 
-        def z_out(n):
-            z_il[n] = work.tile([P, 1024], BF16, name="z_il", align_bytes=64)
+        def z_out(n, g=None):
+            if n not in z_il:
+                z_il[n] = work.tile([P, 1024], BF16, name="z_il", bufs=4, align_bytes=64)
+            gs = slice(0, G2) if g is None else slice(g, g + 1)
             nc.scalar.copy(
-                out=z_il[n][:].bitcast(F32).rearrange("p (g i u) -> p g i u", g=G2, u=2),
-                in_=zt_ps[n][:].rearrange("p g u i -> p g i u"),
+                out=z_il[n][:].bitcast(F32).rearrange("p (g i u) -> p g i u", g=G2, u=2)[:, gs],
+                in_=zt_ps[n][:].rearrange("p g u i -> p g i u")[:, gs],
             )
 
-        def z_quant(n):
-            q = work.tile([P, G2 * P], U32, name="z_q", bufs=8, align_bytes=64)
-            s = work.tile([P, G2 * P], U8, name="z_s", bufs=8, align_bytes=64)
-            nc.vector.quantize_mx(out=q[:].bitcast(FP8X4), scales=s[:], in_=z_il[n][:])
-            z_mx[n] = (q, s)
+        def z_quant(n, g=None):
+            if n not in z_mx:
+                q = work.tile([P, G2 * P], U32, name="z_q", bufs=8, align_bytes=64)
+                s = work.tile([P, G2 * P], U8, name="z_s", bufs=8, align_bytes=64)
+                z_mx[n] = (q, s)
+            q, s = z_mx[n]
+            a, b = (0, G2 * P) if g is None else (P * g, P * g + P)
+            nc.vector.quantize_mx(out=q[:, a:b].bitcast(FP8X4), scales=s[:, a:b], in_=z_il[n][:, 4 * a : 4 * b])
 
         th_w = keep.tile([P, G2, 4, O], BF16, name="th_w")
         th_il = keep.tile([P, G2, O, 4], BF16, name="th_il", align_bytes=64)
@@ -315,14 +320,16 @@ def tile_chebyshev_filter_last_term_d7_kernel(tc, L_bytes, L_scale, t1, t0, thet
         for h in range(G2):
             for n in range(2):
                 mm1(n, h, (1,))
-        t1_copy(2, 0)
-        l_quant(2)
+        widen_on(4, True)
         widen_on(4, False)
         out_l(3)
-        mm1(2, 0, (0, 1))
-        t1_copy(2, 1)
-        t1_quant(2, 0)
         turn_l(4)
+        t1_copy(2, 0)
+        l_quant(2)
+        mm1(2, 0, (0, 1))
+        t1_copy(2, 1, (1,), nc.scalar.copy)
+        t1_copy(2, 1, (0,))
+        t1_quant(2, 0)
         t1_quant(2, 1)
         for n in range(3):
             mm1(n, 0, (2,))
@@ -357,6 +364,8 @@ def tile_chebyshev_filter_last_term_d7_kernel(tc, L_bytes, L_scale, t1, t0, thet
                 mm2(n)
             if s < NT:
                 z_step(s, 0)
+            if k in (4, 6):
+                th_quant(k // 2 - 2)
             for n in spread(s - 1, Z_FROM, Z_DOUBLE):
                 z_quant(n)
             if s < NT:
@@ -373,8 +382,6 @@ def tile_chebyshev_filter_last_term_d7_kernel(tc, L_bytes, L_scale, t1, t0, thet
                 turn_l(a)
                 widen_on(a + 1, True)
                 widen_on(a + 1, False)
-            if k in (4, 6):
-                th_quant(k // 2 - 2)
             if 2 <= k < 2 * G2 + 2:
                 th_scale(k // 2 - 1, (2 * (k % 2), 2 * (k % 2) + 1))
             for n in spread(s, Z_FROM, Z_DOUBLE):
@@ -385,36 +392,41 @@ def tile_chebyshev_filter_last_term_d7_kernel(tc, L_bytes, L_scale, t1, t0, thet
                 th_widen(k // 2, k % 2)
 
         last = NT - 1
-        mm2(last - 6)
-        mm2(last - 5)
-        mm1(last, 0)
-        mm1(last, 1)
-        z_quant(last - 4)
-        z_quant(last - 3)
-        relu_store(last - 8)
-        relu_store(last - 7)
-        add_acc(last - 6)
-        z_step(last, 0)
-        z_step(last, 1)
-        add_acc(last - 5)
         z_turn(last - 2)
         z_turn(last - 1)
+        mm2(last - 6)
+        mm2(last - 5)
         z_out(last - 2)
         z_out(last - 1)
-        z_turn(last)
+        relu_store(last - 8)
+        relu_store(last - 7)
+        z_quant(last - 4)
+        z_quant(last - 3)
+        mm1(last, 0)
+        mm1(last, 1)
+        add_acc(last - 6)
+        z_quant(last - 2)
+        add_acc(last - 5)
+        z_quant(last - 1)
+        z_step(last, 0)
+        z_step(last, 1)
         mm2(last - 4)
         mm2(last - 3)
-        z_out(last)
+        z_turn(last)
         relu_store(last - 6)
         relu_store(last - 5)
-        z_quant(last - 2)
-        z_quant(last - 1)
+        mm2(last - 2)
+        mm2(last - 1)
         add_acc(last - 4)
-        z_quant(last)
-        for n in range(last - 2, NT):
-            mm2(n)
+        add_acc(last - 3)
+        z_out(last, 0)
+        z_out(last, 1)
         relu_store(last - 4)
-        for n in range(last - 3, last):
+        z_quant(last, 0)
+        z_quant(last, 1)
+        relu_store(last - 3)
+        mm2(last)
+        for n in (last - 2, last - 1):
             add_acc(n)
             relu_store(n)
         for cols in (slice(0, O // 2), slice(O // 2, O)):

@@ -21,13 +21,7 @@ G1 = V // 512
 G2 = F // 512
 HEAD = 4
 VEC_FROM = 4
-Z_FROM = 6
-Z_DOUBLE = 7
-Y_FROM = 8
-Y_DOUBLE = 9
 VEC_G = 2
-L_AHEAD = 3
-TH_FROM = 1
 
 
 def tile_chebyshev_filter_last_term_d7_kernel(tc, L_bytes, L_scale, t1, t0, theta_bytes, theta_scale, acc, out):
@@ -82,8 +76,8 @@ def tile_chebyshev_filter_last_term_d7_kernel(tc, L_bytes, L_scale, t1, t0, thet
         warm = keep.tile([P, 2], F32, name="warm")
         nc.vector.memset(warm[:, 0:1], 0.0)
         nc.scalar.activation(out=warm[:, 1:2], in_=warm[:, 0:1], func=ACT.Copy)
-        load_l(0, 1)
         load_t1(0, 0, 512)
+        load_l(0, 1)
         load_l(1, 2)
         load_t1(0, 512, F)
         load_l(2, 3)
@@ -290,27 +284,28 @@ def tile_chebyshev_filter_last_term_d7_kernel(tc, L_bytes, L_scale, t1, t0, thet
             l_out(n, (0, 1))
             l_out(n, (2,))
 
-        widen_on(0, True)
-        widen_on(0, False)
-        turn_l(0)
         t1_copy(0, 0)
+        widen_on(0, False)
+        widen_on(0, True)
+        turn_l(0)
         widen_on(1, False)
+        t1_quant(0, 0)
         out_l(0)
         turn_l(1)
-        t1_quant(0, 0)
         t1_copy(0, 1)
         widen(2, 0)
         l_quant(0)
         out_l(1)
         t1_quant(0, 1)
-        l_quant(1)
-        for n in range(2):
-            for h in range(G2):
-                mm1(n, h, (0,))
+        for h in range(G2):
+            mm1(0, h, (0,))
         widen(2, 1)
         widen(2, 2)
         turn_l(2)
         t1_copy(1, 0)
+        l_quant(1)
+        for h in range(G2):
+            mm1(1, h, (0,))
         widen_on(3, False)
         t1_copy(1, 1)
         t1_quant(1, 0)
@@ -337,98 +332,146 @@ def tile_chebyshev_filter_last_term_d7_kernel(tc, L_bytes, L_scale, t1, t0, thet
             mm1(n, 1, (2,))
         widen_on(5, False)
         out_l(4)
-        th_widen(0, 0)
-        l_quant(3)
-        z_step(0, 0)
-        widen_on(5, True)
-        z_step(1, 0)
-        z_step(0, 1)
-        z_step(1, 1)
+        def both(step, n):
+            for h in range(G2):
+                step(n, h)
 
-        def spread(s, first, double):
-            if s < first:
-                return []
-            done = min(s, double) - first + 2 * max(0, s - double)
-            return [n for n in range(done, done + (2 if s >= double else 1)) if n < NT]
-
-        for s in range(2, NT - 1):
-            a = s + L_AHEAD
-            k = s - TH_FROM
-            if s < NT:
-                if (s, 0) not in p_ps:
-                    mm1(s, 0)
-                mm1(s, 1)
-            if s == 2:
-                turn_banks.append(sum_banks.pop(0))
-            for n in spread(s, Y_FROM, Y_DOUBLE):
-                mm2(n)
-            if s < NT:
-                z_step(s, 0)
-            if k in (4, 6):
-                th_quant(k // 2 - 2)
-            for n in spread(s - 1, Z_FROM, Z_DOUBLE):
-                z_quant(n)
-            if s < NT:
-                z_step(s, 1)
-            if a - 1 < NT:
-                l_quant(a - 1)
-            for n in spread(s - 1, Y_FROM, Y_DOUBLE):
-                relu_store(n)
-            for n in spread(s, Z_FROM, Z_DOUBLE):
-                z_turn(n)
-            for n in spread(s, Y_FROM, Y_DOUBLE):
-                add_acc(n)
-            if a < NT:
-                turn_l(a)
-                widen_on(a + 1, True)
-                widen_on(a + 1, False)
-            if 2 <= k < 2 * G2 + 2:
-                th_scale(k // 2 - 1, (2 * (k % 2), 2 * (k % 2) + 1))
-            for n in spread(s, Z_FROM, Z_DOUBLE):
-                z_out(n)
-            if a < NT:
-                out_l(a)
-            if 0 <= k < 2 * G2:
-                th_widen(k // 2, k % 2)
-
-        last = NT - 1
-        z_turn(last - 2)
-        z_turn(last - 1)
-        mm2(last - 6)
-        mm2(last - 5)
-        z_out(last - 2)
-        z_out(last - 1)
-        relu_store(last - 8)
-        relu_store(last - 7)
-        z_quant(last - 4)
-        z_quant(last - 3)
-        mm1(last, 0)
-        mm1(last, 1)
-        add_acc(last - 6)
-        z_quant(last - 2)
-        add_acc(last - 5)
-        z_quant(last - 1)
-        z_step(last, 0)
-        z_step(last, 1)
-        mm2(last - 4)
-        mm2(last - 3)
-        z_turn(last)
-        relu_store(last - 6)
-        relu_store(last - 5)
-        mm2(last - 2)
-        mm2(last - 1)
-        add_acc(last - 4)
-        add_acc(last - 3)
-        z_out(last, 0)
-        z_out(last, 1)
-        relu_store(last - 4)
-        z_quant(last, 0)
-        z_quant(last, 1)
-        relu_store(last - 3)
-        mm2(last)
-        for n in (last - 2, last - 1):
+        def finish(n):
             add_acc(n)
             relu_store(n)
+
+        z_step(0, 0)
+        mm1(2, 1)
+        turn_banks.append(sum_banks.pop(1))
+        widen_on(5, True)
+        widen_on(6, False)
+        l_quant(3)
+        widen_on(6, True)
+        z_step(1, 0)
+        turn_l(5)
+        turn_l(6)
+        th_widen(0, 0)
+        out_l(5)
+        out_l(6)
+        widen_on(7, False)
+        widen_on(8, False)
+        th_widen(0, 1)
+        z_step(0, 1)
+        z_step(1, 1)
+        z_step(2, 0)
+        l_quant(4)
+        z_step(2, 1)
+        both(mm1, 3)
+        both(mm1, 4)
+        widen_on(7, True)
+        z_step(3, 0)
+        widen_on(8, True)
+        z_step(3, 1)
+        l_quant(5)
+        turn_l(7)
+        turn_l(8)
+        out_l(7)
+        out_l(8)
+        widen_on(9, False)
+        th_widen(1, 0)
+        both(z_step, 4)
+        l_quant(6)
+        th_scale(0, range(4))
+        both(mm1, 5)
+        both(mm1, 6)
+        z_step(5, 0)
+        widen_on(9, True)
+        z_step(5, 1)
+        l_quant(7)
+        z_turn(0)
+        z_turn(1)
+        turn_l(9)
+        z_out(0)
+        z_out(1)
+        out_l(9)
+        widen_on(10, False)
+        th_widen(1, 1)
+        th_quant(0)
+        both(z_step, 6)
+        l_quant(8)
+        widen_on(10, True)
+        both(mm1, 7)
+        z_turn(2)
+        z_turn(3)
+        turn_l(10)
+        z_out(2)
+        z_out(3)
+        out_l(10)
+        widen_on(11, False)
+        z_step(7, 0)
+        l_quant(9)
+        z_step(7, 1)
+        z_quant(0)
+        z_quant(1)
+        th_scale(1, range(4))
+        both(mm1, 8)
+        both(mm1, 9)
+        z_step(8, 0)
+        th_quant(1)
+        z_step(8, 1)
+        mm2(0)
+        mm2(1)
+        widen_on(11, True)
+        l_quant(10)
+        both(z_step, 9)
+        z_turn(4)
+        z_turn(5)
+        turn_l(11)
+        z_quant(2)
+        z_quant(3)
+        z_out(4)
+        z_out(5)
+        out_l(11)
+        finish(0)
+        finish(1)
+        both(mm1, 10)
+        mm2(2)
+        mm2(3)
+        z_quant(4)
+        z_quant(5)
+        both(z_step, 10)
+        l_quant(11)
+        mm2(4)
+        mm2(5)
+        finish(2)
+        finish(3)
+        for n in range(6, 10):
+            z_turn(n)
+        add_acc(4)
+        add_acc(5)
+        for n in range(6, 10):
+            z_out(n)
+        both(mm1, 11)
+        z_quant(6)
+        z_quant(7)
+        mm2(6)
+        mm2(7)
+        relu_store(4)
+        relu_store(5)
+        both(z_step, 11)
+        z_quant(8)
+        z_quant(9)
+        z_turn(10)
+        z_turn(11)
+        add_acc(6)
+        add_acc(7)
+        z_out(10)
+        z_out(11)
+        relu_store(6)
+        relu_store(7)
+        mm2(8)
+        mm2(9)
+        z_quant(10)
+        z_quant(11)
+        mm2(10)
+        mm2(11)
+        for n in (8, 9, 10):
+            finish(n)
         for cols in (slice(0, O // 2), slice(O // 2, O)):
-            add_acc(last, cols)
-            relu_store(last, cols)
+            add_acc(11, cols)
+            relu_store(11, cols)

@@ -69,29 +69,29 @@ def tile_chebyshev_filter_last_term_d7_kernel(tc, L_bytes, L_scale, t1, t0, thet
         def load_t1(g, f0, f1):
             tl = keep.tile([P, 4, f1 - f0], BF16, name="t1_raw%d_%d" % (g, f0))
             nc.sync.dma_start(out=tl[:], in_=t1_src[g][:, :, f0:f1])
-            for f in range(f0, f1, 256):
-                t1_raw[g, f // 256] = tl[:, :, f - f0 : f - f0 + 256]
+            for f in range(f0, f1, 512):
+                t1_raw[g, f // 512] = tl[:, :, f - f0 : f - f0 + 512]
 
         nc.scalar.dma_start(out=l_sc[:], in_=L_scale.rearrange("a b -> (a b)").partition_broadcast(P))
         warm = keep.tile([P, 2], F32, name="warm")
         nc.vector.memset(warm[:, 0:1], 0.0)
         nc.scalar.activation(out=warm[:, 1:2], in_=warm[:, 0:1], func=ACT.Copy)
-        load_t1(0, 0, 512)
         load_l(0, 1)
         load_l(1, 2)
+        load_t1(0, 0, 512)
         load_t1(0, 512, F)
-        load_l(2, 3)
+        load_l(2, 4)
         load_t1(1, 0, F)
-        load_l(3, 4)
+        load_l(4, 5)
         load_t1(2, 0, F)
-        load_l(4, 6)
+        load_l(5, 7)
         load_t0(0, 2)
         load_t0(2, 4)
         rows = theta_scale.rearrange("(g q) o -> q g o", q=4)
         nc.sync.dma_start(out=th_by[:], in_=theta_bytes.rearrange("(g p t) o -> p g t o", p=P, t=4))
         for q in range(4):
             nc.sync.dma_start(out=th_sc[32 * q : 32 * q + 32], in_=rows[q].partition_broadcast(32))
-        load_l(6, 9)
+        load_l(7, 9)
         load_t0(4, 6)
         load_l(9, 12)
         load_t0(6, 9)
@@ -102,14 +102,12 @@ def tile_chebyshev_filter_last_term_d7_kernel(tc, L_bytes, L_scale, t1, t0, thet
 
         t1_il, t1_mx = {}, {}
 
-        def t1_copy(g, h, parts=(0, 1), copy=nc.vector.tensor_copy):
-            if (g, h) not in t1_il:
-                t1_il[g, h] = work.tile([P, 512, 4], BF16, name="t1_il", bufs=4, align_bytes=64)
-            for i in parts:
-                copy(
-                    out=t1_il[g, h][:, 256 * i : 256 * (i + 1), :].rearrange("p (c i) t -> p c t i", i=4),
-                    in_=t1_raw[g, 2 * h + i].rearrange("p t (c i) -> p c t i", i=4),
-                )
+        def t1_copy(g, h, copy=nc.vector.tensor_copy):
+            t1_il[g, h] = work.tile([P, 512, 4], BF16, name="t1_il", bufs=4, align_bytes=64)
+            copy(
+                out=t1_il[g, h][:].rearrange("p (c i) t -> p c t i", i=4),
+                in_=t1_raw[g, h].rearrange("p t (c i) -> p c t i", i=4),
+            )
 
         def t1_quant(g, h):
             q = keep.tile([P, 512], U32, name="t1_q%d_%d" % (g, h), align_bytes=64)
@@ -120,7 +118,7 @@ def tile_chebyshev_filter_last_term_d7_kernel(tc, L_bytes, L_scale, t1, t0, thet
         l_w, l_ps, l_il, l_mx = {}, {}, {}, {}
 
         def on_vector(n, g):
-            return (n == 0 and g > 0) or (n >= VEC_FROM and g >= VEC_G)
+            return (n == 0 and g > 0) or (n == 1 and g == 2) or (n >= VEC_FROM and g >= VEC_G)
 
         def widen(n, g):
             wide = work.tile([P, 512], BF16, name="l_w%d" % g, bufs=3)
@@ -140,21 +138,22 @@ def tile_chebyshev_filter_last_term_d7_kernel(tc, L_bytes, L_scale, t1, t0, thet
                     nc.scalar.activation(out=wide[:, P * q : P * q + P], in_=src[:, P * b : P * b + P], func=ACT.Copy, scale=sc)
             l_w[n, g] = wide
 
-        def l_turn(n, gs):
+        def l_turn(*items):
             ps = next_bank(turn_banks, [P, 2, 2, P])
-            for a, g in enumerate(gs):
+            for a, (n, g) in enumerate(items):
                 words = l_w[n, g][:].bitcast(F32)
                 for u in range(2):
                     part = words[:, P * u : P * u + P] if on_vector(n, g) else words[:, u:256:2]
                     nc.tensor.transpose(ps[:, a, u, :], part, ident[:])
-            l_ps[n, gs] = ps
+                l_ps[n, g] = (ps, a)
 
-        def l_out(n, gs):
+        def l_out(n, g0, g1):
             if n not in l_il:
                 l_il[n] = work.tile([P, V], BF16, name="l_il", bufs=3, align_bytes=64)
+            ps, a = l_ps[n, g0]
             nc.scalar.copy(
-                out=l_il[n][:].bitcast(F32).rearrange("p (g i u) -> p g i u", g=G1, u=2)[:, gs[0] : gs[-1] + 1],
-                in_=l_ps[n, gs][:, : len(gs)].rearrange("p a u i -> p a i u"),
+                out=l_il[n][:].bitcast(F32).rearrange("p (g i u) -> p g i u", g=G1, u=2)[:, g0:g1],
+                in_=ps[:, a : a + g1 - g0].rearrange("p a u i -> p a i u"),
             )
 
         def l_quant(n):
@@ -277,61 +276,61 @@ def tile_chebyshev_filter_last_term_d7_kernel(tc, L_bytes, L_scale, t1, t0, thet
                         widen(n, g)
 
         def turn_l(n):
-            l_turn(n, (0, 1))
-            l_turn(n, (2,))
+            l_turn((n, 0), (n, 1))
+            l_turn((n, 2))
 
         def out_l(n):
-            l_out(n, (0, 1))
-            l_out(n, (2,))
+            l_out(n, 0, 2)
+            l_out(n, 2, 3)
 
-        t1_copy(0, 0)
         widen_on(0, False)
         widen_on(0, True)
         turn_l(0)
+        widen_on(1, True)
         widen_on(1, False)
-        t1_quant(0, 0)
+        t1_copy(0, 0)
         out_l(0)
         turn_l(1)
-        t1_copy(0, 1)
-        widen(2, 0)
-        l_quant(0)
         out_l(1)
-        t1_quant(0, 1)
-        for h in range(G2):
-            mm1(0, h, (0,))
-        widen(2, 1)
-        widen(2, 2)
-        turn_l(2)
-        t1_copy(1, 0)
+        l_quant(0)
+        t1_quant(0, 0)
+        t1_copy(0, 1)
+        widen_on(2, False)
         l_quant(1)
-        for h in range(G2):
-            mm1(1, h, (0,))
+        t1_quant(0, 1)
+        for n in range(2):
+            mm1(n, 0, (0,))
+        turn_l(2)
+        for n in range(2):
+            mm1(n, 1, (0,))
         widen_on(3, False)
-        t1_copy(1, 1)
-        t1_quant(1, 0)
+        t1_copy(1, 0)
+        widen(4, 0)
         out_l(2)
         turn_l(3)
+        t1_copy(1, 1)
+        t1_quant(1, 0)
         t1_quant(1, 1)
+        l_quant(2)
         for h in range(G2):
             for n in range(2):
                 mm1(n, h, (1,))
-        widen_on(4, True)
-        widen_on(4, False)
-        out_l(3)
-        turn_l(4)
-        t1_copy(2, 0)
-        l_quant(2)
         mm1(2, 0, (0, 1))
-        t1_copy(2, 1, (1,), nc.scalar.copy)
-        t1_copy(2, 1, (0,))
+        widen(4, 1)
+        l_turn((4, 0), (4, 1))
+        t1_copy(2, 1, nc.scalar.copy)
+        t1_copy(2, 0)
+        widen(4, 2)
         t1_quant(2, 0)
         t1_quant(2, 1)
+        out_l(3)
         for n in range(3):
             mm1(n, 0, (2,))
         for n in range(2):
             mm1(n, 1, (2,))
         widen_on(5, False)
-        out_l(4)
+        l_out(4, 0, 2)
+
         def both(step, n):
             for h in range(G2):
                 step(n, h)
@@ -342,19 +341,23 @@ def tile_chebyshev_filter_last_term_d7_kernel(tc, L_bytes, L_scale, t1, t0, thet
 
         z_step(0, 0)
         mm1(2, 1)
-        turn_banks.append(sum_banks.pop(1))
+        turn_banks.append(sum_banks.pop(0))
         widen_on(5, True)
         widen_on(6, False)
         l_quant(3)
         widen_on(6, True)
         z_step(1, 0)
-        turn_l(5)
+        l_turn((4, 2), (5, 2))
+        l_turn((5, 0), (5, 1))
         turn_l(6)
-        th_widen(0, 0)
-        out_l(5)
+        widen(7, 0)
+        l_out(4, 2, 3)
+        l_out(5, 2, 3)
+        l_out(5, 0, 2)
         out_l(6)
-        widen_on(7, False)
+        widen(7, 1)
         widen_on(8, False)
+        th_widen(0, 0)
         th_widen(0, 1)
         z_step(0, 1)
         z_step(1, 1)
@@ -373,7 +376,7 @@ def tile_chebyshev_filter_last_term_d7_kernel(tc, L_bytes, L_scale, t1, t0, thet
         out_l(7)
         out_l(8)
         widen_on(9, False)
-        th_widen(1, 0)
+        widen(10, 0)
         both(z_step, 4)
         l_quant(6)
         th_scale(0, range(4))
@@ -389,7 +392,8 @@ def tile_chebyshev_filter_last_term_d7_kernel(tc, L_bytes, L_scale, t1, t0, thet
         z_out(0)
         z_out(1)
         out_l(9)
-        widen_on(10, False)
+        widen(10, 1)
+        th_widen(1, 0)
         th_widen(1, 1)
         th_quant(0)
         both(z_step, 6)

@@ -102,11 +102,12 @@ def tile_chebyshev_filter_last_term_d7_kernel(tc, L_bytes, L_scale, t1, t0, thet
 
         t1_il, t1_mx = {}, {}
 
-        def t1_copy(g, h, copy=nc.vector.tensor_copy):
-            t1_il[g, h] = work.tile([P, 512, 4], BF16, name="t1_il", bufs=4, align_bytes=64)
+        def t1_copy(g, h, copy=nc.vector.tensor_copy, f0=0, f1=512):
+            if (g, h) not in t1_il:
+                t1_il[g, h] = work.tile([P, 512, 4], BF16, name="t1_il", bufs=4, align_bytes=64)
             copy(
-                out=t1_il[g, h][:].rearrange("p (c i) t -> p c t i", i=4),
-                in_=t1_raw[g, h].rearrange("p t (c i) -> p c t i", i=4),
+                out=t1_il[g, h][:, f0:f1, :].rearrange("p (c i) t -> p c t i", i=4),
+                in_=t1_raw[g, h][:, :, f0:f1].rearrange("p t (c i) -> p c t i", i=4),
             )
 
         def t1_quant(g, h):
@@ -118,43 +119,59 @@ def tile_chebyshev_filter_last_term_d7_kernel(tc, L_bytes, L_scale, t1, t0, thet
         l_w, l_ps, l_il, l_mx = {}, {}, {}, {}
 
         def on_vector(n, g):
-            return (n == 0 and g > 0) or (n == 1 and g == 2) or (n >= VEC_FROM and g >= VEC_G)
+            return g == G1 - 1 and n not in (2, 3)
+
+        k_sc = keep.tile([P, NT, G1], F32, name="k_sc")
+
+        def regroup_scales():
+            for q in range(4):
+                rows32 = slice(32 * q, 32 * q + 32)
+                nc.vector.tensor_copy(out=k_sc[rows32], in_=l_sc[rows32].rearrange("p (n g q) -> p n g q", g=G1, q=4)[:, :, :, q])
 
         def widen(n, g):
-            wide = work.tile([P, 512], BF16, name="l_w%d" % g, bufs=3)
+            wide = work.tile([P, 512], BF16, name="l_wv", bufs=3)
             src = l_by[n].bitcast(FP8)
             for q in range(4):
                 b = 4 * g + q
-                sc = l_sc[:, NT * n + b : NT * n + b + 1]
-                if on_vector(n, g):
-                    nc.vector.tensor_scalar(
-                        out=wide[:].rearrange("p (u m e) -> p m u e", u=2, e=2)[:, 32 * q : 32 * q + 32],
-                        in0=src[:, P * b : P * b + P].rearrange("p (m u e) -> p m u e", u=2, e=2),
-                        scalar1=sc,
-                        scalar2=None,
-                        op0=ALU.mult,
-                    )
-                else:
-                    nc.scalar.activation(out=wide[:, P * q : P * q + P], in_=src[:, P * b : P * b + P], func=ACT.Copy, scale=sc)
-            l_w[n, g] = wide
+                nc.vector.tensor_scalar(
+                    out=wide[:].rearrange("p (u m e) -> p m u e", u=2, e=2)[:, 32 * q : 32 * q + 32],
+                    in0=src[:, P * b : P * b + P].rearrange("p (m u e) -> p m u e", u=2, e=2),
+                    scalar1=l_sc[:, NT * n + b : NT * n + b + 1],
+                    scalar2=None,
+                    op0=ALU.mult,
+                )
+            l_w[n, g] = wide[:]
+
+        def cast(n):
+            gs = [g for g in range(G1) if not on_vector(n, g)]
+            wide = work.tile([P, 512 * len(gs)], BF16, name="l_ws", bufs=3)
+            nc.scalar.copy(out=wide[:], in_=l_by[n].bitcast(FP8)[:, : 512 * len(gs)])
+            for g in gs:
+                l_w[n, g] = wide[:, 512 * g : 512 * g + 512]
 
         def l_turn(*items):
             ps = next_bank(turn_banks, [P, 2, 2, P])
             for a, (n, g) in enumerate(items):
-                words = l_w[n, g][:].bitcast(F32)
+                words = l_w[n, g].bitcast(F32)
                 for u in range(2):
                     part = words[:, P * u : P * u + P] if on_vector(n, g) else words[:, u:256:2]
                     nc.tensor.transpose(ps[:, a, u, :], part, ident[:])
-                l_ps[n, g] = (ps, a)
+                l_ps[n, g] = ps[:, a]
 
-        def l_out(n, g0, g1):
+        def l_out(n, g0, g1, vector=False):
             if n not in l_il:
                 l_il[n] = work.tile([P, V], BF16, name="l_il", bufs=3, align_bytes=64)
-            ps, a = l_ps[n, g0]
-            nc.scalar.copy(
-                out=l_il[n][:].bitcast(F32).rearrange("p (g i u) -> p g i u", g=G1, u=2)[:, g0:g1],
-                in_=ps[:, a : a + g1 - g0].rearrange("p a u i -> p a i u"),
-            )
+            for g in range(g0, g1):
+                dst = l_il[n][:, 512 * g : 512 * g + 512]
+                if on_vector(n, g):
+                    nc.scalar.copy(out=dst.bitcast(F32).rearrange("p (i u) -> p i u", u=2), in_=l_ps[n, g].rearrange("p u i -> p i u"))
+                    continue
+                dst = dst.rearrange("p (i u e) -> p i u e", u=2, e=2)
+                src = l_ps[n, g].bitcast(BF16).rearrange("p u (i e) -> p i u e", e=2)
+                if vector:
+                    nc.vector.tensor_scalar(out=dst, in0=src, scalar1=k_sc[:, n, g : g + 1], scalar2=None, op0=ALU.mult)
+                else:
+                    nc.scalar.activation(out=dst, in_=src, func=ACT.Copy, scale=k_sc[:, n, g : g + 1])
 
         def l_quant(n):
             q = work.tile([P, G1 * P], U32, name="l_q", bufs=HEAD + 2, align_bytes=64)
@@ -269,12 +286,6 @@ def tile_chebyshev_filter_last_term_d7_kernel(tc, L_bytes, L_scale, t1, t0, thet
             nc.scalar.activation(out=r[:], in_=sums[n, cols.start][:], func=ACT.Relu)
             nc.sync.dma_start(out=out[P * n : P * n + P, cols], in_=r[:])
 
-        def widen_on(n, vector):
-            if n < NT:
-                for g in range(G1):
-                    if on_vector(n, g) == vector:
-                        widen(n, g)
-
         def turn_l(n):
             l_turn((n, 0), (n, 1))
             l_turn((n, 2))
@@ -283,52 +294,57 @@ def tile_chebyshev_filter_last_term_d7_kernel(tc, L_bytes, L_scale, t1, t0, thet
             l_out(n, 0, 2)
             l_out(n, 2, 3)
 
-        widen_on(0, False)
-        widen_on(0, True)
+        regroup_scales()
+        cast(0)
+        widen(0, 2)
         turn_l(0)
-        widen_on(1, True)
-        widen_on(1, False)
+        cast(1)
+        widen(1, 2)
         t1_copy(0, 0)
         out_l(0)
         turn_l(1)
         out_l(1)
-        l_quant(0)
+        cast(2)
         t1_quant(0, 0)
+        l_quant(0)
         t1_copy(0, 1)
-        widen_on(2, False)
+        mm1(0, 0, (0,))
+        turn_l(2)
+        cast(3)
         l_quant(1)
         t1_quant(0, 1)
-        for n in range(2):
-            mm1(n, 0, (0,))
-        turn_l(2)
+        mm1(1, 0, (0,))
         for n in range(2):
             mm1(n, 1, (0,))
-        widen_on(3, False)
+        t1_copy(1, 1, nc.scalar.copy)
         t1_copy(1, 0)
-        widen(4, 0)
-        out_l(2)
-        turn_l(3)
-        t1_copy(1, 1)
+        l_turn((3, 0), (3, 1))
+        l_out(2, 0, 2)
+        l_out(2, 2, 3, vector=True)
         t1_quant(1, 0)
+        widen(4, 2)
         t1_quant(1, 1)
-        l_quant(2)
+        cast(4)
+        t1_copy(2, 1, nc.scalar.copy, 256, 512)
+        t1_copy(2, 0)
         for h in range(G2):
             for n in range(2):
                 mm1(n, h, (1,))
-        mm1(2, 0, (0, 1))
-        widen(4, 1)
+        l_turn((3, 2))
+        l_quant(2)
+        l_out(3, 0, 2)
         l_turn((4, 0), (4, 1))
-        t1_copy(2, 1, nc.scalar.copy)
-        t1_copy(2, 0)
-        widen(4, 2)
+        mm1(2, 0, (0, 1))
+        t1_copy(2, 1, nc.vector.tensor_copy, 0, 256)
         t1_quant(2, 0)
         t1_quant(2, 1)
-        out_l(3)
+        l_out(3, 2, 3)
         for n in range(3):
             mm1(n, 0, (2,))
         for n in range(2):
             mm1(n, 1, (2,))
-        widen_on(5, False)
+        cast(5)
+        cast(6)
         l_out(4, 0, 2)
 
         def both(step, n):
@@ -342,21 +358,19 @@ def tile_chebyshev_filter_last_term_d7_kernel(tc, L_bytes, L_scale, t1, t0, thet
         z_step(0, 0)
         mm1(2, 1)
         turn_banks.append(sum_banks.pop(0))
-        widen_on(5, True)
-        widen_on(6, False)
+        widen(5, 2)
         l_quant(3)
-        widen_on(6, True)
+        widen(6, 2)
         z_step(1, 0)
         l_turn((4, 2), (5, 2))
         l_turn((5, 0), (5, 1))
         turn_l(6)
-        widen(7, 0)
+        cast(7)
         l_out(4, 2, 3)
         l_out(5, 2, 3)
         l_out(5, 0, 2)
         out_l(6)
-        widen(7, 1)
-        widen_on(8, False)
+        cast(8)
         th_widen(0, 0)
         th_widen(0, 1)
         z_step(0, 1)
@@ -366,24 +380,24 @@ def tile_chebyshev_filter_last_term_d7_kernel(tc, L_bytes, L_scale, t1, t0, thet
         z_step(2, 1)
         both(mm1, 3)
         both(mm1, 4)
-        widen_on(7, True)
+        widen(7, 2)
         z_step(3, 0)
-        widen_on(8, True)
+        widen(8, 2)
         z_step(3, 1)
         l_quant(5)
         turn_l(7)
         turn_l(8)
         out_l(7)
         out_l(8)
-        widen_on(9, False)
-        widen(10, 0)
+        cast(9)
+        cast(10)
         both(z_step, 4)
         l_quant(6)
         th_scale(0, range(4))
         both(mm1, 5)
         both(mm1, 6)
         z_step(5, 0)
-        widen_on(9, True)
+        widen(9, 2)
         z_step(5, 1)
         l_quant(7)
         z_turn(0)
@@ -392,13 +406,12 @@ def tile_chebyshev_filter_last_term_d7_kernel(tc, L_bytes, L_scale, t1, t0, thet
         z_out(0)
         z_out(1)
         out_l(9)
-        widen(10, 1)
         th_widen(1, 0)
         th_widen(1, 1)
         th_quant(0)
         both(z_step, 6)
         l_quant(8)
-        widen_on(10, True)
+        widen(10, 2)
         both(mm1, 7)
         z_turn(2)
         z_turn(3)
@@ -406,7 +419,7 @@ def tile_chebyshev_filter_last_term_d7_kernel(tc, L_bytes, L_scale, t1, t0, thet
         z_out(2)
         z_out(3)
         out_l(10)
-        widen_on(11, False)
+        cast(11)
         z_step(7, 0)
         l_quant(9)
         z_step(7, 1)
@@ -420,7 +433,7 @@ def tile_chebyshev_filter_last_term_d7_kernel(tc, L_bytes, L_scale, t1, t0, thet
         z_step(8, 1)
         mm2(0)
         mm2(1)
-        widen_on(11, True)
+        widen(11, 2)
         l_quant(10)
         both(z_step, 9)
         z_turn(4)

@@ -21,7 +21,7 @@ G1 = V // 512
 G2 = F // 512
 HEAD = 4
 VEC_FROM = 4
-VEC_G = 2
+VEC_TWO = 9
 
 
 def tile_chebyshev_filter_last_term_d7_kernel(tc, L_bytes, L_scale, t1, t0, theta_bytes, theta_scale, acc, out):
@@ -119,7 +119,7 @@ def tile_chebyshev_filter_last_term_d7_kernel(tc, L_bytes, L_scale, t1, t0, thet
         l_w, l_ps, l_il, l_mx = {}, {}, {}, {}
 
         def on_vector(n, g):
-            return g == G1 - 1 and n not in (2, 3)
+            return (g == G1 - 1 and n not in (2, 3)) or (g == 1 and n >= VEC_TWO)
 
         k_sc = keep.tile([P, NT, G1], F32, name="k_sc")
 
@@ -129,7 +129,7 @@ def tile_chebyshev_filter_last_term_d7_kernel(tc, L_bytes, L_scale, t1, t0, thet
                 nc.vector.tensor_copy(out=k_sc[rows32], in_=l_sc[rows32].rearrange("p (n g q) -> p n g q", g=G1, q=4)[:, :, :, q])
 
         def widen(n, g):
-            wide = work.tile([P, 512], BF16, name="l_wv", bufs=3)
+            wide = work.tile([P, 512], BF16, name="l_wv", bufs=4)
             src = l_by[n].bitcast(FP8)
             for q in range(4):
                 b = 4 * g + q
@@ -243,19 +243,17 @@ def tile_chebyshev_filter_last_term_d7_kernel(tc, L_bytes, L_scale, t1, t0, thet
         th_q = keep.tile([P, G2, O], U32, name="th_q", align_bytes=64)
         th_s = keep.tile([P, G2, O], U8, name="th_s", align_bytes=64)
 
-        def th_widen(g, u):
-            ts = slice(2 * u, 2 * u + 2)
-            nc.scalar.copy(out=th_w[:, g, ts].rearrange("p t o -> p (t o)"), in_=th_by[:, g, ts].rearrange("p t o -> p (t o)").bitcast(FP8))
+        def th_widen(g):
+            nc.scalar.copy(out=th_w[:, g].rearrange("p t o -> p (t o)"), in_=th_by[:, g].rearrange("p t o -> p (t o)").bitcast(FP8))
 
-        def th_scale(g, bs):
+        def th_scale(g, vector, bs=range(4)):
             for b in bs:
-                nc.vector.tensor_scalar(
-                    out=th_il[:, g, P * b : P * b + P, :].rearrange("p (c i) t -> p c t i", i=4),
-                    in0=th_w[:, g, :, P * b : P * b + P].rearrange("p t (c i) -> p c t i", i=4),
-                    scalar1=th_sc[:, g, b : b + 1],
-                    scalar2=None,
-                    op0=ALU.mult,
-                )
+                dst = th_il[:, g, P * b : P * b + P, :].rearrange("p (c i) t -> p c t i", i=4)
+                src = th_w[:, g, :, P * b : P * b + P].rearrange("p t (c i) -> p c t i", i=4)
+                if vector:
+                    nc.vector.tensor_scalar(out=dst, in0=src, scalar1=th_sc[:, g, b : b + 1], scalar2=None, op0=ALU.mult)
+                else:
+                    nc.scalar.activation(out=dst, in_=src, func=ACT.Copy, scale=th_sc[:, g, b : b + 1])
 
         def th_quant(g):
             nc.vector.quantize_mx(out=th_q[:, g].bitcast(FP8X4), scales=th_s[:, g], in_=th_il[:, g].rearrange("p o t -> p (o t)"))
@@ -371,8 +369,7 @@ def tile_chebyshev_filter_last_term_d7_kernel(tc, L_bytes, L_scale, t1, t0, thet
         l_out(5, 0, 2)
         out_l(6)
         cast(8)
-        th_widen(0, 0)
-        th_widen(0, 1)
+        th_widen(0)
         z_step(0, 1)
         z_step(1, 1)
         z_step(2, 0)
@@ -387,80 +384,81 @@ def tile_chebyshev_filter_last_term_d7_kernel(tc, L_bytes, L_scale, t1, t0, thet
         l_quant(5)
         turn_l(7)
         turn_l(8)
+        cast(9)
         out_l(7)
         out_l(8)
-        cast(9)
         cast(10)
+        th_scale(0, False, (0, 1))
         both(z_step, 4)
         l_quant(6)
-        th_scale(0, range(4))
+        widen(9, 1)
+        widen(9, 2)
         both(mm1, 5)
         both(mm1, 6)
         z_step(5, 0)
-        widen(9, 2)
-        z_step(5, 1)
         l_quant(7)
+        z_step(5, 1)
         z_turn(0)
         z_turn(1)
         turn_l(9)
         z_out(0)
         z_out(1)
         out_l(9)
-        th_widen(1, 0)
-        th_widen(1, 1)
-        th_quant(0)
+        th_widen(1)
+        widen(10, 1)
+        widen(10, 2)
         both(z_step, 6)
         l_quant(8)
-        widen(10, 2)
+        th_scale(0, True, (2, 3))
         both(mm1, 7)
         z_turn(2)
         z_turn(3)
         turn_l(10)
+        cast(11)
         z_out(2)
         z_out(3)
         out_l(10)
-        cast(11)
+        th_scale(1, False)
         z_step(7, 0)
         l_quant(9)
         z_step(7, 1)
-        z_quant(0)
-        z_quant(1)
-        th_scale(1, range(4))
+        widen(11, 1)
+        widen(11, 2)
+        th_quant(0)
         both(mm1, 8)
         both(mm1, 9)
-        z_step(8, 0)
-        th_quant(1)
-        z_step(8, 1)
-        mm2(0)
-        mm2(1)
-        widen(11, 2)
-        l_quant(10)
-        both(z_step, 9)
         z_turn(4)
         z_turn(5)
         turn_l(11)
-        z_quant(2)
-        z_quant(3)
+        both(z_step, 8)
+        z_quant(0)
+        z_quant(1)
+        l_quant(10)
+        both(z_step, 9)
+        th_quant(1)
         z_out(4)
         z_out(5)
         out_l(11)
-        finish(0)
-        finish(1)
         both(mm1, 10)
+        mm2(0)
+        mm2(1)
+        z_quant(2)
+        z_quant(3)
+        both(z_step, 10)
         mm2(2)
         mm2(3)
         z_quant(4)
+        finish(0)
         z_quant(5)
-        both(z_step, 10)
-        l_quant(11)
+        finish(1)
         mm2(4)
         mm2(5)
+        l_quant(11)
         finish(2)
-        finish(3)
         for n in range(6, 10):
             z_turn(n)
-        add_acc(4)
-        add_acc(5)
+        for n in range(3, 6):
+            add_acc(n)
         for n in range(6, 10):
             z_out(n)
         both(mm1, 11)
@@ -468,6 +466,7 @@ def tile_chebyshev_filter_last_term_d7_kernel(tc, L_bytes, L_scale, t1, t0, thet
         z_quant(7)
         mm2(6)
         mm2(7)
+        relu_store(3)
         relu_store(4)
         relu_store(5)
         both(z_step, 11)

@@ -106,8 +106,8 @@ def tile_chebyshev_filter_last_term_d7_kernel(tc, L_bytes, L_scale, t1, t0, thet
             if (g, h) not in t1_il:
                 t1_il[g, h] = work.tile([P, 512, 4], BF16, name="t1_il", bufs=4, align_bytes=64)
             copy(
-                out=t1_il[g, h][:, f0:f1, :].rearrange("p (c i) t -> p c t i", i=4),
-                in_=t1_raw[g, h][:, :, f0:f1].rearrange("p t (c i) -> p c t i", i=4),
+                out=t1_il[g, h][:].rearrange("p (u c m) t -> p c t m u", u=2, m=2)[:, f0 // 4 : f1 // 4],
+                in_=t1_raw[g, h][:, :, f0:f1].rearrange("p t (c m u) -> p c t m u", m=2, u=2),
             )
 
         def t1_quant(g, h):
@@ -201,17 +201,14 @@ def tile_chebyshev_filter_last_term_d7_kernel(tc, L_bytes, L_scale, t1, t0, thet
 
         def z_step(n, h):
             z = work.tile([P, 2, 256], BF16, name="z_sb%d" % h, bufs=9)
-            pv = p_ps[n, h][:].rearrange("p (m u e) -> p u m e", u=2, e=2)
-            tv = t0_sb[n][:, 512 * h : 512 * h + 512].rearrange("p (m u e) -> p u m e", u=2, e=2)
-            for u in range(2):
-                nc.vector.scalar_tensor_tensor(
-                    out=z[:, u, :].rearrange("p (m e) -> p m e", e=2),
-                    in0=pv[:, u],
-                    scalar=2.0,
-                    in1=tv[:, u],
-                    op0=ALU.mult,
-                    op1=ALU.subtract,
-                )
+            nc.vector.scalar_tensor_tensor(
+                out=z[:],
+                in0=p_ps[n, h][:].rearrange("p (u b) -> p u b", u=2),
+                scalar=2.0,
+                in1=t0_sb[n][:, 512 * h : 512 * h + 512].rearrange("p (b u) -> p u b", u=2),
+                op0=ALU.mult,
+                op1=ALU.subtract,
+            )
             z_sb[n, h] = z
 
         def z_turn(n):
@@ -244,7 +241,9 @@ def tile_chebyshev_filter_last_term_d7_kernel(tc, L_bytes, L_scale, t1, t0, thet
         th_s = keep.tile([P, G2, O], U8, name="th_s", align_bytes=64)
 
         def th_widen(g):
-            nc.scalar.copy(out=th_w[:, g].rearrange("p t o -> p (t o)"), in_=th_by[:, g].rearrange("p t o -> p (t o)").bitcast(FP8))
+            for u in range(2):
+                for e in range(2):
+                    nc.scalar.copy(out=th_w[:, g, 2 * u + e, :], in_=th_by[:, g, 2 * e + u, :].bitcast(FP8))
 
         def th_scale(g, vector, bs=range(4)):
             for b in bs:

@@ -15,13 +15,11 @@ FP8X4 = mybir.dt.float8_e4m3fn_x4
 ACT = mybir.ActivationFunctionType
 ALU = mybir.AluOpType
 
+F32_MAX = (2.0 - 2.0**-23) * 2.0**127
 P = 128
 NT = V // P
 G1 = V // 512
 G2 = F // 512
-HEAD = 4
-VEC_FROM = 4
-VEC_TWO = 9
 
 
 def tile_chebyshev_filter_last_term_d7_kernel(tc, L_bytes, L_scale, t1, t0, theta_bytes, theta_scale, acc, out):
@@ -35,12 +33,24 @@ def tile_chebyshev_filter_last_term_d7_kernel(tc, L_bytes, L_scale, t1, t0, thet
         ident = keep.tile([P, P], F32, name="ident")
         make_identity(nc, ident[:])
 
-        sum_banks, turn_banks = [0, 1, 2, 3, 4], [5, 6, 7]
+        free_banks, held = list(range(8)), {}
 
-        def next_bank(ring, shape):
-            b = ring.pop(0)
-            ring.append(b)
+        def take_bank(shape, *readers):
+            b = free_banks.pop(0)
+            for r in readers:
+                held[r] = b
             return psum.tile(shape, F32, name="bank%d" % b)
+
+        def emptied(reader):
+            b = held.pop(reader)
+            if b not in held.values():
+                free_banks.append(b)
+
+        def warm_up(count):
+            ps = take_bank([P, P], "warm")
+            for k in range(count):
+                nc.tensor.matmul(out=ps[:], lhsT=ident[:], rhs=ident[:], start=True, stop=True)
+            emptied("warm")
 
         l_sc = keep.tile([P, NT * NT], F32, name="l_sc")
         th_sc = keep.tile([P, G2, 4], F32, name="th_sc")
@@ -48,6 +58,7 @@ def tile_chebyshev_filter_last_term_d7_kernel(tc, L_bytes, L_scale, t1, t0, thet
         t1_src = t1.rearrange("(g p t) f -> g p t f", p=P, t=4)
         t0_rows = t0.rearrange("(n p) f -> p n f", p=P)
         acc_rows = acc.rearrange("(n p) o -> p n o", p=P)
+        th_src = theta_bytes.rearrange("(g p t) o -> g p t o", p=P, t=4)
         th_by = keep.tile([P, G2, 4, O], U8, name="th_by")
         l_by, t1_raw, t0_sb, acc_sb = {}, {}, {}, {}
 
@@ -60,51 +71,40 @@ def tile_chebyshev_filter_last_term_d7_kernel(tc, L_bytes, L_scale, t1, t0, thet
         def load_l(n0, n1):
             load_rows(l_by, l_rows, U8, "l_by", n0, n1)
 
-        def load_t0(n0, n1):
-            load_rows(t0_sb, t0_rows, BF16, "t0_sb", n0, n1)
-
         def load_acc(n0, n1):
             load_rows(acc_sb, acc_rows, BF16, "acc_sb", n0, n1)
 
-        def load_t1(g, f0, f1):
-            tl = keep.tile([P, 4, f1 - f0], BF16, name="t1_raw%d_%d" % (g, f0))
-            nc.sync.dma_start(out=tl[:], in_=t1_src[g][:, :, f0:f1])
-            for f in range(f0, f1, 512):
-                t1_raw[g, f // 512] = tl[:, :, f - f0 : f - f0 + 512]
+        def load_t0(n0, n1, h0=0, h1=G2):
+            tl = keep.tile([P, n1 - n0, 512 * (h1 - h0)], BF16, name="t0_sb%d_%d" % (n0, h0))
+            nc.sync.dma_start(out=tl[:], in_=t0_rows[:, n0:n1, 512 * h0 : 512 * h1])
+            for n in range(n0, n1):
+                for h in range(h0, h1):
+                    t0_sb[n, h] = tl[:, n - n0, 512 * (h - h0) : 512 * (h - h0) + 512]
 
-        nc.scalar.dma_start(out=l_sc[:], in_=L_scale.rearrange("a b -> (a b)").partition_broadcast(P))
-        warm = keep.tile([P, 2], F32, name="warm")
-        nc.vector.memset(warm[:, 0:1], 0.0)
-        nc.scalar.activation(out=warm[:, 1:2], in_=warm[:, 0:1], func=ACT.Copy)
-        load_l(0, 1)
-        load_l(1, 2)
-        load_t1(0, 0, 512)
-        load_t1(0, 512, F)
-        load_l(2, 4)
-        load_t1(1, 0, F)
-        load_l(4, 5)
-        load_t1(2, 0, F)
-        load_l(5, 7)
-        load_t0(0, 2)
-        load_t0(2, 4)
-        rows = theta_scale.rearrange("(g q) o -> q g o", q=4)
-        nc.sync.dma_start(out=th_by[:], in_=theta_bytes.rearrange("(g p t) o -> p g t o", p=P, t=4))
-        for q in range(4):
-            nc.sync.dma_start(out=th_sc[32 * q : 32 * q + 32], in_=rows[q].partition_broadcast(32))
-        load_l(7, 9)
-        load_t0(4, 6)
-        load_l(9, 12)
-        load_t0(6, 9)
-        load_acc(0, 4)
-        load_t0(9, 12)
-        load_acc(4, 8)
-        load_acc(8, 12)
+        def load_t1(g, h0, halves=1):
+            tl = keep.tile([P, 4, 512 * halves], BF16, name="t1_raw%d_%d" % (g, h0))
+            nc.sync.dma_start(out=tl[:], in_=t1_src[g][:, :, 512 * h0 : 512 * (h0 + halves)])
+            for h in range(halves):
+                t1_raw[g, h0 + h] = tl[:, :, 512 * h : 512 * h + 512]
+
+        def load_theta(g):
+            nc.sync.dma_start(out=th_by[:, g], in_=th_src[g])
+
+        def load_theta_scales():
+            rows = theta_scale.rearrange("(g q) o -> q g o", q=4)
+            for q in range(4):
+                nc.sync.dma_start(out=th_sc[32 * q : 32 * q + 32], in_=rows[q].partition_broadcast(32))
 
         t1_il, t1_mx = {}, {}
 
-        def t1_copy(g, h, copy=nc.vector.tensor_copy, f0=0, f1=512):
+        def t1_copy(g, h, f0=0, f1=512, engine="vector"):
             if (g, h) not in t1_il:
                 t1_il[g, h] = work.tile([P, 512, 4], BF16, name="t1_il", bufs=4, align_bytes=64)
+            if engine == "gpsimd":
+                src = t1_raw[g, h][:, :, f0:f1].rearrange("p t f -> p f t")
+                nc.gpsimd.tensor_scalar(out=t1_il[g, h][:, f0:f1, :], in0=src, scalar1=1.0, scalar2=0.0, op0=ALU.mult, op1=ALU.add)
+                return
+            copy = nc.vector.tensor_copy if engine == "vector" else nc.scalar.copy
             copy(
                 out=t1_il[g, h][:].rearrange("p (u c m) t -> p c t m u", u=2, m=2)[:, f0 // 4 : f1 // 4],
                 in_=t1_raw[g, h][:, :, f0:f1].rearrange("p t (c m u) -> p c t m u", m=2, u=2),
@@ -116,11 +116,7 @@ def tile_chebyshev_filter_last_term_d7_kernel(tc, L_bytes, L_scale, t1, t0, thet
             nc.vector.quantize_mx(out=q[:].bitcast(FP8X4), scales=s[:], in_=t1_il[g, h][:].rearrange("p f t -> p (f t)"))
             t1_mx[g, h] = (q, s)
 
-        l_w, l_ps, l_il, l_mx = {}, {}, {}, {}
-
-        def on_vector(n, g):
-            return (g == G1 - 1 and n not in (2, 3)) or (g == 1 and n >= VEC_TWO)
-
+        l_w, l_cast, l_ps, l_il, l_mx, stepped, plain = {}, {}, {}, {}, {}, {}, set()
         k_sc = keep.tile([P, NT, G1], F32, name="k_sc")
 
         def regroup_scales():
@@ -128,43 +124,55 @@ def tile_chebyshev_filter_last_term_d7_kernel(tc, L_bytes, L_scale, t1, t0, thet
                 rows32 = slice(32 * q, 32 * q + 32)
                 nc.vector.tensor_copy(out=k_sc[rows32], in_=l_sc[rows32].rearrange("p (n g q) -> p n g q", g=G1, q=4)[:, :, :, q])
 
-        def widen(n, g):
-            wide = work.tile([P, 512], BF16, name="l_wv", bufs=4)
+        def widen(n, *gs):
             src = l_by[n].bitcast(FP8)
-            for q in range(4):
-                b = 4 * g + q
-                nc.vector.tensor_scalar(
-                    out=wide[:].rearrange("p (u m e) -> p m u e", u=2, e=2)[:, 32 * q : 32 * q + 32],
-                    in0=src[:, P * b : P * b + P].rearrange("p (m u e) -> p m u e", u=2, e=2),
-                    scalar1=l_sc[:, NT * n + b : NT * n + b + 1],
-                    scalar2=None,
-                    op0=ALU.mult,
-                )
-            l_w[n, g] = wide[:]
-
-        def cast(n):
-            gs = [g for g in range(G1) if not on_vector(n, g)]
-            wide = work.tile([P, 512 * len(gs)], BF16, name="l_ws", bufs=3)
-            nc.scalar.copy(out=wide[:], in_=l_by[n].bitcast(FP8)[:, : 512 * len(gs)])
             for g in gs:
-                l_w[n, g] = wide[:, 512 * g : 512 * g + 512]
+                wide = work.tile([P, 512], BF16, name="l_wv", bufs=5)
+                for q in range(4):
+                    b = 4 * g + q
+                    nc.vector.tensor_scalar(
+                        out=wide[:].rearrange("p (u m e) -> p m u e", u=2, e=2)[:, 32 * q : 32 * q + 32],
+                        in0=src[:, P * b : P * b + P].rearrange("p (m u e) -> p m u e", u=2, e=2),
+                        scalar1=l_sc[:, NT * n + b : NT * n + b + 1],
+                        scalar2=None,
+                        op0=ALU.mult,
+                    )
+                l_w[n, g] = wide[:]
+
+        def cast(n, g1, g0=0):
+            wide = work.tile([P, 512 * (g1 - g0)], BF16, name="l_ws", bufs=4)
+            nc.scalar.copy(out=wide[:], in_=l_by[n].bitcast(FP8)[:, 512 * g0 : 512 * g1])
+            l_cast[n] = wide[:]
+            for g in range(g0, g1):
+                l_w[n, g] = wide[:, 512 * (g - g0) : 512 * (g - g0) + 512]
+                stepped[n, g] = True
+                plain.add((n, g))
+
+        def reorder(n, g1, g0=0):
+            words = work.tile([P, g1 - g0, 2, P], F32, name="l_wx", bufs=3)
+            nc.scalar.copy(out=words[:], in_=l_cast[n].bitcast(F32).rearrange("p (g m u) -> p g u m", m=P, u=2)[:, g0:g1])
+            for g in range(g0, g1):
+                l_w[n, g] = words[:, g - g0].rearrange("p u m -> p (u m)").bitcast(BF16)
+                stepped[n, g] = False
 
         def l_turn(*items):
-            ps = next_bank(turn_banks, [P, 2, 2, P])
+            ps = take_bank([P, 2, 2, P], *[("l", n, g) for n, g in items])
             for a, (n, g) in enumerate(items):
                 words = l_w[n, g].bitcast(F32)
                 for u in range(2):
-                    part = words[:, P * u : P * u + P] if on_vector(n, g) else words[:, u:256:2]
+                    part = words[:, u:256:2] if stepped.get((n, g)) else words[:, P * u : P * u + P]
                     nc.tensor.transpose(ps[:, a, u, :], part, ident[:])
                 l_ps[n, g] = ps[:, a]
 
-        def l_out(n, g0, g1, vector=False):
+        def l_out(n, *gs, vector=False):
             if n not in l_il:
                 l_il[n] = work.tile([P, V], BF16, name="l_il", bufs=3, align_bytes=64)
-            for g in range(g0, g1):
+            for g in gs:
                 dst = l_il[n][:, 512 * g : 512 * g + 512]
-                if on_vector(n, g):
-                    nc.scalar.copy(out=dst.bitcast(F32).rearrange("p (i u) -> p i u", u=2), in_=l_ps[n, g].rearrange("p u i -> p i u"))
+                emptied(("l", n, g))
+                if (n, g) not in plain:
+                    copy = nc.vector.tensor_copy if vector else nc.scalar.copy
+                    copy(out=dst.bitcast(F32).rearrange("p (i u) -> p i u", u=2), in_=l_ps[n, g].rearrange("p u i -> p i u"))
                     continue
                 dst = dst.rearrange("p (i u e) -> p i u e", u=2, e=2)
                 src = l_ps[n, g].bitcast(BF16).rearrange("p u (i e) -> p i u e", e=2)
@@ -173,20 +181,22 @@ def tile_chebyshev_filter_last_term_d7_kernel(tc, L_bytes, L_scale, t1, t0, thet
                 else:
                     nc.scalar.activation(out=dst, in_=src, func=ACT.Copy, scale=k_sc[:, n, g : g + 1])
 
-        def l_quant(n):
-            q = work.tile([P, G1 * P], U32, name="l_q", bufs=HEAD + 2, align_bytes=64)
-            s = work.tile([P, G1 * P], U8, name="l_s", bufs=HEAD + 2, align_bytes=64)
-            nc.vector.quantize_mx(out=q[:].bitcast(FP8X4), scales=s[:], in_=l_il[n][:])
-            l_mx[n] = (q, s)
+        def l_quant(n, g0=0, g1=G1):
+            if n not in l_mx:
+                q = work.tile([P, G1 * P], U32, name="l_q", bufs=6, align_bytes=64)
+                s = work.tile([P, G1 * P], U8, name="l_s", bufs=6, align_bytes=64)
+                l_mx[n] = (q, s)
+            q, s = l_mx[n]
+            nc.vector.quantize_mx(out=q[:, P * g0 : P * g1].bitcast(FP8X4), scales=s[:, P * g0 : P * g1], in_=l_il[n][:, 512 * g0 : 512 * g1])
 
         p_ps, z_sb, zt_ps, z_il, z_mx = {}, {}, {}, {}, {}
 
-        def mm1(n, h, gs=range(G1)):
+        def mm1(n, h, *gs):
             if (n, h) not in p_ps:
-                p_ps[n, h] = next_bank(sum_banks, [P, 512])
+                p_ps[n, h] = take_bank([P, 512], ("p", n, h))
             ps = p_ps[n, h]
             lq, ls = l_mx[n]
-            for g in gs:
+            for g in gs or range(G1):
                 cols = slice(P * g, P * g + P)
                 tq, ts = t1_mx[g, h]
                 nc.tensor.matmul_mx(
@@ -200,43 +210,45 @@ def tile_chebyshev_filter_last_term_d7_kernel(tc, L_bytes, L_scale, t1, t0, thet
                 )
 
         def z_step(n, h):
-            z = work.tile([P, 2, 256], BF16, name="z_sb%d" % h, bufs=9)
+            z = work.tile([P, 2, 256], BF16, name="z_sb%d" % h, bufs=7)
             nc.vector.scalar_tensor_tensor(
                 out=z[:],
                 in0=p_ps[n, h][:].rearrange("p (u b) -> p u b", u=2),
                 scalar=2.0,
-                in1=t0_sb[n][:, 512 * h : 512 * h + 512].rearrange("p (b u) -> p u b", u=2),
+                in1=t0_sb[n, h].rearrange("p (b u) -> p u b", u=2),
                 op0=ALU.mult,
                 op1=ALU.subtract,
             )
             z_sb[n, h] = z
+            emptied(("p", n, h))
 
-        def z_turn(n):
-            zt_ps[n] = next_bank(turn_banks, [P, G2, 2, P])
-            for g in range(G2):
+        def z_turn(n, *gs):
+            if n not in zt_ps:
+                zt_ps[n] = take_bank([P, G2, 2, P], ("z", n, 0), ("z", n, 1))
+            for g in gs or range(G2):
                 for u in range(2):
                     nc.tensor.transpose(zt_ps[n][:, g, u, :], z_sb[n, g][:, u, :].bitcast(F32), ident[:])
 
-        def z_out(n, g=None):
+        def z_out(n, g0=0, g1=G2):
             if n not in z_il:
                 z_il[n] = work.tile([P, 1024], BF16, name="z_il", bufs=4, align_bytes=64)
-            gs = slice(0, G2) if g is None else slice(g, g + 1)
             nc.scalar.copy(
-                out=z_il[n][:].bitcast(F32).rearrange("p (g i u) -> p g i u", g=G2, u=2)[:, gs],
-                in_=zt_ps[n][:].rearrange("p g u i -> p g i u")[:, gs],
+                out=z_il[n][:].bitcast(F32).rearrange("p (g i u) -> p g i u", g=G2, u=2)[:, g0:g1],
+                in_=zt_ps[n][:].rearrange("p g u i -> p g i u")[:, g0:g1],
             )
+            for g in range(g0, g1):
+                emptied(("z", n, g))
 
-        def z_quant(n, g=None):
+        def z_quant(n, g0=0, g1=G2):
             if n not in z_mx:
                 q = work.tile([P, G2 * P], U32, name="z_q", bufs=8, align_bytes=64)
                 s = work.tile([P, G2 * P], U8, name="z_s", bufs=8, align_bytes=64)
                 z_mx[n] = (q, s)
             q, s = z_mx[n]
-            a, b = (0, G2 * P) if g is None else (P * g, P * g + P)
-            nc.vector.quantize_mx(out=q[:, a:b].bitcast(FP8X4), scales=s[:, a:b], in_=z_il[n][:, 4 * a : 4 * b])
+            nc.vector.quantize_mx(out=q[:, P * g0 : P * g1].bitcast(FP8X4), scales=s[:, P * g0 : P * g1], in_=z_il[n][:, 512 * g0 : 512 * g1])
 
         th_w = keep.tile([P, G2, 4, O], BF16, name="th_w")
-        th_il = keep.tile([P, G2, O, 4], BF16, name="th_il", align_bytes=64)
+        th_il = {}
         th_q = keep.tile([P, G2, O], U32, name="th_q", align_bytes=64)
         th_s = keep.tile([P, G2, O], U8, name="th_s", align_bytes=64)
 
@@ -245,24 +257,31 @@ def tile_chebyshev_filter_last_term_d7_kernel(tc, L_bytes, L_scale, t1, t0, thet
                 for e in range(2):
                     nc.scalar.copy(out=th_w[:, g, 2 * u + e, :], in_=th_by[:, g, 2 * e + u, :].bitcast(FP8))
 
-        def th_scale(g, vector, bs=range(4)):
-            for b in bs:
-                dst = th_il[:, g, P * b : P * b + P, :].rearrange("p (c i) t -> p c t i", i=4)
+        def th_scale(g, engine, *bs):
+            for b in bs or range(4):
+                if (g, b // 2) not in th_il:
+                    th_il[g, b // 2] = work.tile([P, 2, P, 4], BF16, name="th_il", bufs=4, align_bytes=64)
+                dst = th_il[g, b // 2][:, b % 2].rearrange("p (c i) t -> p c t i", i=4)
                 src = th_w[:, g, :, P * b : P * b + P].rearrange("p t (c i) -> p c t i", i=4)
-                if vector:
+                if engine == "vector":
                     nc.vector.tensor_scalar(out=dst, in0=src, scalar1=th_sc[:, g, b : b + 1], scalar2=None, op0=ALU.mult)
+                elif engine == "gpsimd":
+                    dst, src = th_il[g, b // 2][:, b % 2], th_w[:, g, :, P * b : P * b + P].rearrange("p t o -> p o t")
+                    nc.gpsimd.tensor_scalar(out=dst, in0=src, scalar1=th_sc[:, g, b : b + 1], scalar2=0.0, op0=ALU.mult, op1=ALU.add)
                 else:
                     nc.scalar.activation(out=dst, in_=src, func=ACT.Copy, scale=th_sc[:, g, b : b + 1])
 
-        def th_quant(g):
-            nc.vector.quantize_mx(out=th_q[:, g].bitcast(FP8X4), scales=th_s[:, g], in_=th_il[:, g].rearrange("p o t -> p (o t)"))
+        def th_quant(g, half):
+            cols = slice(2 * P * half, 2 * P * half + 2 * P)
+            nc.vector.quantize_mx(out=th_q[:, g, cols].bitcast(FP8X4), scales=th_s[:, g, cols], in_=th_il[g, half][:].rearrange("p b o t -> p (b o t)"))
 
         y_ps, sums = {}, {}
 
-        def mm2(n):
-            y_ps[n] = next_bank(sum_banks, [P, O])
+        def mm2(n, *gs):
+            if n not in y_ps:
+                y_ps[n] = take_bank([P, O], ("y", n))
             zq, zs = z_mx[n]
-            for g in range(G2):
+            for g in gs or range(G2):
                 cols = slice(P * g, P * g + P)
                 nc.tensor.matmul_mx(
                     out=y_ps[n][:],
@@ -274,219 +293,275 @@ def tile_chebyshev_filter_last_term_d7_kernel(tc, L_bytes, L_scale, t1, t0, thet
                     stop=(g == G2 - 1),
                 )
 
-        def add_acc(n, cols=slice(0, O)):
-            sums[n, cols.start] = work.tile([P, cols.stop - cols.start], F32, name="y_acc", bufs=4)
-            nc.vector.tensor_tensor(out=sums[n, cols.start][:], in0=y_ps[n][:, cols], in1=acc_sb[n][:, cols], op=ALU.add)
+        def add_acc(n, c0=0, c1=O):
+            sums[n, c0] = work.tile([P, c1 - c0], F32, name="y_acc", bufs=4)
+            nc.vector.tensor_tensor(out=sums[n, c0][:], in0=y_ps[n][:, c0:c1], in1=acc_sb[n][:, c0:c1], op=ALU.add)
+            if c1 == O:
+                emptied(("y", n))
 
-        def relu_store(n, cols=slice(0, O)):
-            r = work.tile([P, cols.stop - cols.start], F32, name="res", bufs=6)
-            nc.scalar.activation(out=r[:], in_=sums[n, cols.start][:], func=ACT.Relu)
-            nc.sync.dma_start(out=out[P * n : P * n + P, cols], in_=r[:])
+        def relu_store(n, c0=0, c1=O, engine="scalar"):
+            r = work.tile([P, c1 - c0], F32, name="res", bufs=6)
+            if engine == "scalar":
+                nc.scalar.activation(out=r[:], in_=sums[n, c0][:], func=ACT.Relu)
+            else:
+                eng = nc.vector if engine == "vector" else nc.gpsimd
+                eng.tensor_scalar(out=r[:], in0=sums[n, c0][:], scalar1=F32_MAX, scalar2=0.0, op0=ALU.min, op1=ALU.max)
+            nc.sync.dma_start(out=out[P * n : P * n + P, c0:c1], in_=r[:])
 
-        def turn_l(n):
-            l_turn((n, 0), (n, 1))
-            l_turn((n, 2))
+        nc.scalar.dma_start(out=l_sc[:], in_=L_scale.rearrange("a b -> (a b)").partition_broadcast(P))
+        warm = keep.tile([P, 2], F32, name="warm")
+        nc.vector.memset(warm[:, 0:1], 0.0)
+        nc.scalar.activation(out=warm[:, 1:2], in_=warm[:, 0:1], func=ACT.Copy)
+        load_l(0, 1)
+        load_l(1, 2)
+        load_t1(0, 0)
+        load_t1(0, 1)
+        load_l(2, 4)
+        load_t1(1, 0, 2)
+        load_l(4, 5)
+        load_t1(2, 0, 2)
+        load_l(5, 7)
+        load_t0(0, 2)
+        load_t0(2, 4)
+        load_theta(0)
+        load_theta(1)
+        load_theta_scales()
+        load_l(7, 9)
+        load_t0(4, 6)
+        load_l(9, 12)
+        load_t0(6, 9)
+        load_acc(0, 4)
+        load_t0(9, 12)
+        load_acc(4, 8)
+        load_acc(8, 12)
 
-        def out_l(n):
-            l_out(n, 0, 2)
-            l_out(n, 2, 3)
-
+        cast(0, 1)
+        cast(0, 2, 1)
+        cast(1, 2)
+        l_turn((0, 0))
         regroup_scales()
-        cast(0)
         widen(0, 2)
-        turn_l(0)
-        cast(1)
+        l_turn((0, 1), (0, 2))
+        l_out(0, 0, 1, 2)
         widen(1, 2)
         t1_copy(0, 0)
-        out_l(0)
-        turn_l(1)
-        out_l(1)
-        cast(2)
+        l_turn((1, 0), (1, 1))
+        l_turn((1, 2))
+        t1_copy(0, 1, 0, 128)
+        l_out(1, 0, 1, 2)
         t1_quant(0, 0)
         l_quant(0)
-        t1_copy(0, 1)
-        mm1(0, 0, (0,))
-        turn_l(2)
-        cast(3)
+        t1_copy(0, 1, 128, 512)
+        cast(2, 3)
+        mm1(0, 0, 0)
         l_quant(1)
+        cast(3, 3)
         t1_quant(0, 1)
-        mm1(1, 0, (0,))
-        for n in range(2):
-            mm1(n, 1, (0,))
-        t1_copy(1, 1, nc.scalar.copy)
+        l_turn((2, 0), (2, 1))
+        t1_copy(1, 1, engine="scalar")
         t1_copy(1, 0)
-        l_turn((3, 0), (3, 1))
-        l_out(2, 0, 2)
-        l_out(2, 2, 3, vector=True)
+        l_turn((2, 2))
+        mm1(1, 0, 0)
+        l_out(2, 2, vector=True)
+        mm1(0, 1, 0)
         t1_quant(1, 0)
+        mm1(1, 1, 0)
+        l_out(2, 0, 1)
         widen(4, 2)
         t1_quant(1, 1)
-        cast(4)
-        t1_copy(2, 1, nc.scalar.copy, 256, 512)
+        l_turn((3, 0), (3, 1))
         t1_copy(2, 0)
-        for h in range(G2):
-            for n in range(2):
-                mm1(n, h, (1,))
-        l_turn((3, 2))
+        mm1(0, 0, 1)
+        cast(4, 2)
+        mm1(1, 0, 1)
+        mm1(0, 1, 1)
+        t1_copy(2, 1, 192, 512, engine="scalar")
+        mm1(1, 1, 1)
         l_quant(2)
-        l_out(3, 0, 2)
+        l_turn((3, 2))
         l_turn((4, 0), (4, 1))
-        mm1(2, 0, (0, 1))
-        t1_copy(2, 1, nc.vector.tensor_copy, 0, 256)
+        t1_copy(2, 1, 0, 192)
+        l_out(3, 0, 1)
         t1_quant(2, 0)
+        mm1(2, 0, 0, 1)
         t1_quant(2, 1)
-        l_out(3, 2, 3)
-        for n in range(3):
-            mm1(n, 0, (2,))
-        for n in range(2):
-            mm1(n, 1, (2,))
-        cast(5)
-        cast(6)
-        l_out(4, 0, 2)
-
-        def both(step, n):
-            for h in range(G2):
-                step(n, h)
-
-        def finish(n):
-            add_acc(n)
-            relu_store(n)
-
+        mm1(0, 0, 2)
+        l_out(3, 2)
+        mm1(1, 0, 2)
+        mm1(2, 0, 2)
         z_step(0, 0)
-        mm1(2, 1)
-        turn_banks.append(sum_banks.pop(0))
+        cast(5, 2)
+        mm1(0, 1, 2)
+        mm1(1, 1, 2)
         widen(5, 2)
+        cast(6, 2)
+        mm1(2, 1)
         l_quant(3)
+        l_out(4, 0, 1)
         widen(6, 2)
-        z_step(1, 0)
         l_turn((4, 2), (5, 2))
+        z_step(1, 0)
         l_turn((5, 0), (5, 1))
-        turn_l(6)
-        cast(7)
-        l_out(4, 2, 3)
-        l_out(5, 2, 3)
-        l_out(5, 0, 2)
-        out_l(6)
-        cast(8)
-        th_widen(0)
         z_step(0, 1)
+        cast(7, 2)
+        l_turn((6, 0), (6, 1))
         z_step(1, 1)
+        l_out(4, 2)
+        l_out(5, 2)
+        l_turn((6, 2))
         z_step(2, 0)
+        l_out(5, 0, 1)
+        mm1(3, 0)
         l_quant(4)
+        mm1(3, 1)
         z_step(2, 1)
-        both(mm1, 3)
-        both(mm1, 4)
+        l_out(6, 0, 1, 2)
         widen(7, 2)
+        mm1(4, 0)
         z_step(3, 0)
+        mm1(4, 1)
         widen(8, 2)
+        cast(8, 2)
         z_step(3, 1)
+        th_widen(0)
+        l_turn((7, 0), (7, 1))
         l_quant(5)
-        turn_l(7)
-        turn_l(8)
-        cast(9)
-        out_l(7)
-        out_l(8)
-        cast(10)
-        th_scale(0, False, (0, 1))
-        both(z_step, 4)
+        l_turn((7, 2))
+        z_step(4, 0)
+        l_turn((8, 0), (8, 1))
+        cast(9, 1)
+        z_step(4, 1)
+        l_out(7, 0, 1, 2)
+        l_turn((8, 2))
+        mm1(5, 0)
         l_quant(6)
-        widen(9, 1)
-        widen(9, 2)
-        both(mm1, 5)
-        both(mm1, 6)
+        widen(9, 1, 2)
+        mm1(5, 1)
+        l_out(8, 0, 1, 2)
         z_step(5, 0)
+        mm1(6, 0)
         l_quant(7)
         z_step(5, 1)
+        mm1(6, 1)
+        cast(10, 1)
+        th_scale(0, "scalar", 0, 1)
+        widen(10, 1, 2)
         z_turn(0)
         z_turn(1)
-        turn_l(9)
+        z_step(6, 0)
         z_out(0)
+        l_turn((9, 0), (9, 1))
+        z_step(6, 1)
+        l_turn((9, 2))
         z_out(1)
-        out_l(9)
-        th_widen(1)
-        widen(10, 1)
-        widen(10, 2)
-        both(z_step, 6)
+        mm1(7, 0)
         l_quant(8)
-        th_scale(0, True, (2, 3))
-        both(mm1, 7)
-        z_turn(2)
-        z_turn(3)
-        turn_l(10)
-        cast(11)
-        z_out(2)
-        z_out(3)
-        out_l(10)
-        th_scale(1, False)
+        l_out(9, 0, 1, 2)
+        th_scale(0, "vector", 2, 3)
+        mm1(7, 1)
         z_step(7, 0)
+        th_widen(1)
+        z_turn(2)
         l_quant(9)
+        z_turn(3)
         z_step(7, 1)
-        widen(11, 1)
-        widen(11, 2)
-        th_quant(0)
-        both(mm1, 8)
-        both(mm1, 9)
-        z_turn(4)
-        z_turn(5)
-        turn_l(11)
-        both(z_step, 8)
+        l_turn((10, 0), (10, 1))
+        cast(11, 1)
+        widen(11, 1, 2)
+        z_out(2)
+        l_turn((10, 2))
+        mm1(8, 0)
+        z_out(3)
+        th_quant(0, 0)
+        th_quant(0, 1)
+        l_out(10, 0, 1, 2)
+        mm1(8, 1)
+        z_step(8, 0)
+        mm1(9, 0)
+        z_step(8, 1)
+        th_scale(1, "scalar", 0, 1)
+        mm1(9, 1)
         z_quant(0)
         z_quant(1)
+        th_scale(1, "scalar", 2, 3)
         l_quant(10)
-        both(z_step, 9)
-        th_quant(1)
+        z_turn(4)
+        z_step(9, 0)
+        z_turn(5)
+        l_turn((11, 0), (11, 1))
         z_out(4)
+        z_step(9, 1)
+        l_turn((11, 2))
         z_out(5)
-        out_l(11)
-        both(mm1, 10)
-        mm2(0)
-        mm2(1)
+        z_turn(6)
+        th_quant(1, 0)
+        th_quant(1, 1)
+        mm1(10, 0)
+        l_out(11, 0, 1, 2)
         z_quant(2)
         z_quant(3)
-        both(z_step, 10)
-        mm2(2)
-        mm2(3)
+        mm1(10, 1)
+        z_step(10, 0)
+        z_out(6)
+        mm2(0)
+        z_step(10, 1)
+        mm2(1)
         z_quant(4)
-        finish(0)
+        mm2(2)
+        add_acc(0)
+        mm2(3)
         z_quant(5)
-        finish(1)
+        add_acc(1)
+        relu_store(0)
         mm2(4)
-        mm2(5)
         l_quant(11)
-        finish(2)
-        for n in range(6, 10):
-            z_turn(n)
-        for n in range(3, 6):
-            add_acc(n)
-        for n in range(6, 10):
-            z_out(n)
-        both(mm1, 11)
+        mm2(5)
+        relu_store(1)
+        add_acc(2)
+        z_turn(7)
         z_quant(6)
-        z_quant(7)
-        mm2(6)
-        mm2(7)
-        relu_store(3)
-        relu_store(4)
-        relu_store(5)
-        both(z_step, 11)
-        z_quant(8)
-        z_quant(9)
+        z_turn(8)
+        add_acc(3)
+        relu_store(2)
+        z_turn(9)
+        z_out(7)
+        add_acc(4)
         z_turn(10)
-        z_turn(11)
+        mm1(11, 0)
+        relu_store(3)
+        add_acc(5)
+        z_out(8)
+        z_quant(7)
+        mm1(11, 1)
+        z_step(11, 0)
+        relu_store(4)
+        mm2(6)
+        z_out(9)
+        z_quant(8)
+        z_step(11, 1)
+        mm2(7)
+        relu_store(5)
         add_acc(6)
-        add_acc(7)
         z_out(10)
-        z_out(11)
-        relu_store(6)
-        relu_store(7)
+        z_turn(11)
+        z_quant(9)
         mm2(8)
+        add_acc(7)
+        z_out(11)
         mm2(9)
         z_quant(10)
-        z_quant(11)
+        relu_store(6)
+        add_acc(8)
+        relu_store(7)
         mm2(10)
+        z_quant(11)
+        add_acc(9)
+        relu_store(8)
         mm2(11)
-        for n in (8, 9, 10):
-            finish(n)
-        for cols in (slice(0, O // 2), slice(O // 2, O)):
-            add_acc(11, cols)
-            relu_store(11, cols)
+        add_acc(10)
+        relu_store(9)
+        add_acc(11, 0, 256)
+        relu_store(10)
+        add_acc(11, 256, 512)
+        relu_store(11, 0, 256)
+        relu_store(11, 256, 512)

@@ -15,11 +15,13 @@ FP8X4 = mybir.dt.float8_e4m3fn_x4
 ACT = mybir.ActivationFunctionType
 ALU = mybir.AluOpType
 
-F32_MAX = (2.0 - 2.0**-23) * 2.0**127
 P = 128
+K = 512
 NT = V // P
-G1 = V // 512
-G2 = F // 512
+G1 = V // K
+G2 = F // K
+FILL = 128
+SPLIT = 192
 
 
 def tile_chebyshev_filter_last_term_d7_kernel(tc, L_bytes, L_scale, t1, t0, theta_bytes, theta_scale, acc, out):
@@ -33,33 +35,24 @@ def tile_chebyshev_filter_last_term_d7_kernel(tc, L_bytes, L_scale, t1, t0, thet
         ident = keep.tile([P, P], F32, name="ident")
         make_identity(nc, ident[:])
 
-        free_banks, held = list(range(8)), {}
+        sum_banks, turn_banks = [0, 1, 2, 3, 4], [5, 6, 7]
 
-        def take_bank(shape, *readers):
-            b = free_banks.pop(0)
-            for r in readers:
-                held[r] = b
+        def next_bank(ring, shape):
+            b = ring.pop(0)
+            ring.append(b)
             return psum.tile(shape, F32, name="bank%d" % b)
 
-        def emptied(reader):
-            b = held.pop(reader)
-            if b not in held.values():
-                free_banks.append(b)
-
-        def warm_up(count):
-            ps = take_bank([P, P], "warm")
-            for k in range(count):
-                nc.tensor.matmul(out=ps[:], lhsT=ident[:], rhs=ident[:], start=True, stop=True)
-            emptied("warm")
+        def hand_over(giver, taker):
+            taker.append(giver.pop(0))
 
         l_sc = keep.tile([P, NT * NT], F32, name="l_sc")
         th_sc = keep.tile([P, G2, 4], F32, name="th_sc")
+        th_by = keep.tile([P, G2, 4, O], U8, name="th_by")
         l_rows = L_bytes.rearrange("(n p) j -> p n j", p=P)
         t1_src = t1.rearrange("(g p t) f -> g p t f", p=P, t=4)
         t0_rows = t0.rearrange("(n p) f -> p n f", p=P)
         acc_rows = acc.rearrange("(n p) o -> p n o", p=P)
-        th_src = theta_bytes.rearrange("(g p t) o -> g p t o", p=P, t=4)
-        th_by = keep.tile([P, G2, 4, O], U8, name="th_by")
+        th_src = theta_bytes.rearrange("(g p j) o -> g p j o", p=P, j=4)
         l_by, t1_raw, t0_sb, acc_sb = {}, {}, {}, {}
 
         def load_rows(store, rows, dtype, name, n0, n1):
@@ -71,52 +64,42 @@ def tile_chebyshev_filter_last_term_d7_kernel(tc, L_bytes, L_scale, t1, t0, thet
         def load_l(n0, n1):
             load_rows(l_by, l_rows, U8, "l_by", n0, n1)
 
+        def load_t0(n0, n1):
+            load_rows(t0_sb, t0_rows, BF16, "t0_sb", n0, n1)
+
         def load_acc(n0, n1):
             load_rows(acc_sb, acc_rows, BF16, "acc_sb", n0, n1)
 
-        def load_t0(n0, n1, h0=0, h1=G2):
-            tl = keep.tile([P, n1 - n0, 512 * (h1 - h0)], BF16, name="t0_sb%d_%d" % (n0, h0))
-            nc.sync.dma_start(out=tl[:], in_=t0_rows[:, n0:n1, 512 * h0 : 512 * h1])
-            for n in range(n0, n1):
-                for h in range(h0, h1):
-                    t0_sb[n, h] = tl[:, n - n0, 512 * (h - h0) : 512 * (h - h0) + 512]
+        def load_t1(g, h0, h1):
+            tl = keep.tile([P, 4, K * (h1 - h0)], BF16, name="t1_raw%d_%d" % (g, h0))
+            nc.sync.dma_start(out=tl[:], in_=t1_src[g][:, :, K * h0 : K * h1])
+            for h in range(h0, h1):
+                t1_raw[g, h] = tl[:, :, K * (h - h0) : K * (h - h0 + 1)]
 
-        def load_t1(g, h0, halves=1):
-            tl = keep.tile([P, 4, 512 * halves], BF16, name="t1_raw%d_%d" % (g, h0))
-            nc.sync.dma_start(out=tl[:], in_=t1_src[g][:, :, 512 * h0 : 512 * (h0 + halves)])
-            for h in range(halves):
-                t1_raw[g, h0 + h] = tl[:, :, 512 * h : 512 * h + 512]
-
-        def load_theta(g):
-            nc.sync.dma_start(out=th_by[:, g], in_=th_src[g])
-
-        def load_theta_scales():
+        def load_theta():
+            for g in range(G2):
+                nc.sync.dma_start(out=th_by[:, g], in_=th_src[g])
             rows = theta_scale.rearrange("(g q) o -> q g o", q=4)
             for q in range(4):
                 nc.sync.dma_start(out=th_sc[32 * q : 32 * q + 32], in_=rows[q].partition_broadcast(32))
 
         t1_il, t1_mx = {}, {}
 
-        def t1_copy(g, h, f0=0, f1=512, engine="vector"):
+        def t1_copy(g, h, f0=0, f1=K, copy=nc.vector.tensor_copy):
             if (g, h) not in t1_il:
-                t1_il[g, h] = work.tile([P, 512, 4], BF16, name="t1_il", bufs=4, align_bytes=64)
-            if engine == "gpsimd":
-                src = t1_raw[g, h][:, :, f0:f1].rearrange("p t f -> p f t")
-                nc.gpsimd.tensor_scalar(out=t1_il[g, h][:, f0:f1, :], in0=src, scalar1=1.0, scalar2=0.0, op0=ALU.mult, op1=ALU.add)
-                return
-            copy = nc.vector.tensor_copy if engine == "vector" else nc.scalar.copy
+                t1_il[g, h] = work.tile([P, K, 4], BF16, name="t1_il", bufs=4, align_bytes=64)
             copy(
                 out=t1_il[g, h][:].rearrange("p (u c m) t -> p c t m u", u=2, m=2)[:, f0 // 4 : f1 // 4],
                 in_=t1_raw[g, h][:, :, f0:f1].rearrange("p t (c m u) -> p c t m u", m=2, u=2),
             )
 
         def t1_quant(g, h):
-            q = keep.tile([P, 512], U32, name="t1_q%d_%d" % (g, h), align_bytes=64)
-            s = keep.tile([P, 512], U8, name="t1_s%d_%d" % (g, h), align_bytes=64)
+            q = keep.tile([P, K], U32, name="t1_q%d_%d" % (g, h), align_bytes=64)
+            s = keep.tile([P, K], U8, name="t1_s%d_%d" % (g, h), align_bytes=64)
             nc.vector.quantize_mx(out=q[:].bitcast(FP8X4), scales=s[:], in_=t1_il[g, h][:].rearrange("p f t -> p (f t)"))
             t1_mx[g, h] = (q, s)
 
-        l_w, l_cast, l_ps, l_il, l_mx, stepped, plain = {}, {}, {}, {}, {}, {}, set()
+        l_w, l_ps, l_il, l_mx, unscaled = {}, {}, {}, {}, set()
         k_sc = keep.tile([P, NT, G1], F32, name="k_sc")
 
         def regroup_scales():
@@ -127,7 +110,7 @@ def tile_chebyshev_filter_last_term_d7_kernel(tc, L_bytes, L_scale, t1, t0, thet
         def widen(n, *gs):
             src = l_by[n].bitcast(FP8)
             for g in gs:
-                wide = work.tile([P, 512], BF16, name="l_wv", bufs=5)
+                wide = work.tile([P, K], BF16, name="l_wv", bufs=5)
                 for q in range(4):
                     b = 4 * g + q
                     nc.vector.tensor_scalar(
@@ -139,40 +122,33 @@ def tile_chebyshev_filter_last_term_d7_kernel(tc, L_bytes, L_scale, t1, t0, thet
                     )
                 l_w[n, g] = wide[:]
 
-        def cast(n, g1, g0=0):
-            wide = work.tile([P, 512 * (g1 - g0)], BF16, name="l_ws", bufs=4)
-            nc.scalar.copy(out=wide[:], in_=l_by[n].bitcast(FP8)[:, 512 * g0 : 512 * g1])
-            l_cast[n] = wide[:]
+        def cast(n, g0, g1):
+            wide = work.tile([P, K * (g1 - g0)], BF16, name="l_ws", bufs=4)
+            nc.scalar.copy(out=wide[:], in_=l_by[n].bitcast(FP8)[:, K * g0 : K * g1])
             for g in range(g0, g1):
-                l_w[n, g] = wide[:, 512 * (g - g0) : 512 * (g - g0) + 512]
-                stepped[n, g] = True
-                plain.add((n, g))
-
-        def reorder(n, g1, g0=0):
-            words = work.tile([P, g1 - g0, 2, P], F32, name="l_wx", bufs=3)
-            nc.scalar.copy(out=words[:], in_=l_cast[n].bitcast(F32).rearrange("p (g m u) -> p g u m", m=P, u=2)[:, g0:g1])
-            for g in range(g0, g1):
-                l_w[n, g] = words[:, g - g0].rearrange("p u m -> p (u m)").bitcast(BF16)
-                stepped[n, g] = False
+                l_w[n, g] = wide[:, K * (g - g0) : K * (g - g0 + 1)]
+                unscaled.add((n, g))
 
         def l_turn(*items):
-            ps = take_bank([P, 2, 2, P], *[("l", n, g) for n, g in items])
+            ps = next_bank(turn_banks, [P, 2, 2, P])
             for a, (n, g) in enumerate(items):
-                words = l_w[n, g].bitcast(F32)
+                pairs = l_w[n, g].bitcast(F32)
                 for u in range(2):
-                    part = words[:, u:256:2] if stepped.get((n, g)) else words[:, P * u : P * u + P]
+                    part = pairs[:, u : 2 * P : 2] if (n, g) in unscaled else pairs[:, P * u : P * u + P]
                     nc.tensor.transpose(ps[:, a, u, :], part, ident[:])
                 l_ps[n, g] = ps[:, a]
 
-        def l_out(n, *gs, vector=False):
+        def turn_tile(n):
+            l_turn((n, 0), (n, 1))
+            l_turn((n, 2))
+
+        def l_out(n, gs=range(G1), vector=False):
             if n not in l_il:
                 l_il[n] = work.tile([P, V], BF16, name="l_il", bufs=3, align_bytes=64)
             for g in gs:
-                dst = l_il[n][:, 512 * g : 512 * g + 512]
-                emptied(("l", n, g))
-                if (n, g) not in plain:
-                    copy = nc.vector.tensor_copy if vector else nc.scalar.copy
-                    copy(out=dst.bitcast(F32).rearrange("p (i u) -> p i u", u=2), in_=l_ps[n, g].rearrange("p u i -> p i u"))
+                dst = l_il[n][:, K * g : K * g + K]
+                if (n, g) not in unscaled:
+                    nc.scalar.copy(out=dst.bitcast(F32).rearrange("p (i u) -> p i u", u=2), in_=l_ps[n, g].rearrange("p u i -> p i u"))
                     continue
                 dst = dst.rearrange("p (i u e) -> p i u e", u=2, e=2)
                 src = l_ps[n, g].bitcast(BF16).rearrange("p u (i e) -> p i u e", e=2)
@@ -181,26 +157,23 @@ def tile_chebyshev_filter_last_term_d7_kernel(tc, L_bytes, L_scale, t1, t0, thet
                 else:
                     nc.scalar.activation(out=dst, in_=src, func=ACT.Copy, scale=k_sc[:, n, g : g + 1])
 
-        def l_quant(n, g0=0, g1=G1):
-            if n not in l_mx:
-                q = work.tile([P, G1 * P], U32, name="l_q", bufs=6, align_bytes=64)
-                s = work.tile([P, G1 * P], U8, name="l_s", bufs=6, align_bytes=64)
-                l_mx[n] = (q, s)
-            q, s = l_mx[n]
-            nc.vector.quantize_mx(out=q[:, P * g0 : P * g1].bitcast(FP8X4), scales=s[:, P * g0 : P * g1], in_=l_il[n][:, 512 * g0 : 512 * g1])
+        def l_quant(n):
+            q = work.tile([P, G1 * P], U32, name="l_q", bufs=6, align_bytes=64)
+            s = work.tile([P, G1 * P], U8, name="l_s", bufs=6, align_bytes=64)
+            nc.vector.quantize_mx(out=q[:].bitcast(FP8X4), scales=s[:], in_=l_il[n][:])
+            l_mx[n] = (q, s)
 
         p_ps, z_sb, zt_ps, z_il, z_mx = {}, {}, {}, {}, {}
 
-        def mm1(n, h, *gs):
+        def mm1(n, h, gs=range(G1)):
             if (n, h) not in p_ps:
-                p_ps[n, h] = take_bank([P, 512], ("p", n, h))
-            ps = p_ps[n, h]
+                p_ps[n, h] = next_bank(sum_banks, [P, K])
             lq, ls = l_mx[n]
-            for g in gs or range(G1):
+            for g in gs:
                 cols = slice(P * g, P * g + P)
                 tq, ts = t1_mx[g, h]
                 nc.tensor.matmul_mx(
-                    out=ps[:],
+                    out=p_ps[n, h][:],
                     lhsT=lq[:, cols].bitcast(FP8X4),
                     lhsT_scale=ls[:, cols],
                     rhs=tq[:].bitcast(FP8X4),
@@ -210,78 +183,68 @@ def tile_chebyshev_filter_last_term_d7_kernel(tc, L_bytes, L_scale, t1, t0, thet
                 )
 
         def z_step(n, h):
-            z = work.tile([P, 2, 256], BF16, name="z_sb%d" % h, bufs=7)
+            z = work.tile([P, 2, 2 * P], BF16, name="z_sb%d" % h, bufs=7)
             nc.vector.scalar_tensor_tensor(
                 out=z[:],
                 in0=p_ps[n, h][:].rearrange("p (u b) -> p u b", u=2),
                 scalar=2.0,
-                in1=t0_sb[n, h].rearrange("p (b u) -> p u b", u=2),
+                in1=t0_sb[n][:, K * h : K * h + K].rearrange("p (b u) -> p u b", u=2),
                 op0=ALU.mult,
                 op1=ALU.subtract,
             )
             z_sb[n, h] = z
-            emptied(("p", n, h))
 
-        def z_turn(n, *gs):
-            if n not in zt_ps:
-                zt_ps[n] = take_bank([P, G2, 2, P], ("z", n, 0), ("z", n, 1))
-            for g in gs or range(G2):
+        def z_turn(n):
+            zt_ps[n] = next_bank(turn_banks, [P, G2, 2, P])
+            for g in range(G2):
                 for u in range(2):
                     nc.tensor.transpose(zt_ps[n][:, g, u, :], z_sb[n, g][:, u, :].bitcast(F32), ident[:])
 
-        def z_out(n, g0=0, g1=G2):
-            if n not in z_il:
-                z_il[n] = work.tile([P, 1024], BF16, name="z_il", bufs=4, align_bytes=64)
+        def z_out(n):
+            z_il[n] = work.tile([P, F], BF16, name="z_il", bufs=4, align_bytes=64)
             nc.scalar.copy(
-                out=z_il[n][:].bitcast(F32).rearrange("p (g i u) -> p g i u", g=G2, u=2)[:, g0:g1],
-                in_=zt_ps[n][:].rearrange("p g u i -> p g i u")[:, g0:g1],
+                out=z_il[n][:].bitcast(F32).rearrange("p (g i u) -> p g i u", g=G2, u=2),
+                in_=zt_ps[n][:].rearrange("p g u i -> p g i u"),
             )
-            for g in range(g0, g1):
-                emptied(("z", n, g))
 
-        def z_quant(n, g0=0, g1=G2):
-            if n not in z_mx:
-                q = work.tile([P, G2 * P], U32, name="z_q", bufs=8, align_bytes=64)
-                s = work.tile([P, G2 * P], U8, name="z_s", bufs=8, align_bytes=64)
-                z_mx[n] = (q, s)
-            q, s = z_mx[n]
-            nc.vector.quantize_mx(out=q[:, P * g0 : P * g1].bitcast(FP8X4), scales=s[:, P * g0 : P * g1], in_=z_il[n][:, 512 * g0 : 512 * g1])
+        def z_quant(n):
+            q = work.tile([P, G2 * P], U32, name="z_q", bufs=8, align_bytes=64)
+            s = work.tile([P, G2 * P], U8, name="z_s", bufs=8, align_bytes=64)
+            nc.vector.quantize_mx(out=q[:].bitcast(FP8X4), scales=s[:], in_=z_il[n][:])
+            z_mx[n] = (q, s)
 
         th_w = keep.tile([P, G2, 4, O], BF16, name="th_w")
         th_il = {}
         th_q = keep.tile([P, G2, O], U32, name="th_q", align_bytes=64)
         th_s = keep.tile([P, G2, O], U8, name="th_s", align_bytes=64)
 
-        def th_widen(g):
+        def th_cast(g):
             for u in range(2):
                 for e in range(2):
                     nc.scalar.copy(out=th_w[:, g, 2 * u + e, :], in_=th_by[:, g, 2 * e + u, :].bitcast(FP8))
 
-        def th_scale(g, engine, *bs):
-            for b in bs or range(4):
-                if (g, b // 2) not in th_il:
-                    th_il[g, b // 2] = work.tile([P, 2, P, 4], BF16, name="th_il", bufs=4, align_bytes=64)
-                dst = th_il[g, b // 2][:, b % 2].rearrange("p (c i) t -> p c t i", i=4)
+        def th_scale(g, half, vector=False):
+            th_il[g, half] = work.tile([P, 2, P, 4], BF16, name="th_il", bufs=4, align_bytes=64)
+            for b in (2 * half, 2 * half + 1):
+                dst = th_il[g, half][:, b % 2].rearrange("p (c i) t -> p c t i", i=4)
                 src = th_w[:, g, :, P * b : P * b + P].rearrange("p t (c i) -> p c t i", i=4)
-                if engine == "vector":
+                if vector:
                     nc.vector.tensor_scalar(out=dst, in0=src, scalar1=th_sc[:, g, b : b + 1], scalar2=None, op0=ALU.mult)
-                elif engine == "gpsimd":
-                    dst, src = th_il[g, b // 2][:, b % 2], th_w[:, g, :, P * b : P * b + P].rearrange("p t o -> p o t")
-                    nc.gpsimd.tensor_scalar(out=dst, in0=src, scalar1=th_sc[:, g, b : b + 1], scalar2=0.0, op0=ALU.mult, op1=ALU.add)
                 else:
                     nc.scalar.activation(out=dst, in_=src, func=ACT.Copy, scale=th_sc[:, g, b : b + 1])
 
-        def th_quant(g, half):
-            cols = slice(2 * P * half, 2 * P * half + 2 * P)
-            nc.vector.quantize_mx(out=th_q[:, g, cols].bitcast(FP8X4), scales=th_s[:, g, cols], in_=th_il[g, half][:].rearrange("p b o t -> p (b o t)"))
+        def th_quant(g):
+            for half in range(2):
+                cols = slice(2 * P * half, 2 * P * half + 2 * P)
+                src = th_il[g, half][:].rearrange("p b o t -> p (b o t)")
+                nc.vector.quantize_mx(out=th_q[:, g, cols].bitcast(FP8X4), scales=th_s[:, g, cols], in_=src)
 
         y_ps, sums = {}, {}
 
-        def mm2(n, *gs):
-            if n not in y_ps:
-                y_ps[n] = take_bank([P, O], ("y", n))
+        def mm2(n):
+            y_ps[n] = next_bank(sum_banks, [P, O])
             zq, zs = z_mx[n]
-            for g in gs or range(G2):
+            for g in range(G2):
                 cols = slice(P * g, P * g + P)
                 nc.tensor.matmul_mx(
                     out=y_ps[n][:],
@@ -296,17 +259,15 @@ def tile_chebyshev_filter_last_term_d7_kernel(tc, L_bytes, L_scale, t1, t0, thet
         def add_acc(n, c0=0, c1=O):
             sums[n, c0] = work.tile([P, c1 - c0], F32, name="y_acc", bufs=4)
             nc.vector.tensor_tensor(out=sums[n, c0][:], in0=y_ps[n][:, c0:c1], in1=acc_sb[n][:, c0:c1], op=ALU.add)
-            if c1 == O:
-                emptied(("y", n))
 
-        def relu_store(n, c0=0, c1=O, engine="scalar"):
+        def relu_store(n, c0=0, c1=O):
             r = work.tile([P, c1 - c0], F32, name="res", bufs=6)
-            if engine == "scalar":
-                nc.scalar.activation(out=r[:], in_=sums[n, c0][:], func=ACT.Relu)
-            else:
-                eng = nc.vector if engine == "vector" else nc.gpsimd
-                eng.tensor_scalar(out=r[:], in0=sums[n, c0][:], scalar1=F32_MAX, scalar2=0.0, op0=ALU.min, op1=ALU.max)
+            nc.scalar.activation(out=r[:], in_=sums[n, c0][:], func=ACT.Relu)
             nc.sync.dma_start(out=out[P * n : P * n + P, c0:c1], in_=r[:])
+
+        def both(step, n):
+            for h in range(G2):
+                step(n, h)
 
         nc.scalar.dma_start(out=l_sc[:], in_=L_scale.rearrange("a b -> (a b)").partition_broadcast(P))
         warm = keep.tile([P, 2], F32, name="warm")
@@ -314,8 +275,8 @@ def tile_chebyshev_filter_last_term_d7_kernel(tc, L_bytes, L_scale, t1, t0, thet
         nc.scalar.activation(out=warm[:, 1:2], in_=warm[:, 0:1], func=ACT.Copy)
         load_l(0, 1)
         load_l(1, 2)
-        load_t1(0, 0)
-        load_t1(0, 1)
+        load_t1(0, 0, 1)
+        load_t1(0, 1, 2)
         load_l(2, 4)
         load_t1(1, 0, 2)
         load_l(4, 5)
@@ -323,9 +284,7 @@ def tile_chebyshev_filter_last_term_d7_kernel(tc, L_bytes, L_scale, t1, t0, thet
         load_l(5, 7)
         load_t0(0, 2)
         load_t0(2, 4)
-        load_theta(0)
-        load_theta(1)
-        load_theta_scales()
+        load_theta()
         load_l(7, 9)
         load_t0(4, 6)
         load_l(9, 12)
@@ -335,233 +294,188 @@ def tile_chebyshev_filter_last_term_d7_kernel(tc, L_bytes, L_scale, t1, t0, thet
         load_acc(4, 8)
         load_acc(8, 12)
 
-        cast(0, 1)
-        cast(0, 2, 1)
-        cast(1, 2)
-        l_turn((0, 0))
         regroup_scales()
         widen(0, 2)
-        l_turn((0, 1), (0, 2))
-        l_out(0, 0, 1, 2)
         widen(1, 2)
+        cast(0, 0, 1)
+        cast(0, 1, 2)
+        cast(1, 0, 2)
+        l_turn((0, 0))
+        l_turn((0, 1), (0, 2))
+        l_out(0)
+        turn_tile(1)
+        l_out(1)
         t1_copy(0, 0)
-        l_turn((1, 0), (1, 1))
-        l_turn((1, 2))
-        t1_copy(0, 1, 0, 128)
-        l_out(1, 0, 1, 2)
+        t1_copy(0, 1, 0, FILL)
         t1_quant(0, 0)
         l_quant(0)
-        t1_copy(0, 1, 128, 512)
-        cast(2, 3)
-        mm1(0, 0, 0)
+        t1_copy(0, 1, FILL, K)
         l_quant(1)
-        cast(3, 3)
         t1_quant(0, 1)
-        l_turn((2, 0), (2, 1))
-        t1_copy(1, 1, engine="scalar")
+        cast(2, 0, 3)
+        cast(3, 0, 3)
+        mm1(0, 0, (0,))
+        turn_tile(2)
+        mm1(1, 0, (0,))
+        for n in range(2):
+            mm1(n, 1, (0,))
+        t1_copy(1, 1, copy=nc.scalar.copy)
         t1_copy(1, 0)
-        l_turn((2, 2))
-        mm1(1, 0, 0)
-        l_out(2, 2, vector=True)
-        mm1(0, 1, 0)
+        l_out(2, (2,), vector=True)
         t1_quant(1, 0)
-        mm1(1, 1, 0)
-        l_out(2, 0, 1)
         widen(4, 2)
         t1_quant(1, 1)
+        l_out(2, (0, 1))
+        cast(4, 0, 2)
         l_turn((3, 0), (3, 1))
+        for h in range(G2):
+            for n in range(2):
+                mm1(n, h, (1,))
+        t1_copy(2, 1, SPLIT, K, copy=nc.scalar.copy)
         t1_copy(2, 0)
-        mm1(0, 0, 1)
-        cast(4, 2)
-        mm1(1, 0, 1)
-        mm1(0, 1, 1)
-        t1_copy(2, 1, 192, 512, engine="scalar")
-        mm1(1, 1, 1)
         l_quant(2)
+        t1_copy(2, 1, 0, SPLIT)
+        both(t1_quant, 2)
         l_turn((3, 2))
+        l_out(3, (0, 1))
         l_turn((4, 0), (4, 1))
-        t1_copy(2, 1, 0, 192)
-        l_out(3, 0, 1)
-        t1_quant(2, 0)
-        mm1(2, 0, 0, 1)
-        t1_quant(2, 1)
-        mm1(0, 0, 2)
-        l_out(3, 2)
-        mm1(1, 0, 2)
-        mm1(2, 0, 2)
+        l_out(3, (2,))
+        mm1(2, 0, (0, 1))
+        for n in range(3):
+            mm1(n, 0, (2,))
+        for n in range(2):
+            mm1(n, 1, (2,))
+        cast(5, 0, 2)
+        cast(6, 0, 2)
+        l_out(4, (0, 1))
+        cast(7, 0, 2)
+
         z_step(0, 0)
-        cast(5, 2)
-        mm1(0, 1, 2)
-        mm1(1, 1, 2)
-        widen(5, 2)
-        cast(6, 2)
         mm1(2, 1)
+        hand_over(sum_banks, turn_banks)
+        widen(5, 2)
         l_quant(3)
-        l_out(4, 0, 1)
         widen(6, 2)
-        l_turn((4, 2), (5, 2))
         z_step(1, 0)
-        l_turn((5, 0), (5, 1))
         z_step(0, 1)
-        cast(7, 2)
-        l_turn((6, 0), (6, 1))
         z_step(1, 1)
-        l_out(4, 2)
-        l_out(5, 2)
-        l_turn((6, 2))
         z_step(2, 0)
-        l_out(5, 0, 1)
-        mm1(3, 0)
+        l_turn((4, 2), (5, 2))
+        l_turn((5, 0), (5, 1))
+        turn_tile(6)
+        l_out(4, (2,))
         l_quant(4)
-        mm1(3, 1)
         z_step(2, 1)
-        l_out(6, 0, 1, 2)
+        l_out(5, (2, 0, 1))
+        both(mm1, 3)
+        both(mm1, 4)
         widen(7, 2)
-        mm1(4, 0)
         z_step(3, 0)
-        mm1(4, 1)
         widen(8, 2)
-        cast(8, 2)
         z_step(3, 1)
-        th_widen(0)
-        l_turn((7, 0), (7, 1))
+        l_out(6)
         l_quant(5)
-        l_turn((7, 2))
-        z_step(4, 0)
-        l_turn((8, 0), (8, 1))
-        cast(9, 1)
-        z_step(4, 1)
-        l_out(7, 0, 1, 2)
-        l_turn((8, 2))
-        mm1(5, 0)
+        both(z_step, 4)
         l_quant(6)
+        cast(8, 0, 2)
+        th_cast(0)
+        turn_tile(7)
+        turn_tile(8)
+        cast(9, 0, 1)
         widen(9, 1, 2)
-        mm1(5, 1)
-        l_out(8, 0, 1, 2)
+        l_out(7)
+        both(mm1, 5)
+        both(mm1, 6)
         z_step(5, 0)
-        mm1(6, 0)
         l_quant(7)
         z_step(5, 1)
-        mm1(6, 1)
-        cast(10, 1)
-        th_scale(0, "scalar", 0, 1)
         widen(10, 1, 2)
-        z_turn(0)
-        z_turn(1)
-        z_step(6, 0)
-        z_out(0)
-        l_turn((9, 0), (9, 1))
-        z_step(6, 1)
-        l_turn((9, 2))
-        z_out(1)
-        mm1(7, 0)
+        both(z_step, 6)
+        l_out(8)
         l_quant(8)
-        l_out(9, 0, 1, 2)
-        th_scale(0, "vector", 2, 3)
-        mm1(7, 1)
+        cast(10, 0, 1)
+        th_scale(0, 0)
+        th_scale(0, 1, vector=True)
+        for n in (0, 1):
+            z_turn(n)
+        turn_tile(9)
+        for n in (0, 1):
+            z_out(n)
+        l_out(9)
+        both(mm1, 7)
         z_step(7, 0)
-        th_widen(1)
-        z_turn(2)
         l_quant(9)
-        z_turn(3)
         z_step(7, 1)
-        l_turn((10, 0), (10, 1))
-        cast(11, 1)
         widen(11, 1, 2)
-        z_out(2)
-        l_turn((10, 2))
-        mm1(8, 0)
-        z_out(3)
-        th_quant(0, 0)
-        th_quant(0, 1)
-        l_out(10, 0, 1, 2)
-        mm1(8, 1)
-        z_step(8, 0)
-        mm1(9, 0)
-        z_step(8, 1)
-        th_scale(1, "scalar", 0, 1)
-        mm1(9, 1)
-        z_quant(0)
-        z_quant(1)
-        th_scale(1, "scalar", 2, 3)
+        th_quant(0)
+        th_cast(1)
+        cast(11, 0, 1)
+        for n in (2, 3):
+            z_turn(n)
+        turn_tile(10)
+        for n in (2, 3):
+            z_out(n)
+        l_out(10)
+        both(mm1, 8)
+        both(mm1, 9)
+        both(z_step, 8)
+        for n in (0, 1):
+            z_quant(n)
         l_quant(10)
-        z_turn(4)
-        z_step(9, 0)
-        z_turn(5)
-        l_turn((11, 0), (11, 1))
-        z_out(4)
-        z_step(9, 1)
-        l_turn((11, 2))
-        z_out(5)
+        both(z_step, 9)
+        for half in range(2):
+            th_scale(1, half)
+        th_quant(1)
+        for n in (2, 3):
+            z_quant(n)
+        hand_over(sum_banks, turn_banks)
+        for n in (4, 5):
+            z_turn(n)
+        turn_tile(11)
         z_turn(6)
-        th_quant(1, 0)
-        th_quant(1, 1)
-        mm1(10, 0)
-        l_out(11, 0, 1, 2)
-        z_quant(2)
-        z_quant(3)
-        mm1(10, 1)
-        z_step(10, 0)
+        for n in (4, 5):
+            z_out(n)
+        l_out(11)
         z_out(6)
-        mm2(0)
-        z_step(10, 1)
-        mm2(1)
-        z_quant(4)
-        mm2(2)
-        add_acc(0)
-        mm2(3)
-        z_quant(5)
-        add_acc(1)
-        relu_store(0)
-        mm2(4)
-        l_quant(11)
-        mm2(5)
-        relu_store(1)
-        add_acc(2)
-        z_turn(7)
-        z_quant(6)
-        z_turn(8)
-        add_acc(3)
-        relu_store(2)
-        z_turn(9)
-        z_out(7)
-        add_acc(4)
-        z_turn(10)
-        mm1(11, 0)
-        relu_store(3)
-        add_acc(5)
-        z_out(8)
+        hand_over(turn_banks, sum_banks)
+        both(mm1, 10)
+        both(z_step, 10)
+        before_add = {0: (z_quant, 4), 1: (z_quant, 5), 2: (l_quant, 11), 3: (z_quant, 6)}
+        for n in range(6):
+            if n in before_add:
+                step, tile = before_add[n]
+                step(tile)
+            mm2(n)
+            add_acc(n)
+            if n < 3:
+                relu_store(n)
+        for n in range(7, 11):
+            z_turn(n)
+        for n in range(7, 11):
+            z_out(n)
+            if n < 10:
+                relu_store(n - 4)
+        both(mm1, 11)
         z_quant(7)
-        mm1(11, 1)
         z_step(11, 0)
-        relu_store(4)
-        mm2(6)
-        z_out(9)
         z_quant(8)
         z_step(11, 1)
-        mm2(7)
-        relu_store(5)
-        add_acc(6)
-        z_out(10)
+        for n in (6, 7):
+            mm2(n)
+            add_acc(n)
+            z_quant(n + 3)
         z_turn(11)
-        z_quant(9)
-        mm2(8)
-        add_acc(7)
         z_out(11)
-        mm2(9)
-        z_quant(10)
-        relu_store(6)
-        add_acc(8)
-        relu_store(7)
-        mm2(10)
-        z_quant(11)
-        add_acc(9)
-        relu_store(8)
-        mm2(11)
-        add_acc(10)
-        relu_store(9)
-        add_acc(11, 0, 256)
-        relu_store(10)
-        add_acc(11, 256, 512)
-        relu_store(11, 0, 256)
-        relu_store(11, 256, 512)
+        for n in (6, 7):
+            relu_store(n)
+        for n in range(8, NT - 1):
+            mm2(n)
+            add_acc(n)
+            if n == 8:
+                z_quant(NT - 1)
+            relu_store(n)
+        mm2(NT - 1)
+        for c0 in (0, O // 2):
+            add_acc(NT - 1, c0, c0 + O // 2)
+        for c0 in (0, O // 2):
+            relu_store(NT - 1, c0, c0 + O // 2)

@@ -89,8 +89,8 @@ def tile_chebyshev_filter_last_term_d7_kernel(tc, L_bytes, L_scale, t1, t0, thet
             if (g, h) not in t1_il:
                 t1_il[g, h] = work.tile([P, K, 4], BF16, name="t1_il", bufs=4, align_bytes=64)
             copy(
-                out=t1_il[g, h][:].rearrange("p (u c m) t -> p c t m u", u=2, m=2)[:, f0 // 4 : f1 // 4],
-                in_=t1_raw[g, h][:, :, f0:f1].rearrange("p t (c m u) -> p c t m u", m=2, u=2),
+                out=t1_il[g, h][:].rearrange("p (u c m) t -> p c t m u", u=2, m=4)[:, f0 // 8 : f1 // 8],
+                in_=t1_raw[g, h][:, :, f0:f1].rearrange("p t (c m u) -> p c t m u", m=4, u=2),
             )
 
         def t1_quant(g, h):
@@ -226,8 +226,8 @@ def tile_chebyshev_filter_last_term_d7_kernel(tc, L_bytes, L_scale, t1, t0, thet
         def th_scale(g, half, vector=False):
             th_il[g, half] = work.tile([P, 2, P, 4], BF16, name="th_il", bufs=4, align_bytes=64)
             for b in (2 * half, 2 * half + 1):
-                dst = th_il[g, half][:, b % 2].rearrange("p (c i) t -> p c t i", i=4)
-                src = th_w[:, g, :, P * b : P * b + P].rearrange("p t (c i) -> p c t i", i=4)
+                dst = th_il[g, half][:, b % 2].rearrange("p (c i) t -> p c t i", i=8)
+                src = th_w[:, g, :, P * b : P * b + P].rearrange("p t (c i) -> p c t i", i=8)
                 if vector:
                     nc.vector.tensor_scalar(out=dst, in0=src, scalar1=th_sc[:, g, b : b + 1], scalar2=None, op0=ALU.mult)
                 else:

from contextlib import ExitStack

import concourse.mybir as mybir
from concourse.masks import make_identity

V, F, O = 1536, 1024, 512
FLOPS = 2 * V * V * F + 2 * V * F * O

F32 = mybir.dt.float32
BF16 = mybir.dt.bfloat16
U32 = mybir.dt.uint32
U8 = mybir.dt.uint8
FP8 = mybir.dt.float8_e4m3fn
FP8X4 = mybir.dt.float8_e4m3fn_x4
ACT = mybir.ActivationFunctionType
ALU = mybir.AluOpType

P = 128
K = 512
NT = V // P
G1 = V // K
G2 = F // K
FILL = 128
SPLIT = 192


def tile_chebyshev_filter_last_term_d7_kernel(tc, L_bytes, L_scale, t1, t0, theta_bytes, theta_scale, acc, out):
    nc = tc.nc
    with ExitStack() as ctx:
        keep = ctx.enter_context(tc.tile_pool(name="keep", bufs=1))
        work = ctx.enter_context(tc.tile_pool(name="work", bufs=3))
        psum = ctx.enter_context(tc.psum_pool(name="psum", bufs=1))
        ctx.enter_context(tc.manual_schedule())

        ident = keep.tile([P, P], F32, name="ident")
        make_identity(nc, ident[:])

        sum_banks, turn_banks = [0, 1, 2, 3, 4], [5, 6, 7]

        def next_bank(ring, shape):
            b = ring.pop(0)
            ring.append(b)
            return psum.tile(shape, F32, name="bank%d" % b)

        def hand_over(giver, taker):
            taker.append(giver.pop(0))

        l_sc = keep.tile([P, NT * NT], F32, name="l_sc")
        th_sc = keep.tile([P, G2, 4], F32, name="th_sc")
        th_by = keep.tile([P, G2, 4, O], U8, name="th_by")
        l_rows = L_bytes.rearrange("(n p) j -> p n j", p=P)
        t1_src = t1.rearrange("(g p t) f -> g p t f", p=P, t=4)
        t0_rows = t0.rearrange("(n p) f -> p n f", p=P)
        acc_rows = acc.rearrange("(n p) o -> p n o", p=P)
        th_src = theta_bytes.rearrange("(g p j) o -> g p j o", p=P, j=4)
        l_by, t1_raw, t0_sb, acc_sb = {}, {}, {}, {}

        def load_rows(store, rows, dtype, name, n0, n1):
            tl = keep.tile([P, n1 - n0, rows.shape[2]], dtype, name="%s%d" % (name, n0))
            nc.sync.dma_start(out=tl[:], in_=rows[:, n0:n1, :])
            for n in range(n0, n1):
                store[n] = tl[:, n - n0, :]

        def load_l(n0, n1):
            load_rows(l_by, l_rows, U8, "l_by", n0, n1)

        def load_t0(n0, n1):
            load_rows(t0_sb, t0_rows, BF16, "t0_sb", n0, n1)

        def load_acc(n0, n1):
            load_rows(acc_sb, acc_rows, BF16, "acc_sb", n0, n1)

        def load_t1(g, h0, h1):
            tl = keep.tile([P, 4, K * (h1 - h0)], BF16, name="t1_raw%d_%d" % (g, h0))
            nc.sync.dma_start(out=tl[:], in_=t1_src[g][:, :, K * h0 : K * h1])
            for h in range(h0, h1):
                t1_raw[g, h] = tl[:, :, K * (h - h0) : K * (h - h0 + 1)]

        def load_theta():
            for g in range(G2):
                nc.sync.dma_start(out=th_by[:, g], in_=th_src[g])
            rows = theta_scale.rearrange("(g q) o -> q g o", q=4)
            for q in range(4):
                nc.sync.dma_start(out=th_sc[32 * q : 32 * q + 32], in_=rows[q].partition_broadcast(32))

        t1_il, t1_mx = {}, {}

        def t1_copy(g, h, f0=0, f1=K, copy=nc.vector.tensor_copy):
            if (g, h) not in t1_il:
                t1_il[g, h] = work.tile([P, K, 4], BF16, name="t1_il", bufs=4, align_bytes=64)
            copy(
                out=t1_il[g, h][:].rearrange("p (u c m) t -> p c t m u", u=2, m=4)[:, f0 // 8 : f1 // 8],
                in_=t1_raw[g, h][:, :, f0:f1].rearrange("p t (c m u) -> p c t m u", m=4, u=2),
            )

        def t1_quant(g, h):
            q = keep.tile([P, K], U32, name="t1_q%d_%d" % (g, h), align_bytes=64)
            s = keep.tile([P, K], U8, name="t1_s%d_%d" % (g, h), align_bytes=64)
            nc.vector.quantize_mx(out=q[:].bitcast(FP8X4), scales=s[:], in_=t1_il[g, h][:].rearrange("p f t -> p (f t)"))
            t1_mx[g, h] = (q, s)

        l_w, l_ps, l_il, l_mx, unscaled = {}, {}, {}, {}, set()
        k_sc = keep.tile([P, NT, G1], F32, name="k_sc")

        def regroup_scales():
            for q in range(4):
                rows32 = slice(32 * q, 32 * q + 32)
                nc.vector.tensor_copy(out=k_sc[rows32], in_=l_sc[rows32].rearrange("p (n g q) -> p n g q", g=G1, q=4)[:, :, :, q])

        def widen(n, *gs):
            src = l_by[n].bitcast(FP8)
            for g in gs:
                wide = work.tile([P, K], BF16, name="l_wv", bufs=5)
                for q in range(4):
                    b = 4 * g + q
                    nc.vector.tensor_scalar(
                        out=wide[:].rearrange("p (u m e) -> p m u e", u=2, e=2)[:, 32 * q : 32 * q + 32],
                        in0=src[:, P * b : P * b + P].rearrange("p (m u e) -> p m u e", u=2, e=2),
                        scalar1=l_sc[:, NT * n + b : NT * n + b + 1],
                        scalar2=None,
                        op0=ALU.mult,
                    )
                l_w[n, g] = wide[:]

        def cast(n, g0, g1):
            wide = work.tile([P, K * (g1 - g0)], BF16, name="l_ws", bufs=4)
            nc.scalar.copy(out=wide[:], in_=l_by[n].bitcast(FP8)[:, K * g0 : K * g1])
            for g in range(g0, g1):
                l_w[n, g] = wide[:, K * (g - g0) : K * (g - g0 + 1)]
                unscaled.add((n, g))

        def l_turn(*items):
            ps = next_bank(turn_banks, [P, 2, 2, P])
            for a, (n, g) in enumerate(items):
                pairs = l_w[n, g].bitcast(F32)
                for u in range(2):
                    part = pairs[:, u : 2 * P : 2] if (n, g) in unscaled else pairs[:, P * u : P * u + P]
                    nc.tensor.transpose(ps[:, a, u, :], part, ident[:])
                l_ps[n, g] = ps[:, a]

        def turn_tile(n):
            l_turn((n, 0), (n, 1))
            l_turn((n, 2))

        def l_out(n, gs=range(G1), vector=False):
            if n not in l_il:
                l_il[n] = work.tile([P, V], BF16, name="l_il", bufs=3, align_bytes=64)
            for g in gs:
                dst = l_il[n][:, K * g : K * g + K]
                if (n, g) not in unscaled:
                    nc.scalar.copy(out=dst.bitcast(F32).rearrange("p (i u) -> p i u", u=2), in_=l_ps[n, g].rearrange("p u i -> p i u"))
                    continue
                dst = dst.rearrange("p (i u e) -> p i u e", u=2, e=2)
                src = l_ps[n, g].bitcast(BF16).rearrange("p u (i e) -> p i u e", e=2)
                if vector:
                    nc.vector.tensor_scalar(out=dst, in0=src, scalar1=k_sc[:, n, g : g + 1], scalar2=None, op0=ALU.mult)
                else:
                    nc.scalar.activation(out=dst, in_=src, func=ACT.Copy, scale=k_sc[:, n, g : g + 1])

        def l_quant(n):
            q = work.tile([P, G1 * P], U32, name="l_q", bufs=6, align_bytes=64)
            s = work.tile([P, G1 * P], U8, name="l_s", bufs=6, align_bytes=64)
            nc.vector.quantize_mx(out=q[:].bitcast(FP8X4), scales=s[:], in_=l_il[n][:])
            l_mx[n] = (q, s)

        p_ps, z_sb, zt_ps, z_il, z_mx = {}, {}, {}, {}, {}

        def mm1(n, h, gs=range(G1)):
            if (n, h) not in p_ps:
                p_ps[n, h] = next_bank(sum_banks, [P, K])
            lq, ls = l_mx[n]
            for g in gs:
                cols = slice(P * g, P * g + P)
                tq, ts = t1_mx[g, h]
                nc.tensor.matmul_mx(
                    out=p_ps[n, h][:],
                    lhsT=lq[:, cols].bitcast(FP8X4),
                    lhsT_scale=ls[:, cols],
                    rhs=tq[:].bitcast(FP8X4),
                    rhs_scale=ts[:],
                    start=(g == 0),
                    stop=(g == G1 - 1),
                )

        def z_step(n, h):
            z = work.tile([P, 2, 2 * P], BF16, name="z_sb%d" % h, bufs=7)
            nc.vector.scalar_tensor_tensor(
                out=z[:],
                in0=p_ps[n, h][:].rearrange("p (u b) -> p u b", u=2),
                scalar=2.0,
                in1=t0_sb[n][:, K * h : K * h + K].rearrange("p (b u) -> p u b", u=2),
                op0=ALU.mult,
                op1=ALU.subtract,
            )
            z_sb[n, h] = z

        def z_turn(n):
            zt_ps[n] = next_bank(turn_banks, [P, G2, 2, P])
            for g in range(G2):
                for u in range(2):
                    nc.tensor.transpose(zt_ps[n][:, g, u, :], z_sb[n, g][:, u, :].bitcast(F32), ident[:])

        def z_out(n):
            z_il[n] = work.tile([P, F], BF16, name="z_il", bufs=4, align_bytes=64)
            nc.scalar.copy(
                out=z_il[n][:].bitcast(F32).rearrange("p (g i u) -> p g i u", g=G2, u=2),
                in_=zt_ps[n][:].rearrange("p g u i -> p g i u"),
            )

        def z_quant(n):
            q = work.tile([P, G2 * P], U32, name="z_q", bufs=8, align_bytes=64)
            s = work.tile([P, G2 * P], U8, name="z_s", bufs=8, align_bytes=64)
            nc.vector.quantize_mx(out=q[:].bitcast(FP8X4), scales=s[:], in_=z_il[n][:])
            z_mx[n] = (q, s)

        th_w = keep.tile([P, G2, 4, O], BF16, name="th_w")
        th_il = {}
        th_q = keep.tile([P, G2, O], U32, name="th_q", align_bytes=64)
        th_s = keep.tile([P, G2, O], U8, name="th_s", align_bytes=64)

        def th_cast(g):
            for u in range(2):
                for e in range(2):
                    nc.scalar.copy(out=th_w[:, g, 2 * u + e, :], in_=th_by[:, g, 2 * e + u, :].bitcast(FP8))

        def th_scale(g, half, vector=False):
            th_il[g, half] = work.tile([P, 2, P, 4], BF16, name="th_il", bufs=4, align_bytes=64)
            for b in (2 * half, 2 * half + 1):
                dst = th_il[g, half][:, b % 2].rearrange("p (c i) t -> p c t i", i=8)
                src = th_w[:, g, :, P * b : P * b + P].rearrange("p t (c i) -> p c t i", i=8)
                if vector:
                    nc.vector.tensor_scalar(out=dst, in0=src, scalar1=th_sc[:, g, b : b + 1], scalar2=None, op0=ALU.mult)
                else:
                    nc.scalar.activation(out=dst, in_=src, func=ACT.Copy, scale=th_sc[:, g, b : b + 1])

        def th_quant(g):
            for half in range(2):
                cols = slice(2 * P * half, 2 * P * half + 2 * P)
                src = th_il[g, half][:].rearrange("p b o t -> p (b o t)")
                nc.vector.quantize_mx(out=th_q[:, g, cols].bitcast(FP8X4), scales=th_s[:, g, cols], in_=src)

        y_ps, sums = {}, {}

        def mm2(n):
            y_ps[n] = next_bank(sum_banks, [P, O])
            zq, zs = z_mx[n]
            for g in range(G2):
                cols = slice(P * g, P * g + P)
                nc.tensor.matmul_mx(
                    out=y_ps[n][:],
                    lhsT=zq[:, cols].bitcast(FP8X4),
                    lhsT_scale=zs[:, cols],
                    rhs=th_q[:, g].bitcast(FP8X4),
                    rhs_scale=th_s[:, g],
                    start=(g == 0),
                    stop=(g == G2 - 1),
                )

        def add_acc(n, c0=0, c1=O):
            sums[n, c0] = work.tile([P, c1 - c0], F32, name="y_acc", bufs=4)
            nc.vector.tensor_tensor(out=sums[n, c0][:], in0=y_ps[n][:, c0:c1], in1=acc_sb[n][:, c0:c1], op=ALU.add)

        def relu_store(n, c0=0, c1=O):
            r = work.tile([P, c1 - c0], F32, name="res", bufs=6)
            nc.scalar.activation(out=r[:], in_=sums[n, c0][:], func=ACT.Relu)
            nc.sync.dma_start(out=out[P * n : P * n + P, c0:c1], in_=r[:])

        def both(step, n):
            for h in range(G2):
                step(n, h)

        nc.scalar.dma_start(out=l_sc[:], in_=L_scale.rearrange("a b -> (a b)").partition_broadcast(P))
        warm = keep.tile([P, 2], F32, name="warm")
        nc.vector.memset(warm[:, 0:1], 0.0)
        nc.scalar.activation(out=warm[:, 1:2], in_=warm[:, 0:1], func=ACT.Copy)
        load_l(0, 1)
        load_l(1, 2)
        load_t1(0, 0, 1)
        load_t1(0, 1, 2)
        load_l(2, 4)
        load_t1(1, 0, 2)
        load_l(4, 5)
        load_t1(2, 0, 2)
        load_l(5, 7)
        load_t0(0, 2)
        load_t0(2, 4)
        load_theta()
        load_l(7, 9)
        load_t0(4, 6)
        load_l(9, 12)
        load_t0(6, 9)
        load_acc(0, 4)
        load_t0(9, 12)
        load_acc(4, 8)
        load_acc(8, 12)

        regroup_scales()
        widen(0, 2)
        widen(1, 2)
        cast(0, 0, 1)
        cast(0, 1, 2)
        cast(1, 0, 2)
        l_turn((0, 0))
        l_turn((0, 1), (0, 2))
        l_out(0)
        turn_tile(1)
        l_out(1)
        t1_copy(0, 0)
        t1_copy(0, 1, 0, FILL)
        t1_quant(0, 0)
        l_quant(0)
        t1_copy(0, 1, FILL, K)
        l_quant(1)
        t1_quant(0, 1)
        cast(2, 0, 3)
        cast(3, 0, 3)
        mm1(0, 0, (0,))
        turn_tile(2)
        mm1(1, 0, (0,))
        for n in range(2):
            mm1(n, 1, (0,))
        t1_copy(1, 1, copy=nc.scalar.copy)
        t1_copy(1, 0)
        l_out(2, (2,), vector=True)
        t1_quant(1, 0)
        widen(4, 2)
        t1_quant(1, 1)
        l_out(2, (0, 1))
        cast(4, 0, 2)
        l_turn((3, 0), (3, 1))
        for h in range(G2):
            for n in range(2):
                mm1(n, h, (1,))
        t1_copy(2, 1, SPLIT, K, copy=nc.scalar.copy)
        t1_copy(2, 0)
        l_quant(2)
        t1_copy(2, 1, 0, SPLIT)
        both(t1_quant, 2)
        l_turn((3, 2))
        l_out(3, (0, 1))
        l_turn((4, 0), (4, 1))
        l_out(3, (2,))
        mm1(2, 0, (0, 1))
        for n in range(3):
            mm1(n, 0, (2,))
        for n in range(2):
            mm1(n, 1, (2,))
        cast(5, 0, 2)
        cast(6, 0, 2)
        l_out(4, (0, 1))
        cast(7, 0, 2)

        z_step(0, 0)
        mm1(2, 1)
        hand_over(sum_banks, turn_banks)
        widen(5, 2)
        l_quant(3)
        widen(6, 2)
        z_step(1, 0)
        z_step(0, 1)
        z_step(1, 1)
        z_step(2, 0)
        l_turn((4, 2), (5, 2))
        l_turn((5, 0), (5, 1))
        turn_tile(6)
        l_out(4, (2,))
        l_quant(4)
        z_step(2, 1)
        l_out(5, (2, 0, 1))
        both(mm1, 3)
        both(mm1, 4)
        widen(7, 2)
        z_step(3, 0)
        widen(8, 2)
        z_step(3, 1)
        l_out(6)
        l_quant(5)
        both(z_step, 4)
        l_quant(6)
        cast(8, 0, 2)
        th_cast(0)
        turn_tile(7)
        turn_tile(8)
        cast(9, 0, 1)
        widen(9, 1, 2)
        l_out(7)
        both(mm1, 5)
        both(mm1, 6)
        z_step(5, 0)
        l_quant(7)
        z_step(5, 1)
        widen(10, 1, 2)
        both(z_step, 6)
        l_out(8)
        l_quant(8)
        cast(10, 0, 1)
        th_scale(0, 0)
        th_scale(0, 1, vector=True)
        for n in (0, 1):
            z_turn(n)
        turn_tile(9)
        for n in (0, 1):
            z_out(n)
        l_out(9)
        both(mm1, 7)
        z_step(7, 0)
        l_quant(9)
        z_step(7, 1)
        widen(11, 1, 2)
        th_quant(0)
        th_cast(1)
        cast(11, 0, 1)
        for n in (2, 3):
            z_turn(n)
        turn_tile(10)
        for n in (2, 3):
            z_out(n)
        l_out(10)
        both(mm1, 8)
        both(mm1, 9)
        both(z_step, 8)
        for n in (0, 1):
            z_quant(n)
        l_quant(10)
        both(z_step, 9)
        for half in range(2):
            th_scale(1, half)
        th_quant(1)
        for n in (2, 3):
            z_quant(n)
        hand_over(sum_banks, turn_banks)
        for n in (4, 5):
            z_turn(n)
        turn_tile(11)
        z_turn(6)
        for n in (4, 5):
            z_out(n)
        l_out(11)
        z_out(6)
        hand_over(turn_banks, sum_banks)
        both(mm1, 10)
        both(z_step, 10)
        before_add = {0: (z_quant, 4), 1: (z_quant, 5), 2: (l_quant, 11), 3: (z_quant, 6)}
        for n in range(6):
            if n in before_add:
                step, tile = before_add[n]
                step(tile)
            mm2(n)
            add_acc(n)
            if n < 3:
                relu_store(n)
        for n in range(7, 11):
            z_turn(n)
        for n in range(7, 11):
            z_out(n)
            if n < 10:
                relu_store(n - 4)
        both(mm1, 11)
        z_quant(7)
        z_step(11, 0)
        z_quant(8)
        z_step(11, 1)
        for n in (6, 7):
            mm2(n)
            add_acc(n)
            z_quant(n + 3)
        z_turn(11)
        z_out(11)
        for n in (6, 7):
            relu_store(n)
        for n in range(8, NT - 1):
            mm2(n)
            add_acc(n)
            if n == 8:
                z_quant(NT - 1)
            relu_store(n)
        mm2(NT - 1)
        for c0 in (0, O // 2):
            add_acc(NT - 1, c0, c0 + O // 2)
        for c0 in (0, O // 2):
            relu_store(NT - 1, c0, c0 + O // 2)
